import numpy as np, ml_dtypes
CORES = [3,11,19,27,35,43]
N = 6
BF = ml_dtypes.bfloat16
P, S, M, RO = 768, 3, 6, 5
W, E, Q = N * P, P // S, 2 ** M
def pack(nm, mk):
    z = (nm << M) | mk
    return {"kin": np.ascontiguousarray(z.reshape(128, N, P).transpose(1, 0, 2)).astype(np.int32)}
def town(rng, caps, nin, skew=False):
    order = rng.permutation(W); pos = np.empty(W, np.int64); pos[order] = np.arange(W); blk = pos >> 6; nb = W >> 6
    if skew: key = rng.standard_exponential((8, W, 64), dtype=np.float32) * np.exp2(np.arange(64) * 0.125).astype(np.float32)
    else: key = rng.random((8, W, 64), dtype=np.float32) + 2 * (np.arange(64) >= rng.choice(np.array(caps), nb)[blk][:, None]).astype(np.float32)
    inn = order[64 * blk[None, :, None] + np.argsort(key, axis=-1)[..., :16]]
    ob = (blk + 1 + rng.integers(0, nb - 1, (8, W))) % nb
    far = (rng.integers(0, 64, (8, W, 1)) + (2 * rng.integers(0, 32, (8, W, 1)) + 1) * np.arange(16)) & 63
    m = np.argsort(rng.random((8, W, 16)), axis=-1) < rng.choice(np.array(nin), nb)[blk][None, :, None]
    return np.ascontiguousarray(np.where(m, inn, order[64 * ob[..., None] + far]).transpose(0, 2, 1))
def flips(rng, q):
    f = np.zeros((8, 16, W), np.int64)
    for m in range(M): f |= (rng.random((8, 16, W), dtype=np.float32) < q).astype(np.int64) << m
    return f
def marks(rng, nm, shares):
    lab = rng.integers(0, Q, W)
    return lab[None, None, :] ^ lab[nm] ^ flips(rng, rng.choice(np.array(shares), (8, 1, W)))
def setup_inputs(rng):
    nm = town(rng, [20, 32, 48, 64], [8, 10, 12, 14, 15])
    return pack(nm, marks(rng, nm, [0.05, 0.2, 0.5]))
def setup_inputs_spread(rng):
    nm = town(rng, [64], [9, 12, 14], True); k = np.argsort(rng.random((8, 16, W)), axis=1)
    wide_ = (rng.integers(0, W, (8, 1, W)) + k * rng.integers(1, W // 16, (8, 1, W))) % W
    nm = np.where(rng.random((8, 1, W)) < 0.33, wide_, nm)
    return pack(nm, flips(rng, rng.choice(np.array([0.02, 0.1, 0.5, 0.9, 0.98]), (8, 1, W))))
def setup_inputs_ends(rng):
    e = np.concatenate([np.arange(8), np.arange(W - 8, W)]); x = np.array([8, 9, W - 10, W - 9]); pool = np.concatenate([e, x])
    full = rng.random(W) < 0.5; kind = rng.integers(0, 6, W)
    for r in range(N): kind[P * r + P - 22:P * r + P] = (np.arange(22) + r) % 6
    full[e] = True; full[x] = False; kind[e] = 0; kind[x] = 4
    idx = np.where(full[None, :, None], np.argsort(rng.random((8, W, 16)), axis=-1), np.argsort(rng.random((8, W, 20)), axis=-1)[..., :16])
    nm = np.ascontiguousarray(pool[idx].transpose(0, 2, 1))
    lab = rng.integers(0, 2, W); lab[0] = 0; lab[W - 1] = 1
    half = np.broadcast_to((np.argsort(rng.random((8, W)), axis=0) < 4)[:, None, :], (8, 16, W))
    spot = np.arange(128).reshape(8, 16, 1) == np.where(rng.random(W) < 0.5, 127, rng.integers(0, 128, W))[None, None, :]
    f = np.zeros((8, 16, W), bool)
    for c, v in ((1, half), (2, half & ~spot), (3, half | spot), (4, rng.random((8, 16, W)) < 0.5), (5, ~spot)): f = np.where(kind == c, v, f)
    return pack(nm, (lab[None, None, :] ^ lab[nm] ^ f.astype(np.int64)) * (Q - 1))
def setup_inputs_crowd(rng):
    rot = rng.permutation(N)
    order = np.ascontiguousarray((np.argsort(rng.random((N, P)), axis=1) + P * rot[:, None]).reshape(N, P >> 4, 16).transpose(1, 0, 2)).reshape(-1)
    pos = np.empty(W, np.int64); pos[order] = np.arange(W); blk = pos // (16 * N); lay = (pos >> 4) % N; nb = P >> 4
    typ = (rng.permutation(nb) % 3)[blk]
    p = (16 * N * blk + 16 * np.where(typ == 2, 0, (lay + 1) % N))[None, :, None] + np.argsort(rng.random((8, W, 16)), axis=-1)
    gs = rng.integers(0, 8, (nb, N))[blk, lay]; js = rng.integers(0, 16, (nb, N))[blk, lay]
    hit = (typ == 1)[None, :] & (np.arange(8)[:, None] == gs[None, :]) & ((pos & 15) == js)[None, :]
    nm = np.ascontiguousarray(order[np.where(hit[..., None], (p + 16 * N) % W, p)].transpose(0, 2, 1))
    pat = np.argsort(rng.random((nb, 8, M)), axis=1) < rng.choice(np.array([0, 3, 4, 5, 8]), (nb, 1, M))
    u = np.sum(pat.astype(np.int64) << np.arange(M), axis=2)[blk].T
    on = np.where(typ == 2, lay > 0, (lay & 1) == 0)
    noise = np.where(rng.random((8, 16, W)) < (rng.choice(np.array([0.0, 0.04]), nb)[blk])[None, None, :], rng.integers(0, Q, (8, 16, W)), 0)
    return pack(nm, np.where(on[None, :], u, 0)[:, None, :] ^ noise)
def put(a, k, v, on):
    w = a[k].copy(); a[:] = np.where((a == v) & on, w, a); a[k] = np.where(on, v, a[k])
def setup_inputs_corners(rng):
    nm = town(rng, [20, 40, 64], [10, 13]); p = np.arange(W); every = np.ones(W, bool)
    nm[7] = (p + 1 + np.argsort(rng.random((16, W)), axis=0)) % W
    nm[6] = (p + W - 8 + np.argsort(rng.random((16, W)), axis=0)) % W
    put(nm[0], 0, p, every)
    on = ((p >> 5) & 1) == rng.integers(0, 2)
    put(nm[1], 1, (p + 1) % W, on); put(nm[1], 4, (p + W - 1) % W, on)
    put(nm[2], 2, np.where(rng.random(W) < 0.5, 0, W - 1), every)
    put(nm[2], 5, np.where(p == 0, W - 1, 0), (p == 0) | (p == W - 1))
    put(nm[3], 3, (p + 1) % W, every); put(nm[3], 6, (p + 2) % W, every)
    put(nm[4], 15, np.zeros(W, np.int64), every); put(nm[5], 15, np.full(W, W - 1), every); put(nm[5], 0, np.zeros(W, np.int64), rng.random(W) < 0.5)
    kind = rng.integers(0, 4, (8, W >> 5))[:, p >> 5][:, None, :]
    mk = marks(rng, nm, [0.0, 0.1]); rnd = rng.integers(0, Q, (8, 16, W))
    return pack(nm, np.where(kind == 0, 0, np.where(kind == 1, Q - 1, np.where(kind == 2, mk, rnd))))
def setup_inputs_calm(rng):
    nm = town(rng, [64], [2, 3, 4, 5, 6]); p = np.arange(W); i = rng.permutation(E - 1)[:9]
    one = np.add.outer(P * np.arange(N), S * i[:8]).reshape(-1); two = one + 1
    h = P * int(rng.integers(0, N)) + S * int(i[8])
    on1 = np.zeros(W, bool); on1[one] = True
    on2 = np.zeros(W, bool); on2[two] = True
    for g in range(8):
        put(nm[g], 15, W - 1, on1)
        for j in range(8): put(nm[g], 4 + j, P * ((p // P + 1) % N) + S * int(i[j]), on2)
    put(nm[0], 0, h, on1); put(nm[S], S, h, on1); put(nm[1], 1, h, on2)
    put(nm[0], 0, h + 1, p == h); put(nm[0], 3, W - 1, p == h); put(nm[1], 4, W - 1, p == h); put(nm[S], S + 3, W - 1, p == h)
    put(nm[0], 3, h, p == h + 1)
    mk = marks(rng, nm, [0.1, 0.5])
    mk[:, 15, one] = np.where(np.argsort(rng.random((8, 8 * N)), axis=0) < 2, 0, Q - 1)
    mk[0, 0, one] = Q - 1; mk[S, S, one] = Q - 1; mk[:, 4:12, two] = 0
    mk[0, 3, h] = 0; mk[1, 4, h] = 0; mk[S, S + 3, h] = 0
    return pack(nm, mk)
def check_inputs(d):
    bad = []; z = np.asarray(d["kin"]).astype(np.int64)
    if np.min(z) < 0 or np.max(z) > Q * W - 1: bad.append("range of kin")
    s = np.sort((z >> M).reshape(N, 8, 16, P), axis=2)
    if np.any(s[:, :, 1:] == s[:, :, :-1]): bad.append("equal names in one list of kin")
    return bad
def reference(kin):
    z = np.ascontiguousarray(kin.astype(np.int64).transpose(1, 0, 2)).reshape(8, 16, W)
    for t in range(RO):
        a = np.add.outer(P * np.arange(N), S * np.arange(E) + t % S).reshape(-1)
        nm = z >> M; mk = z & (Q - 1)
        c = nm[t, t, a]; b = nm[t, t + 3, c]
        tes = np.zeros((8, 16, N * E), bool); own = np.zeros((8, 16, N * E), bool); val = np.zeros((8, 16, N * E), np.int64)
        for g in range(8):
            ca = nm[g][:, a]; ma = mk[g][:, a]
            eq = nm[g][:, ca] == b
            m2 = np.add.reduce(np.where(eq, mk[g][:, ca], 0), axis=0)
            own[g] = ca == b; tes[g] = np.any(eq, axis=0) | own[g]
            val[g] = np.where(own[g], ma, ma ^ m2)
        n = np.sum(tes.astype(np.int64), axis=(0, 1)); won = np.zeros(N * E, np.int64); dif = np.zeros((8, 16, N * E), np.int64)
        for m in range(M):
            bit = (val >> m) & 1
            w = (2 * np.sum(np.where(tes, bit, 0), axis=(0, 1)) > n).astype(np.int64)
            won = won + (w << m); dif = dif + (bit != w)
        key = np.where(own, 1000, np.where(tes, dif, -1))
        row = np.argmax(key, axis=1)
        gi, ai = np.nonzero(np.any(tes, axis=1) & (b != a))
        z[gi, row[gi, ai], a[ai]] = (Q * b + won)[ai]
    return {"yk": np.ascontiguousarray(z.reshape(128, N, P).transpose(1, 0, 2)).astype(np.float32)}

@@ -1,0 +1,495 @@
+import math
+from concourse.bass import DstId, RemoteDMATransfer
+from concourse.mybir import AluOpType as A, ActivationFunctionType as F
+
+P, E, RO, NR = 768, 256, 5, 6
+REG = NR * E
+HALF = NR * P // 2
+CHUNKS = [(0, 128), (128, 128)]
+VG = 48
+SG = 40
+CEN = 684.0
+HI, LO = 3412.0 / 1024, -4780.0 / 1024
+SHIFT = 32768.0
+LN2 = math.log(2.0)
+RC = [0, 4096.0, 2048.0, 8192.0, 32768.0, 131072.0, 0.0]
+NH = 8
+UP = [2000, 0]
+HOP, LOOK, GAP, PEC = 120, 0.3, 300, 0.7
+KCUT = [0, 5, 10, 14, 16]
+PLACE = ["SSSSSSSSSSS", "VVVVSVSVVVV"]
+
+SCRATCH = {
+    "TAB": ("sbuf", [128, 7 * REG], "float32"), "Z": ("sbuf", [128, P], "int32"), "RAW": ("sbuf", [128, P], "float32"),
+    "G": ("sbuf", [128, 16 * E], "float32"), "D": ("sbuf", [128, 16 * E], "float16"),
+    "NE": ("sbuf", [128, P], "float32"), "SK": ("sbuf", [128, P], "float16"), "AE": ("sbuf", [128, P], "float32"),
+    "NI": ("sbuf", [128, P], "int32"), "OFF": ("sbuf", [128, RO * E], "uint16"), "COFF": ("sbuf", [128, RO * 16], "uint16"),
+    "SEL": ("sbuf", [128, RO * 128], "float32"), "SELB": ("sbuf", [128, RO * 128], "bfloat16"),
+    "SLOT": ("sbuf", [128, 512], "float32"), "ZI": ("sbuf", [128, E], "int32"),
+    "I1": ("sbuf", [128, P], "int32"), "I2": ("sbuf", [128, P], "int32"), "EQ": ("sbuf", [128, P], "float16"),
+    "Q1": ("sbuf", [128, E], "int32"), "F1": ("sbuf", [128, E], "float32"), "F2": ("sbuf", [128, E], "float32"),
+    "F3": ("sbuf", [128, E], "float32"),
+    "VB": ("sbuf", [128, E], "float32"), "FL": ("sbuf", [128, E], "bfloat16"),
+    "OWN": ("sbuf", [128, E], "float16"), "SKIP": ("sbuf", [128, E], "float16"),
+    "SI": ("sbuf", [128, E], "int32"), "U": ("sbuf", [128, E], "int32"), "W": ("sbuf", [128, E], "float16"),
+    "TES": ("sbuf", [128, E], "float16"), "R1": ("sbuf", [128, E], "float16"), "R2": ("sbuf", [128, E], "bfloat16"),
+    "R3": ("sbuf", [128, E], "bfloat16"), "R4": ("sbuf", [128, E], "bfloat16"), "R5": ("sbuf", [128, E], "bfloat16"),
+    "SG": ("sbuf", [128, E], "bfloat16"), "QF": ("sbuf", [128, E], "float32"), "EX": ("sbuf", [128, E], "bfloat16"),
+    "SE": ("sbuf", [128, E], "float32"), "M1": ("sbuf", [128, E], "float32"), "TB": ("sbuf", [128, E], "float32"),
+    "DR": ("sbuf", [128, E], "float32"),
+    "ONE": ("sbuf", [128, 128], "float32"), "ID": ("sbuf", [128, 128], "float32"), "COL": ("sbuf", [128, 144], "float32"),
+    "WB": ("sbuf", [128, 144], "float16"), "IH": ("sbuf", [128, 7 * 128], "float16"), "ZM": ("sbuf", [128, 256], "bfloat16"),
+    "BLK": ("sbuf", [128, 128], "float32"), "BI": ("sbuf", [128, 128], "int32"),
+    "VW": ("sbuf", [128, 56], "bfloat16"), "WS": ("sbuf", [128, 384], "bfloat16"),
+    "PI": ("sbuf", [128, 8], "int32"), "PF": ("sbuf", [128, 16], "float32"),
+    "LAND": ("sbuf", [128, NH * E], "float32"),
+}
+for _b in range(8):
+    SCRATCH["P%d" % _b] = ("psum", [128, 512], "float32")
+SEMAPHORES = ["sV", "sS", "sP", "sG", "ld", "st0", "st1", "sent"] + ["arr%d" % t for t in range(RO)] + ["h%d" % k for k in range(NH)]
+
+
+def pieces():
+    out = [(0, 0, 0, E, ("far", 0)), (0, 1, 0, E // 2, ("far", 1)), (0, 1, E // 2, E // 2, ("near", 0)), (0, 2, 0, E, None)]
+    for t in range(RO - 1):
+        out.append((t + 1, t + 3, CHUNKS[0][0], CHUNKS[0][1], ("far", 0)))
+        out.append((t + 1, t + 3, CHUNKS[1][0], CHUNKS[1][1], None))
+    return out
+
+
+def helpers(rc, way, T, topo):
+    dsts = [c for c in T.cores if c != rc]
+    side = [h for h in topo.cores_of(rc) if T.rank_of(h) is None and (topo.die(h) != topo.die(rc)) == (way[0] == "far")]
+    full = [h for h in side if all(topo.may_write(h, d) for d in dsts)]
+    part = [h for h in side if h not in full]
+    a, b = full[way[1] % len(full)], part[way[1] % len(part)]
+    return {b: [d for d in dsts if topo.may_write(b, d)], a: [d for d in dsts if not topo.may_write(b, d)]}
+
+
+def ones(m):
+    return bin(m).count("1")
+
+
+def dst(c, topo):
+    rid, pid, _ = topo.addr(c)
+    return DstId(rid=rid, pnc=pid)
+
+
+def helper_program(g, core, T, topo):
+    home = [c for c in topo.cores_of(core) if T.rank_of(c) is not None]
+    if not home:
+        return
+    rc = home[0]; r = T.rank_of(rc); sent = 0; k = 0
+    for (arr, reg, c0, w, way) in pieces():
+        if way is None:
+            continue
+        hs = helpers(rc, way, T, topo)
+        if core in hs:
+            ds = hs[core]; m = topo.mask(core, ds[0]); col = reg * REG + r * E + c0
+            g.wait_ge(T.sem["h%d" % k], ones(topo.mask(rc, core)))
+            g.remote_dma_fused([RemoteDMATransfer(dst_ids=[dst(d, topo) for d in ds], dma_engine_mask=m, remote_sem=T.sem["arr%d" % arr],
+                                                  src=T.LAND[:, k * E:k * E + w], dsts=[T.TAB[:, col:col + w] for d in ds])], local_sem=T.sem.sent)
+            sent += ones(m)
+        k += 1
+    if sent:
+        g.wait_ge(T.sem.sent, sent)
+
+
+def build(g, core, T, topo, r):
+    ops = []
+    CY = 1.04
+
+    def ap(x):
+        n, a, b, s, pn = x
+        return T[n][0:pn, a:b:s] if s != 1 else T[n][0:pn, a:b]
+
+    def R(n, a, w, s=1, pn=128):
+        return (n, a, a + (w - 1) * s + 1, s, pn)
+
+    def wd(x):
+        return (x[2] - x[1] - 1) // x[3] + 1
+
+    def two(x):
+        return SCRATCH[x[0]][2] in ("float16", "bfloat16", "uint16")
+
+    def ps(x):
+        return SCRATCH[x[0]][0] == "psum"
+
+    def add(q, fn, rd, wr, cost, after=(), ext=None):
+        ops.append({"q": q, "fn": fn, "rd": list(rd), "wr": list(wr), "cost": cost, "after": list(after), "ext": ext})
+        return len(ops) - 1
+
+    def col(s):
+        return [s] if isinstance(s, tuple) else []
+
+    def sc(s):
+        return ap(s) if isinstance(s, tuple) else s
+
+    def ts(o, i, s1, op0, s2=None, op1=None):
+        c = 60 + CY * max(64, wd(o) * (0.5 if two(o) and two(i) else 1))
+        if op1 is None:
+            return add("V", lambda: g.vector.tensor_scalar(ap(o), ap(i), sc(s1), None, op0), [i] + col(s1), [o], c)
+        return add("V", lambda: g.vector.tensor_scalar(ap(o), ap(i), sc(s1), sc(s2), op0, op1), [i] + col(s1) + col(s2), [o], c)
+
+    def tt(o, a, b, op):
+        c = 60 + CY * max(64, wd(o) * (1 if ps(a) or ps(b) else 2))
+        return add("V", lambda: g.vector.tensor_tensor(ap(o), ap(a), ap(b), op), [a, b], [o], c)
+
+    def cp(o, i):
+        return add("V", lambda: g.vector.tensor_copy(ap(o), ap(i)), [i], [o], 60 + CY * max(64, wd(o)))
+
+    def ms(o, v):
+        return add("V", lambda: g.vector.memset(ap(o), v), [], [o], 60 + CY * max(64, wd(o)))
+
+    def act(o, i, f, bias=0.0, scale=1.0):
+        return add("S", lambda: g.scalar.activation(ap(o), ap(i), f, bias=sc(bias), scale=sc(scale)), [i] + col(bias) + col(scale), [o],
+                   80 + CY * max(64, wd(o)))
+
+    def aff(q, o, i, scale, bias):
+        if q == "S":
+            return act(o, i, F.Identity, bias=bias, scale=scale)
+        return ts(o, i, bias, A.add) if scale == 1.0 else ts(o, i, scale, A.mult, bias, A.add)
+
+    lastmm = {}
+
+    def mm(items):
+        def fn():
+            for (o, l, x, s0, s1) in items:
+                ins = g.tensor.matmul(ap(o), ap(l), ap(x), s0, s1)
+            return ins
+        c = 60 + sum(PEC * max(min(64, wd(l)), wd(x)) * (1 if two(x) else 4) for (o, l, x, s0, s1) in items)
+        banks = {it[0][0] for it in items}
+        o = add("P", fn, [y for it in items for y in it[1:3]], [it[0] for it in items], c, [lastmm[b] for b in banks if b in lastmm])
+        lastmm.update({b: o for b in banks})
+        return o
+
+    def iota(o, pat, base, cm):
+        fl = SCRATCH[o[0]][2] != "int32"
+        if fl:
+            return add("G", lambda: g.iota(ap(o), pat, base, cm, allow_small_or_imprecise_dtypes=True), [], [o], 160 + 2 * CY * wd(o))
+        return add("G", lambda: g.iota(ap(o), pat, base, cm), [], [o], 160 + 2 * CY * wd(o))
+
+    def setrow(o, j, v):
+        return add("G", lambda: g.affine_select(ap(o), ap(o), [[0, wd(o)]], A.not_equal, v, -j, 1), [o], [o], 200 + 2 * CY * wd(o))
+
+    others = [c for c in T.cores if c != core]
+    sent = [0]; hk = [0]; nets = {}; need = {}
+    plist = pieces()
+    for (arr, reg, c0, w, way) in plist:
+        need[arr] = need.get(arr, 0) + sum(ones(topo.mask(c, core)) for c in others)
+
+    def send(reg, c0):
+        arr, _, _, w, way = [p for p in plist if p[1] == reg and p[2] == c0][0]
+        src = R("TAB", reg * REG + r * E + c0, w)
+        if way is None:
+            ds = others; sem = T.sem["arr%d" % arr]; to = src; lat = 2000 + w * 512 * 5 / 130.0
+        else:
+            k = [p for p in plist if p[4] is not None].index((arr, reg, c0, w, way))
+            ds = list(helpers(core, way, T, topo)); sem = T.sem["h%d" % k]; to = R("LAND", k * E, w); lat = 4500 + w * 512 * 4 / 130.0
+        m = topo.mask(core, ds[0]); sent[0] += ones(m)
+        o = add("G", lambda: g.remote_dma_fused([RemoteDMATransfer(dst_ids=[dst(d, topo) for d in ds], dma_engine_mask=m, remote_sem=sem,
+                                                                   src=ap(src), dsts=[ap(to) for d in ds])], local_sem=T.sem.sent), [src], [], 800)
+        ops[o]["noinc"] = True
+        nets.setdefault(arr, []).append(add("N%d" % o, None, [], [], lat, [o]))
+
+    def gather(q, o, t, off):
+        win = R("TAB", t * REG, 3 * REG); n = wd(o); ext = ("arr%d" % t, need[t])
+        src = lambda: ap(win).indirect(ap(off))
+        if q == "S":
+            return add("S", lambda: g.scalar.activation(ap(o), src(), F.Identity), [win, off], [o], 80 + 1.56 * CY * n, nets[t], ext)
+        if q == "V":
+            return add("V", lambda: g.vector.tensor_copy(ap(o), src()), [win, off], [o], 60 + 1.56 * CY * n, nets[t], ext)
+        M2 = 1.5 * 2 ** 24
+        return add("V", lambda: g.vector.tensor_scalar(ap(o), src(), M2, M2, A.add, A.subtract), [win, off], [o], 60 + 1.56 * CY * n, nets[t], ext)
+
+    o = add("Y", lambda: g.sync.dma_start(T.Z[:], T.kin[:]), [], [R("Z", 0, P)], 3000); ops[o]["dma"] = "ld"
+    iota(R("AE", 0, P), [[6, 3], [18, E]], 6 * (P * r - HALF), 0)
+    act(R("P0", 0, 512), R("AE", 0, 512), F.Identity); act(R("P1", 0, 256), R("AE", 512, 256), F.Identity)
+    AEP = [R("P0", 0, E), R("P0", 256, E), R("P1", 0, E)]
+    ONE = R("ONE", 0, 128); ID = R("ID", 0, 128)
+    ms(ONE, 1.0)
+    add("G", lambda: g.affine_select(ap(ID), ap(ONE), [[-1, 128]], A.is_equal, 0.0, 0, 1), [ONE], [ID], 470)
+    IH = {}
+    for j, v in enumerate([1.0 / 1024, SHIFT, 1.0, 4096.0, 1025.0, -1033.0]):
+        IH[v] = R("IH", 128 * j, 128); act(IH[v], ID, F.Identity, scale=v)
+    pi = lambda j: R("PI", j, 1)
+    pf = lambda j, pn=128: R("PF", j, 1, 1, pn)
+    iota(pi(0), [[0, 1]], 0, 1)
+    ts(pi(1), pi(0), -16, A.bitwise_and); cp(pf(0), pi(1))
+    iota(R("COL", 0, 144), [[1, 144]], -15, 0)
+    ts(R("WB", 0, 144), R("COL", 0, 144), pf(0), A.is_equal, 1024.0, A.mult)
+    iota(R("BI", 0, 128), [[16, 8], [0, 16]], 0, 0)
+    ts(R("BLK", 0, 128), R("BI", 0, 128), pf(0), A.is_equal, -0.5, A.mult)
+    ZM, ZB = R("ZM", 0, 128), R("ZM", 128, 128)
+    tt(ZM, R("BLK", 0, 128), ID, A.add); act(ZB, ZM, F.Identity, scale=2.0 ** 70)
+    ts(pi(2), pi(0), 15, A.bitwise_and); ts(pf(1), pi(2), 180.0, A.add, -LN2, A.mult)
+    ts(pi(3), pi(0), 7, A.bitwise_and); ts(pi(4), pi(0), 1, A.bitwise_and)
+    ts(pf(2), pi(3), 2 * LN2, A.mult, -11 * LN2, A.add)
+    ts(pf(3), pi(4), 10 * LN2, A.mult, 10 * LN2, A.add); tt(pf(4), pf(2), pf(3), A.add)
+    ts(pf(5), pi(3), 3.0, A.is_ge, -5 * LN2, A.mult); ts(pf(6), pf(5), 10 * LN2, A.add); tt(pf(7), pf(2), pf(6), A.add)
+    WX, WE, WR = R("WS", 0, 128, 1, 8), R("WS", 128, 128, 1, 8), R("WS", 256, 128, 1, 8)
+    for wv, c in ((WX, 4), (WE, 2), (WR, 7)):
+        act(wv, R("ONE", 0, 128, 1, 8), F.Exp, scale=pf(c, 8))
+    setrow(WE, 6, (682.5 - CEN) / 1024); setrow(WR, 6, 31.5)
+    WX, WE, WR = R("WS", 0, 128, 1, 6), R("WS", 128, 128, 1, 7), R("WS", 256, 128, 1, 7)
+    ms(R("VW", 0, 56), 0.0); ms(R("VW", 0, 1), 2.0); ms(R("VW", 48, 1), -3.0); ms(R("VW", 49, 5), -1.0)
+    for j in range(1, 6):
+        ms(R("VW", 8 * j + j, 1), 2.0 / 4 ** j); ms(R("VW", 8 * j + j - 1, 1), -2.0 / 4 ** (j - 1))
+    KJ = [256.0 / 4 ** j * (RC[j] - RC[j + 1]) for j in range(6)]
+    ms(pf(8), -KJ[2] - 0.5)
+    for j in (0, 1, 5):
+        setrow(pf(8), j, -KJ[j] - 0.5)
+    setrow(pf(8), 6, 1.0)
+    ms(R("SLOT", 0, 128), 0.0); ms(R("COFF", 0, 16 * RO), 0)
+
+    def split(zi, s, bank):
+        c = s * E
+        ts(R("I1", c, E), zi, 42, A.bitwise_and); aff("S", R(bank, 0, E), R("I1", c, E), 31.0, -CEN)
+        ts(R("I2", c, E), zi, 63, A.bitwise_and); tt(R("SK", c, E), R("I2", c, E), R(bank, 0, E), A.add)
+        ts(R("NI", c, E), zi, 6, A.arith_shift_right); aff("S", R("NE", c, E), R("NI", c, E), 6.0, -6.0 * HALF)
+
+    def plain(dr, b64, raw, wo, se):
+        tt(dr, b64, raw, A.subtract); tt(wo, dr, wo, A.add); tt(wo, se, wo, A.mult); tt(raw, raw, wo, A.add)
+
+    def behind(first):
+        gate = max(i for i in range(first) if "noinc" in ops[i])
+        for o in ops[first:]:
+            o["after"].append(gate)
+
+    def prep(t):
+        s = t % 3; c = s * E
+        n = R("NI", c, E); sl = R("SLOT", 128, E); f1, f2, f3 = R("F1", 0, E), R("F2", 0, E), R("F3", 0, E)
+        ts(R("Q1", 0, E), n, 1.0 / 3, A.mult, -1.0 / 3, A.add)
+        f1 = R("P1", 256, E)
+        aff("S", f1, n, float(REG), -float(REG * s)); aff("S", f2, R("Q1", 0, E), 1.0 - 3 * REG, 0.0)
+        if s == 0:
+            tt(sl, f1, f2, A.add)
+        else:
+            tt(f3, f1, f2, A.add); ts(f1, f3, 0.0, A.is_lt, 3.0 * REG, A.mult); tt(sl, f3, f1, A.add)
+        cp(R("OFF", t * E, E), sl)
+
+    def wrap(t):
+        m = 16 * (t + 1)
+        for h4 in range(0, 16, 4):
+            mm([(R("P4", 496 + h, 1, 1, m), R("SLOT", 128 + 16 * h - 16 * t, m), R("ID", 17 * t, 1), True, True) for h in range(h4, h4 + 4)])
+        cp(R("COFF", 16 * t, 16, 1, m), R("P4", 496, 16, 1, m))
+        act(R("SEL", 128 * t, 128), ONE, F.Identity, scale=R("ID", 17 * t + 3, 1))
+        act(R("SELB", 128 * t, 128), ONE, F.Identity, scale=R("ID", 17 * t + 3, 1))
+
+    for s in range(3):
+        c = s * E; bk = "P%d" % (2 + s); b2 = "P%d" % (5 + s)
+        first = len(ops)
+        split(R("Z", s, E, 3), s, bk)
+        tt(R("EQ", c, E), R("NE", c, E), AEP[s], A.is_equal)
+        mm([(R(b2, 0, E), IH[1.0 / 1024], R("SK", c, E), True, False), (R(b2, 0, E), IH[SHIFT], R("EQ", c, E), False, True)])
+        tt(R("TAB", s * REG + r * E, E), R("NE", c, E), R(b2, 0, E), A.add)
+        for p in plist:
+            if p[1] == s:
+                send(s, p[2])
+        for o in ops[first:]:
+            o["up"] = 6000 - 2000 * s
+    first = len(ops)
+    prep(0); wrap(0)
+    aff("S", R("RAW", 0, P), R("Z", 0, P), 1.0, 0.0)
+    prep(1); wrap(1); prep(2)
+    behind(first)
+    late = []
+
+    for t in range(RO):
+        s = t % 3; last = t == RO - 1
+        for ci, (i0, w) in enumerate(CHUNKS):
+            gather("B", R("VB", i0, w), t, R("COFF", 16 * t + i0 // 16, w // 16))
+            o = ts(R("FL", i0, w), R("VB", i0, w), 16384.0, A.is_ge, -SHIFT, A.mult)
+            a = i0
+            if ci == 0 and VG:
+                o2 = gather("V", R("G", 16 * a, 16 * VG), t, R("OFF", t * E + a, VG)); a += VG
+                ops[o2]["after"].append(o)
+            while a < i0 + w:
+                n = min(SG, i0 + w - a)
+                gather("S", R("G", 16 * a, 16 * n), t, R("OFF", t * E + a, n)); a += n
+        for ci, (i0, w) in enumerate(CHUNKS):
+            pa, pb, pc, pd = ["P%d" % (4 * ci + j) for j in range(4)]
+            X = lambda n, pn=128: R(n, i0, w, 1, pn)
+            sel, selb = R("SEL", 128 * t, 128), R("SELB", 128 * t, 128)
+            B = R(pa, 0, w); S1 = R(pb, 0, w); XP = R(pb, 256, w); NV = R(pd, 0, w); WO = R(pd, 256, w)
+            first = len(ops)
+            mm([(B, sel, X("VB"), True, False)])
+            mm([(B, selb, X("FL"), False, True)])
+            tt(X("OWN"), R("NE", s * E + i0, w), B, A.is_equal)
+            tt(X("SKIP"), R("AE", s * E + i0, w), B, A.is_equal)
+            mm([(S1, IH[1.0], R("SK", s * E + i0, w), True, False)])
+            for k0, k1 in zip(KCUT, KCUT[1:]):
+                for k in range(k0, k1):
+                    tt(R("D", 16 * i0 + k * w, w), R("G", 16 * i0 + k, w, 16), B, A.subtract)
+                d4 = R("D", 16 * i0 + k0 * w, (k1 - k0) * w)
+                ts(d4, d4, HI, A.min, LO, A.max)
+                it = [(S1, R("WB", 15 - k, 128), R("D", 16 * i0 + k * w, w), False, k == 15) for k in range(k0, k1)]
+                if k0 == KCUT[1]:
+                    it = it + [(S1, IH[4096.0], X("OWN"), False, False)]
+                mm(it)
+            if not last:
+                mm([(NV, sel, X("VB"), True, False), (NV, selb, X("FL"), False, False)])
+            qs = PLACE[ci]
+            aff(qs[0], X("SI"), S1, 1.0, 16 * 4780.0 + CEN)
+            ts(X("U"), X("SI"), 0x1555, A.bitwise_and)
+            if qs[1] == "S":
+                act(X("W"), X("U"), F.Relu, bias=-4095.0)
+            else:
+                ts(X("W"), X("U"), 4095.0, A.subtract, 0.0, A.max)
+            if qs[2] == "S":
+                act(X("TES"), X("W"), F.Sign)
+            else:
+                ts(X("TES"), X("W"), 1.0, A.min)
+            VO = R(pc, 0, w, 1, 8); vw = lambda j: R("VW", 8 * j, 8)
+            for j in range(1, 6):
+                aff(qs[2 + j], X("R%d" % j), X("W"), 1.0, RC[j] - 0.5)
+            mm([(VO, vw(0), X("W"), True, False), (VO, vw(6), X("TES"), False, False)])
+            mm([(VO, vw(1), X("R1"), False, False), (VO, vw(2), X("R2"), False, False)])
+            mm([(VO, vw(j), X("R%d" % j), False, j == 5) for j in (3, 4, 5)])
+            mm([(XP, IH[1025.0], X("W"), True, False), (XP, IH[-1033.0], X("TES"), False, False)])
+            act(X("SG", 8), VO, F.Sign, bias=pf(8, 8))
+            mm([(XP, WX, X("SG", 6), False, True)])
+            it = [(WO, WR, X("SG", 7), True, True)]
+            if not last:
+                it = [(NV, WE, X("SG", 7), False, True)] + it
+            mm(it)
+            aff(qs[8], X("SI"), XP, 1.0, 0x111111 / 2.0 + 8)
+            ts(X("U"), X("SI"), 0x111119, A.bitwise_and)
+            aff(qs[9], X("SI"), X("U"), 0x111111 / 2.0 ** 20, 1.5 * 2 ** 23 + 8)
+            ts(X("U"), X("SI"), 15, A.bitwise_and)
+            act(X("EX"), X("U"), F.Exp, bias=pf(1), scale=17 * LN2)
+            ZZ = R(pc, 0, w); NS = R(pc, 256, w)
+            mm([(ZZ, ZB, X("OWN"), True, False), (ZZ, ZB, X("SKIP"), False, False)])
+            mm([(ZZ, ZM, X("EX"), False, True)])
+            ts(X("SE"), ZZ, 1.5 * 2.0 ** -62, A.is_gt)
+            if not last:
+                if qs[10] == "S":
+                    act(NS, X("SE"), F.Identity, bias=1.0, scale=-1.0)
+                else:
+                    ts(NS, ZZ, 1.5 * 2.0 ** -62, A.is_le)
+                tt(NV, X("SE"), NV, A.mult)
+                tt(X("M1"), R("TAB", t * REG + r * E + i0, w), NS, A.mult)
+                tt(R("TAB", (t + 3) * REG + r * E + i0, w), X("M1"), NV, A.add)
+                send(t + 3, i0)
+            for o in ops[first:]:
+                o["up"] = UP[ci]
+            M = 1.5 * 2 ** 23; B64 = R(pa, 256, w); raw = R("RAW", 3 * i0 + s, w, 3)
+            act(X("TB"), B, F.Identity, bias=64.0 * HALF + M, scale=32.0 / 3)
+            act(B64, X("TB"), F.Identity, bias=-M)
+            late.append((X("DR"), B64, raw, WO, X("SE")))
+            if last:
+                plain(*late.pop())
+                o = add("Y", lambda i0=i0, w=w: g.sync.dma_start(T.yk[:, 3 * i0:3 * (i0 + w)], T.RAW[:, 3 * i0:3 * (i0 + w)]),
+                        [R("RAW", 3 * i0, 3 * w)], [], 2500)
+                ops[o]["dma"] = "st%d" % ci
+        if not last:
+            first = len(ops)
+            while late:
+                plain(*late.pop(0))
+            if t != 1:
+                wrap(max(t + 1, 2))
+            if t in (1, 2):
+                prep(t + 2)
+            if t < 2:
+                cp(R("ZI", 0, E), R("RAW", t, E, 3)); split(R("ZI", 0, E), t, "P1")
+            behind(first)
+    return ops, sent[0]
+
+
+def order(ops):
+    n = len(ops); deps = [set(o["after"]) for o in ops]; acc = {}
+    for i, o in enumerate(ops):
+        for kind, lst in (("r", o["rd"]), ("w", o["wr"])):
+            for x in lst:
+                for (j, k2, y) in acc.get(x[0], []):
+                    if j != i and (kind == "w" or k2 == "w") and x[1] < y[2] and y[1] < x[2]:
+                        if x[3] == y[3] == 3 and (x[1] - y[1]) % 3 and ops[j]["q"] == o["q"]:
+                            continue
+                        deps[i].add(j)
+        for kind, lst in (("r", o["rd"]), ("w", o["wr"])):
+            for x in lst:
+                l = acc.setdefault(x[0], [])
+                if kind == "w" and x[3] == 1 and x[4] == 128:
+                    l[:] = [z for z in l if not (x[1] <= z[2][1] and z[2][2] <= x[2])]
+                l.append((i, kind, x))
+    succ = [[] for _ in ops]
+    for i in range(n):
+        for j in deps[i]:
+            succ[j].append(i)
+    pr = [0.0] * n
+    for i in range(n - 1, -1, -1):
+        pr[i] = ops[i]["cost"] + max([pr[j] + HOP for j in succ[i]] or [0])
+    pr = [p + o.get("up", 0) for p, o in zip(pr, ops)]
+    left = [len(d) for d in deps]; ready = [i for i in range(n) if not left[i]]
+    free = {}; end = [0.0] * n; bank = {}; seq = []
+    while ready:
+        st = {}
+        for i in ready:
+            q = ops[i]["q"]; s = free.get(q, 0.0)
+            for j in deps[i]:
+                s = max(s, end[j] + (0 if q == ops[j]["q"] == "P" else HOP))
+            for x in ops[i]["rd"] + ops[i]["wr"]:
+                if SCRATCH[x[0]][0] == "psum":
+                    for q2, j in bank.get(x[0], {}).items():
+                        if q2 != q:
+                            s = max(s, end[j] + HOP)
+            st[i] = s
+        b = min(ready, key=lambda i: (st[i], -pr[i])); q = ops[b]["q"]
+        top = max([i for i in ready if ops[i]["q"] == q and st[i] <= st[b] + LOOK * ops[b]["cost"]], key=lambda i: pr[i])
+        if pr[top] > pr[b] + GAP or st[top] <= st[b] + 40:
+            b = top
+        for x in ops[b]["rd"] + ops[b]["wr"]:
+            if SCRATCH[x[0]][0] == "psum":
+                d = bank.setdefault(x[0], {})
+                for q2, j in d.items():
+                    if q2 != q:
+                        deps[b].add(j)
+                d[q] = b
+        end[b] = st[b] + ops[b]["cost"]; free[q] = end[b]; ops[b]["t"] = st[b]
+        seq.append(b); ready.remove(b)
+        for j in succ[b]:
+            left[j] -= 1
+            if not left[j]:
+                ready.append(j)
+    return seq, deps
+
+
+def rank_program(g, core, T, topo):
+    r = T.rank_of(core)
+    if r is None:
+        return helper_program(g, core, T, topo)
+    ops, sent = build(g, core, T, topo, r)
+    seq, deps = order(ops)
+    Q = {"V": g.vector, "S": g.scalar, "P": g.tensor, "G": g, "Y": g.sync}
+    used = set()
+    for i in seq:
+        for j in deps[i]:
+            if not (ops[i]["q"] == ops[j]["q"] == "P"):
+                used.add(j)
+    cnt = {}; sig = {}; known = {}; clock = {}
+    for i in seq:
+        o = ops[i]; q = o["q"]
+        if o["fn"] is None:
+            continue
+        kn = known.setdefault(q, {}); want = {}
+        for j in deps[i]:
+            if j in sig and not (q == ops[j]["q"] == "P"):
+                s, v = sig[j]
+                if v > want.get(s, (0, 0))[0]:
+                    want[s] = (v, j)
+        if o["ext"]:
+            want[o["ext"][0]] = (o["ext"][1], None)
+        for s, (v, j) in sorted(want.items(), key=lambda z: -(seq.index(z[1][1]) if z[1][1] is not None else 10 ** 9)):
+            if kn.get(s, 0) < v:
+                Q[q].wait_ge(T.sem[s], v); kn[s] = v
+                for s2, v2 in clock.get(j, {}).items():
+                    kn[s2] = max(kn.get(s2, 0), v2)
+        ins = o["fn"]()
+        clock[i] = dict(kn)
+        if "dma" in o:
+            ins.then_inc(T.sem[o["dma"]], 16); sig[i] = (o["dma"], 16); cnt[o["dma"]] = 16
+        elif i in used and "noinc" not in o:
+            s = "s" + q; cnt[s] = cnt.get(s, 0) + 1; ins.then_inc(T.sem[s], 1); sig[i] = (s, cnt[s])
+    for s, v in cnt.items():
+        g.sync.wait_ge(T.sem[s], v)
+    g.wait_ge(T.sem.sent, sent)

@@ -7,6 +7,14 @@ REG = NR * E
 HALF = NR * P // 2
 CHUNKS = [(0, 128), (128, 128)]
 VG = 48
+SG0 = 20
+UPO = 0
+UPB = 0
+SUB = 0
+BGL = 0.7
+MMN = 2
+SEED = 0
+JIT = 0
 SG = 40
 CEN = 684.0
 HI, LO = 3412.0 / 1024, -4780.0 / 1024
@@ -18,6 +26,8 @@ UP = [2000, 0]
 HOP, LOOK, GAP, PEC = 120, 0.3, 300, 0.7
 KCUT = [0, 5, 10, 14, 16]
 PLACE = ["SSSSSSSSSSS", "VVVVSVSVVVV"]
+VG, SG0, SG, UP, UPO, UPB, KCUT, MMN, LOOK, GAP = 56, 8, 40, [1500, 0], 0, 0, [0, 6, 11, 15, 16], 8, 0.3, 300
+PLACE = ["SSSSSSSSSSS", "VVSVSVSVVVV"]
 
 SCRATCH = {
     "TAB": ("sbuf", [128, 7 * REG], "float32"), "Z": ("sbuf", [128, P], "int32"), "RAW": ("sbuf", [128, P], "float32"),
@@ -25,7 +35,7 @@ SCRATCH = {
     "NE": ("sbuf", [128, P], "float32"), "SK": ("sbuf", [128, P], "float16"), "AE": ("sbuf", [128, P], "float32"),
     "NI": ("sbuf", [128, P], "int32"), "OFF": ("sbuf", [128, RO * E], "uint16"), "COFF": ("sbuf", [128, RO * 16], "uint16"),
     "SEL": ("sbuf", [128, RO * 128], "float32"), "SELB": ("sbuf", [128, RO * 128], "bfloat16"),
-    "SLOT": ("sbuf", [128, 512], "float32"), "ZI": ("sbuf", [128, E], "int32"),
+    "SLOT": ("sbuf", [128, 768], "float32"), "ZI": ("sbuf", [128, 2 * E], "int32"),
     "I1": ("sbuf", [128, P], "int32"), "I2": ("sbuf", [128, P], "int32"), "EQ": ("sbuf", [128, P], "float16"),
     "Q1": ("sbuf", [128, E], "int32"), "F1": ("sbuf", [128, E], "float32"), "F2": ("sbuf", [128, E], "float32"),
     "F3": ("sbuf", [128, E], "float32"),
@@ -50,9 +60,11 @@ SEMAPHORES = ["sV", "sS", "sP", "sG", "ld", "st0", "st1", "sent"] + ["arr%d" % t
 
 
 def pieces():
-    out = [(0, 0, 0, E, ("far", 0)), (0, 1, 0, E // 2, ("far", 1)), (0, 1, E // 2, E // 2, ("near", 0)), (0, 2, 0, E, None)]
+    out = [(0, 0, 0, E, ("far", 0, "all")), (0, 1, 0, E // 2, ("far", 1, "in")), (0, 1, E // 2, E // 2, ("near", 0, "out")), (0, 2, 0, E, None)]
+    h = CHUNKS[0][1] // 2
     for t in range(RO - 1):
-        out.append((t + 1, t + 3, CHUNKS[0][0], CHUNKS[0][1], ("far", 0)))
+        out.append((t + 1, t + 3, 0, h, ("far", t % 2, "in")))
+        out.append((t + 1, t + 3, h, h, None))
         out.append((t + 1, t + 3, CHUNKS[1][0], CHUNKS[1][1], None))
     return out
 
@@ -64,6 +76,11 @@ def helpers(rc, way, T, topo):
     part = [h for h in side if h not in full]
     a, b = full[way[1] % len(full)], part[way[1] % len(part)]
     return {b: [d for d in dsts if topo.may_write(b, d)], a: [d for d in dsts if not topo.may_write(b, d)]}
+
+
+def inmask(rc, h, way, T, topo):
+    full = topo.mask(rc, h); out = topo.mask(rc, [c for c in T.cores if c != rc][0])
+    return {"all": full, "out": out, "in": full & ~out}[way[2]]
 
 
 def ones(m):
@@ -86,7 +103,7 @@ def helper_program(g, core, T, topo):
         hs = helpers(rc, way, T, topo)
         if core in hs:
             ds = hs[core]; m = topo.mask(core, ds[0]); col = reg * REG + r * E + c0
-            g.wait_ge(T.sem["h%d" % k], ones(topo.mask(rc, core)))
+            g.wait_ge(T.sem["h%d" % k], ones(inmask(rc, core, way, T, topo)))
             g.remote_dma_fused([RemoteDMATransfer(dst_ids=[dst(d, topo) for d in ds], dma_engine_mask=m, remote_sem=T.sem["arr%d" % arr],
                                                   src=T.LAND[:, k * E:k * E + w], dsts=[T.TAB[:, col:col + w] for d in ds])], local_sem=T.sem.sent)
             sent += ones(m)
@@ -178,19 +195,24 @@ def build(g, core, T, topo, r):
     for (arr, reg, c0, w, way) in plist:
         need[arr] = need.get(arr, 0) + sum(ones(topo.mask(c, core)) for c in others)
 
-    def send(reg, c0):
-        arr, _, _, w, way = [p for p in plist if p[1] == reg and p[2] == c0][0]
-        src = R("TAB", reg * REG + r * E + c0, w)
-        if way is None:
-            ds = others; sem = T.sem["arr%d" % arr]; to = src; lat = 2000 + w * 512 * 5 / 130.0
-        else:
-            k = [p for p in plist if p[4] is not None].index((arr, reg, c0, w, way))
-            ds = list(helpers(core, way, T, topo)); sem = T.sem["h%d" % k]; to = R("LAND", k * E, w); lat = 4500 + w * 512 * 4 / 130.0
-        m = topo.mask(core, ds[0]); sent[0] += ones(m)
+    def send(reg, c0, c1):
+        tr = []; ps_ = [p for p in plist if p[1] == reg and c0 <= p[2] < c1]
+        for p in ps_:
+            arr, _, a, w, way = p
+            src = R("TAB", reg * REG + r * E + a, w)
+            if way is None:
+                ds = others; sem = T.sem["arr%d" % arr]; to = src; m = topo.mask(core, ds[0])
+            else:
+                k = [x for x in plist if x[4] is not None].index(p)
+                ds = list(helpers(core, way, T, topo)); sem = T.sem["h%d" % k]; to = R("LAND", k * E, w); m = inmask(core, ds[0], way, T, topo)
+            sent[0] += ones(m); tr.append((ds, m, sem, src, to))
         o = add("G", lambda: g.remote_dma_fused([RemoteDMATransfer(dst_ids=[dst(d, topo) for d in ds], dma_engine_mask=m, remote_sem=sem,
-                                                                   src=ap(src), dsts=[ap(to) for d in ds])], local_sem=T.sem.sent), [src], [], 800)
+                                                                   src=ap(src), dsts=[ap(to) for d in ds]) for (ds, m, sem, src, to) in tr],
+                                                local_sem=T.sem.sent), [x[3] for x in tr], [], 800)
         ops[o]["noinc"] = True
-        nets.setdefault(arr, []).append(add("N%d" % o, None, [], [], lat, [o]))
+        for (arr, _, a, w, way) in ps_:
+            n = add("N", None, [], [], 600 + w * 512 * 5 / 250.0, [o]) if way is None else o
+            nets.setdefault(arr, []).append(add("N%d" % len(ops), None, [], [], 1200 if way is None else 4000 + w * 512 * 4 / 200.0, [n]))
 
     def gather(q, o, t, off):
         win = R("TAB", t * REG, 3 * REG); n = wd(o); ext = ("arr%d" % t, need[t])
@@ -200,7 +222,7 @@ def build(g, core, T, topo, r):
         if q == "V":
             return add("V", lambda: g.vector.tensor_copy(ap(o), src()), [win, off], [o], 60 + 1.56 * CY * n, nets[t], ext)
         M2 = 1.5 * 2 ** 24
-        return add("V", lambda: g.vector.tensor_scalar(ap(o), src(), M2, M2, A.add, A.subtract), [win, off], [o], 60 + 1.56 * CY * n, nets[t], ext)
+        return add("V", lambda: g.vector.tensor_scalar(ap(o), src(), M2, M2 + SHIFT / 2, A.add, A.subtract), [win, off], [o], 60 + 1.56 * CY * n, nets[t], ext)
 
     o = add("Y", lambda: g.sync.dma_start(T.Z[:], T.kin[:]), [], [R("Z", 0, P)], 3000); ops[o]["dma"] = "ld"
     iota(R("AE", 0, P), [[6, 3], [18, E]], 6 * (P * r - HALF), 0)
@@ -240,7 +262,7 @@ def build(g, core, T, topo, r):
     for j in (0, 1, 5):
         setrow(pf(8), j, -KJ[j] - 0.5)
     setrow(pf(8), 6, 1.0)
-    ms(R("SLOT", 0, 128), 0.0); ms(R("COFF", 0, 16 * RO), 0)
+    ms(R("SLOT", 0, 128), 0.0); ms(R("SLOT", 384, 128), 0.0); ms(R("COFF", 0, 16 * RO), 0)
 
     def split(zi, s, bank):
         c = s * E
@@ -251,30 +273,31 @@ def build(g, core, T, topo, r):
     def plain(dr, b64, raw, wo, se):
         tt(dr, b64, raw, A.subtract); tt(wo, dr, wo, A.add); tt(wo, se, wo, A.mult); tt(raw, raw, wo, A.add)
 
-    def behind(first):
-        gate = max(i for i in range(first) if "noinc" in ops[i])
+    def behind(first, back=1):
+        gate = [i for i in range(first) if ops[i]["wr"] and ops[i]["wr"][0][0] == "TAB"][-back]
         for o in ops[first:]:
             o["after"].append(gate)
 
     def prep(t):
         s = t % 3; c = s * E
-        n = R("NI", c, E); sl = R("SLOT", 128, E); f1, f2, f3 = R("F1", 0, E), R("F2", 0, E), R("F3", 0, E)
+        n = R("NI", c, E); sl = R("SLOT", 384 * (t % 2) + 128, E); f1, f2, f3 = R("F1", 0, E), R("F2", 0, E), R("F3", 0, E)
         ts(R("Q1", 0, E), n, 1.0 / 3, A.mult, -1.0 / 3, A.add)
         f1 = R("P1", 256, E)
         aff("S", f1, n, float(REG), -float(REG * s)); aff("S", f2, R("Q1", 0, E), 1.0 - 3 * REG, 0.0)
         if s == 0:
             tt(sl, f1, f2, A.add)
         else:
-            tt(f3, f1, f2, A.add); ts(f1, f3, 0.0, A.is_lt, 3.0 * REG, A.mult); tt(sl, f3, f1, A.add)
+            tt(f3, f1, f2, A.add); act(f2, f3, F.Sign, bias=0.5); aff("S", f1, f2, -1.5 * REG, 1.5 * REG); tt(sl, f3, f1, A.add)
         cp(R("OFF", t * E, E), sl)
 
     def wrap(t):
         m = 16 * (t + 1)
-        for h4 in range(0, 16, 4):
-            mm([(R("P4", 496 + h, 1, 1, m), R("SLOT", 128 + 16 * h - 16 * t, m), R("ID", 17 * t, 1), True, True) for h in range(h4, h4 + 4)])
-        cp(R("COFF", 16 * t, 16, 1, m), R("P4", 496, 16, 1, m))
+        for h4 in range(0, 16, 2):
+            mm([(R("P5", 496 + h, 1, 1, m), R("SLOT", 384 * (t % 2) + 128 + 16 * h - 16 * t, m), R("ID", 17 * t, 1), True, True)
+                for h in range(h4, h4 + 2)])
+        cp(R("COFF", 16 * t, 16, 1, m), R("P5", 496, 16, 1, m))
         act(R("SEL", 128 * t, 128), ONE, F.Identity, scale=R("ID", 17 * t + 3, 1))
-        act(R("SELB", 128 * t, 128), ONE, F.Identity, scale=R("ID", 17 * t + 3, 1))
+        act(R("SELB", 128 * t, 128), R("SEL", 128 * t, 128), F.Identity, scale=-SHIFT / 2)
 
     for s in range(3):
         c = s * E; bk = "P%d" % (2 + s); b2 = "P%d" % (5 + s)
@@ -283,30 +306,36 @@ def build(g, core, T, topo, r):
         tt(R("EQ", c, E), R("NE", c, E), AEP[s], A.is_equal)
         mm([(R(b2, 0, E), IH[1.0 / 1024], R("SK", c, E), True, False), (R(b2, 0, E), IH[SHIFT], R("EQ", c, E), False, True)])
         tt(R("TAB", s * REG + r * E, E), R("NE", c, E), R(b2, 0, E), A.add)
-        for p in plist:
-            if p[1] == s:
-                send(s, p[2])
+        send(s, 0, E)
         for o in ops[first:]:
             o["up"] = 6000 - 2000 * s
     first = len(ops)
     prep(0); wrap(0)
     aff("S", R("RAW", 0, P), R("Z", 0, P), 1.0, 0.0)
-    prep(1); wrap(1); prep(2)
+    prep(1)
     behind(first)
     late = []
 
     for t in range(RO):
         s = t % 3; last = t == RO - 1
         for ci, (i0, w) in enumerate(CHUNKS):
-            gather("B", R("VB", i0, w), t, R("COFF", 16 * t + i0 // 16, w // 16))
-            o = ts(R("FL", i0, w), R("VB", i0, w), 16384.0, A.is_ge, -SHIFT, A.mult)
+            o = gather("B", R("VB", i0, w), t, R("COFF", 16 * t + i0 // 16, w // 16)); ops[o]["up"] = 9000 - UPB * ci
+            ops[o]["after"] += [i for i, x in enumerate(ops) if x.get("up", 0) < 0 and x["q"] == "V"]
+            o = act(R("FL", i0, w), R("VB", i0, w), F.Sign); ops[o]["up"] = 4000
             a = i0
             if ci == 0 and VG:
                 o2 = gather("V", R("G", 16 * a, 16 * VG), t, R("OFF", t * E + a, VG)); a += VG
-                ops[o2]["after"].append(o)
+                ops[o2]["after"].append(o - 1)
             while a < i0 + w:
-                n = min(SG, i0 + w - a)
-                gather("S", R("G", 16 * a, 16 * n), t, R("OFF", t * E + a, n)); a += n
+                n = min(SG0 if a == VG else SG, i0 + w - a)
+                if a < SUB:
+                    n = min(n, SUB - a)
+                o3 = gather("S", R("G", 16 * a, 16 * n), t, R("OFF", t * E + a, n)); a += n
+                ops[o3]["up"] = 3900 - 10 * a
+        if not last:
+            mark = len(ops); wrap(t + 1)
+            for o in ops[mark:]:
+                o["after"].append(o2)
         for ci, (i0, w) in enumerate(CHUNKS):
             pa, pb, pc, pd = ["P%d" % (4 * ci + j) for j in range(4)]
             X = lambda n, pn=128: R(n, i0, w, 1, pn)
@@ -315,18 +344,23 @@ def build(g, core, T, topo, r):
             first = len(ops)
             mm([(B, sel, X("VB"), True, False)])
             mm([(B, selb, X("FL"), False, True)])
-            tt(X("OWN"), R("NE", s * E + i0, w), B, A.is_equal)
-            tt(X("SKIP"), R("AE", s * E + i0, w), B, A.is_equal)
-            mm([(S1, IH[1.0], R("SK", s * E + i0, w), True, False)])
-            for k0, k1 in zip(KCUT, KCUT[1:]):
-                for k in range(k0, k1):
-                    tt(R("D", 16 * i0 + k * w, w), R("G", 16 * i0 + k, w, 16), B, A.subtract)
-                d4 = R("D", 16 * i0 + k0 * w, (k1 - k0) * w)
-                ts(d4, d4, HI, A.min, LO, A.max)
-                it = [(S1, R("WB", 15 - k, 128), R("D", 16 * i0 + k * w, w), False, k == 15) for k in range(k0, k1)]
-                if k0 == KCUT[1]:
-                    it = it + [(S1, IH[4096.0], X("OWN"), False, False)]
-                mm(it)
+            early = [tt(X("OWN"), R("NE", s * E + i0, w), B, A.is_equal), tt(X("SKIP"), R("AE", s * E + i0, w), B, A.is_equal)]
+            ZZ = R(pa, 256, w); NS = R(pc, 0, w)
+            early.append(mm([(ZZ, ZB, X("OWN"), True, False), (ZZ, ZB, X("SKIP"), False, False)]))
+            subs = [(i0, SUB), (i0 + SUB, w - SUB)] if ci == 0 and SUB else [(i0, w)]
+            for (j0, v) in subs:
+                sv = R(pb, j0 - i0, v); mark = len(ops)
+                mm([(sv, IH[1.0], R("SK", s * E + j0, v), True, False)])
+                for k0, k1 in zip(KCUT, KCUT[1:]):
+                    for k in range(k0, k1):
+                        tt(R("D", 16 * j0 + k * v, v), R("G", 16 * j0 + k, v, 16), R(pa, j0 - i0, v), A.subtract)
+                    d4 = R("D", 16 * j0 + k0 * v, (k1 - k0) * v)
+                    ts(d4, d4, HI, A.min, LO, A.max)
+                    it = [(sv, R("WB", 15 - k, 128), R("D", 16 * j0 + k * v, v), False, k == 15) for k in range(k0, k1)]
+                    if k0 == KCUT[1]:
+                        it = [(sv, IH[4096.0], R("OWN", j0, v), False, False)] + it
+                    for j in range(0, len(it), MMN):
+                        mm(it[j:j + MMN])
             if not last:
                 mm([(NV, sel, X("VB"), True, False), (NV, selb, X("FL"), False, False)])
             qs = PLACE[ci]
@@ -343,9 +377,10 @@ def build(g, core, T, topo, r):
             VO = R(pc, 0, w, 1, 8); vw = lambda j: R("VW", 8 * j, 8)
             for j in range(1, 6):
                 aff(qs[2 + j], X("R%d" % j), X("W"), 1.0, RC[j] - 0.5)
-            mm([(VO, vw(0), X("W"), True, False), (VO, vw(6), X("TES"), False, False)])
-            mm([(VO, vw(1), X("R1"), False, False), (VO, vw(2), X("R2"), False, False)])
-            mm([(VO, vw(j), X("R%d" % j), False, j == 5) for j in (3, 4, 5)])
+            mm([(VO, vw(0), X("W"), True, False)])
+            mm([(VO, vw(6), X("TES"), False, False), (VO, vw(1), X("R1"), False, False)])
+            mm([(VO, vw(j), X("R%d" % j), False, False) for j in (2, 3)])
+            mm([(VO, vw(j), X("R%d" % j), False, j == 5) for j in (4, 5)])
             mm([(XP, IH[1025.0], X("W"), True, False), (XP, IH[-1033.0], X("TES"), False, False)])
             act(X("SG", 8), VO, F.Sign, bias=pf(8, 8))
             mm([(XP, WX, X("SG", 6), False, True)])
@@ -358,8 +393,6 @@ def build(g, core, T, topo, r):
             aff(qs[9], X("SI"), X("U"), 0x111111 / 2.0 ** 20, 1.5 * 2 ** 23 + 8)
             ts(X("U"), X("SI"), 15, A.bitwise_and)
             act(X("EX"), X("U"), F.Exp, bias=pf(1), scale=17 * LN2)
-            ZZ = R(pc, 0, w); NS = R(pc, 256, w)
-            mm([(ZZ, ZB, X("OWN"), True, False), (ZZ, ZB, X("SKIP"), False, False)])
             mm([(ZZ, ZM, X("EX"), False, True)])
             ts(X("SE"), ZZ, 1.5 * 2.0 ** -62, A.is_gt)
             if not last:
@@ -370,13 +403,19 @@ def build(g, core, T, topo, r):
                 tt(NV, X("SE"), NV, A.mult)
                 tt(X("M1"), R("TAB", t * REG + r * E + i0, w), NS, A.mult)
                 tt(R("TAB", (t + 3) * REG + r * E + i0, w), X("M1"), NV, A.add)
-                send(t + 3, i0)
+                send(t + 3, i0, i0 + w)
             for o in ops[first:]:
                 o["up"] = UP[ci]
-            M = 1.5 * 2 ** 23; B64 = R(pa, 256, w); raw = R("RAW", 3 * i0 + s, w, 3)
+            for o in early:
+                ops[o]["up"] += UPO
+            M = 1.5 * 2 ** 23; B64 = R(pc, 256, w); raw = R("RAW", 3 * i0 + s, w, 3)
             act(X("TB"), B, F.Identity, bias=64.0 * HALF + M, scale=32.0 / 3)
             act(B64, X("TB"), F.Identity, bias=-M)
             late.append((X("DR"), B64, raw, WO, X("SE")))
+            if ci == 0 and not last:
+                first = len(ops); plain(*late.pop()); behind(first)
+                for o in ops[first:]:
+                    o["up"] = -20000
             if last:
                 plain(*late.pop())
                 o = add("Y", lambda i0=i0, w=w: g.sync.dma_start(T.yk[:, 3 * i0:3 * (i0 + w)], T.RAW[:, 3 * i0:3 * (i0 + w)]),
@@ -386,13 +425,19 @@ def build(g, core, T, topo, r):
             first = len(ops)
             while late:
                 plain(*late.pop(0))
-            if t != 1:
-                wrap(max(t + 1, 2))
-            if t in (1, 2):
-                prep(t + 2)
-            if t < 2:
-                cp(R("ZI", 0, E), R("RAW", t, E, 3)); split(R("ZI", 0, E), t, "P1")
+            for o in ops[first:]:
+                o["up"] = -20000
             behind(first)
+            first = len(ops)
+            if t in (1, 2):
+                split(R("ZI", E * (t - 1), E), t - 1, "P1")
+            if t <= 2:
+                prep(t + 2)
+            behind(first, 2)
+            for o in ops[first:]:
+                o["up"] = -10000
+            if t < 2:
+                aff("S", R("ZI", E * t, E), R("RAW", t, E, 3), 1.0, 0.0)
     return ops, sent[0]
 
 
@@ -420,6 +465,14 @@ def order(ops):
     for i in range(n - 1, -1, -1):
         pr[i] = ops[i]["cost"] + max([pr[j] + HOP for j in succ[i]] or [0])
     pr = [p + o.get("up", 0) for p, o in zip(pr, ops)]
+    tie = {}
+    for i, o in enumerate(ops):
+        k = (o["q"],) + tuple(o["wr"][-1][0:1] + (o["wr"][-1][1] % REG % 768,) if o["wr"] else ())
+        if k not in tie:
+            tie[k] = ((len(tie) + 1) * 7919 + SEED * 104729) * 2654435761 % 1000003 / 1000003.0
+        pr[i] += JIT * tie[k]
+        if o.get("up", 0) < 0:
+            pr[i] = o["up"] - i
     left = [len(d) for d in deps]; ready = [i for i in range(n) if not left[i]]
     free = {}; end = [0.0] * n; bank = {}; seq = []
     while ready:
@@ -435,7 +488,7 @@ def order(ops):
                             s = max(s, end[j] + HOP)
             st[i] = s
         b = min(ready, key=lambda i: (st[i], -pr[i])); q = ops[b]["q"]
-        top = max([i for i in ready if ops[i]["q"] == q and st[i] <= st[b] + LOOK * ops[b]["cost"]], key=lambda i: pr[i])
+        top = max([i for i in ready if ops[i]["q"] == q and st[i] <= st[b] + (LOOK if ops[b].get("up", 0) >= 0 else BGL) * ops[b]["cost"]], key=lambda i: pr[i])
         if pr[top] > pr[b] + GAP or st[top] <= st[b] + 40:
             b = top
         for x in ops[b]["rd"] + ops[b]["wr"]:

@@ -1,33 +1,35 @@
 import math
+import numpy
 from concourse.bass import DstId, RemoteDMATransfer
 from concourse.mybir import AluOpType as A, ActivationFunctionType as F
 
 P, E, RO, NR = 768, 256, 5, 6
 REG = NR * E
 HALF = NR * P // 2
-CHUNKS = [(0, 128), (128, 128)]
-VG = 48
-SG0 = 20
-UPO = 0
-UPB = 0
-SUB = 0
-BGL = 0.7
-MMN = 2
-SEED = 0
-JIT = 0
-SG = 40
 CEN = 684.0
-HI, LO = 3412.0 / 1024, -4780.0 / 1024
+U10 = 1.0 / 1024
+HI, LO = 3412.0 * U10, -4780.0 * U10
 SHIFT = 32768.0
 LN2 = math.log(2.0)
 RC = [0, 4096.0, 2048.0, 8192.0, 32768.0, 131072.0, 0.0]
-NH = 8
-UP = [2000, 0]
-HOP, LOOK, GAP, PEC = 120, 0.3, 300, 0.7
-KCUT = [0, 5, 10, 14, 16]
-PLACE = ["SSSSSSSSSSS", "VVVVSVSVVVV"]
-VG, SG0, SG, UP, UPO, UPB, KCUT, MMN, LOOK, GAP = 56, 8, 40, [1500, 0], 0, 0, [0, 6, 11, 15, 16], 8, 0.3, 300
-PLACE = ["SSSSSSSSSSS", "VVSVSVSVVVV"]
+NH = 20
+HOP, PEC = 120, 0.7
+FAR0, FAR1, NEAR0, NEAR1 = ("far", 0), ("far", 1), ("near", 0), ("near", 1)
+CFG = {
+    "CH": [(0, 128), (128, 128)],
+    "CHL": [(0, 128), (128, 128)],
+    "WAY": [[FAR0 + ("in",), FAR1 + ("out",)], [None]],
+    "START": [(0, 0, 256, [FAR0 + ("in",), FAR1 + ("out",)]), (1, 0, 256, [NEAR0 + ("out",), FAR0 + ("in",)]),
+              (2, 0, 256, [NEAR1 + ("in",), None])],
+    "VG": 56, "SG0": 8, "SG": 40,
+    "KCUT": [[0, 4, 8, 12, 16]] * 3, "MMN": 8,
+    "UP": [1500, 0, -500], "UPO": 0, "UPW": 1.0, "PASSES": 3, "SEED": 0, "JIT": 500.0, "JP": 0.1,
+    "PLACE": ["SSSSSSSSSSS", "VVSVSVSVVVS", "VVSVSVSVVVS"],
+    "FL": "VV", "REP": [1, 1],
+}
+CFG.update({"VG": 48, "SG0": 40, "SG": 48, "KCUT": [[0, 6, 12, 14, 16], [0, 4, 8, 12, 16], [0, 4, 8, 12, 16]], "MMN": 4,
+            "PLACE": ["SSSSSSSSSSS", "VVSVSVSVSVS", "VVSVSVSVVVS"], "REP": [2, 4], "BKW": 1, "BK0": 3, "BKP": 2, "PASSES": 150,
+            "NVP": "PPV"})
 
 SCRATCH = {
     "TAB": ("sbuf", [128, 7 * REG], "float32"), "Z": ("sbuf", [128, P], "int32"), "RAW": ("sbuf", [128, P], "float32"),
@@ -35,37 +37,37 @@ SCRATCH = {
     "NE": ("sbuf", [128, P], "float32"), "SK": ("sbuf", [128, P], "float16"), "AE": ("sbuf", [128, P], "float32"),
     "NI": ("sbuf", [128, P], "int32"), "OFF": ("sbuf", [128, RO * E], "uint16"), "COFF": ("sbuf", [128, RO * 16], "uint16"),
     "SEL": ("sbuf", [128, RO * 128], "float32"), "SELB": ("sbuf", [128, RO * 128], "bfloat16"),
-    "SLOT": ("sbuf", [128, 768], "float32"), "ZI": ("sbuf", [128, 2 * E], "int32"),
-    "I1": ("sbuf", [128, P], "int32"), "I2": ("sbuf", [128, P], "int32"), "EQ": ("sbuf", [128, P], "float16"),
-    "Q1": ("sbuf", [128, E], "int32"), "F1": ("sbuf", [128, E], "float32"), "F2": ("sbuf", [128, E], "float32"),
-    "F3": ("sbuf", [128, E], "float32"),
+    "SLOT": ("sbuf", [128, 768], "float32"), "ZI": ("sbuf", [128, 2 * E], "int32"), "AN": ("sbuf", [128, E], "float32"),
+    "I1": ("sbuf", [128, P], "int32"), "I2": ("sbuf", [128, P], "int32"), "EQ": ("sbuf", [128, P], "bfloat16"),
+    "MF": ("sbuf", [128, P], "bfloat16"), "NP": ("sbuf", [128, P], "float32"),
+    "Q1": ("sbuf", [128, E], "int32"), "F2": ("sbuf", [128, E], "float32"), "F3": ("sbuf", [128, E], "float32"),
     "VB": ("sbuf", [128, E], "float32"), "FL": ("sbuf", [128, E], "bfloat16"),
     "OWN": ("sbuf", [128, E], "float16"), "SKIP": ("sbuf", [128, E], "float16"),
     "SI": ("sbuf", [128, E], "int32"), "U": ("sbuf", [128, E], "int32"), "W": ("sbuf", [128, E], "float16"),
     "TES": ("sbuf", [128, E], "float16"), "R1": ("sbuf", [128, E], "float16"), "R2": ("sbuf", [128, E], "bfloat16"),
     "R3": ("sbuf", [128, E], "bfloat16"), "R4": ("sbuf", [128, E], "bfloat16"), "R5": ("sbuf", [128, E], "bfloat16"),
-    "SG": ("sbuf", [128, E], "bfloat16"), "QF": ("sbuf", [128, E], "float32"), "EX": ("sbuf", [128, E], "bfloat16"),
-    "SE": ("sbuf", [128, E], "float32"), "M1": ("sbuf", [128, E], "float32"), "TB": ("sbuf", [128, E], "float32"),
+    "SG": ("sbuf", [128, E], "bfloat16"), "EX": ("sbuf", [128, E], "bfloat16"),
+    "NV": ("sbuf", [128, E], "float32"), "M1": ("sbuf", [128, E], "float32"), "TB": ("sbuf", [128, E], "int32"),
     "DR": ("sbuf", [128, E], "float32"),
     "ONE": ("sbuf", [128, 128], "float32"), "ID": ("sbuf", [128, 128], "float32"), "COL": ("sbuf", [128, 144], "float32"),
-    "WB": ("sbuf", [128, 144], "float16"), "IH": ("sbuf", [128, 7 * 128], "float16"), "ZM": ("sbuf", [128, 256], "bfloat16"),
-    "BLK": ("sbuf", [128, 128], "float32"), "BI": ("sbuf", [128, 128], "int32"),
-    "VW": ("sbuf", [128, 56], "bfloat16"), "WS": ("sbuf", [128, 384], "bfloat16"),
+    "WB": ("sbuf", [128, 144], "float16"), "IH": ("sbuf", [128, 4 * 128], "float16"), "IB": ("sbuf", [128, 256], "bfloat16"),
+    "ZM": ("sbuf", [128, 6 * 128], "bfloat16"), "BLK": ("sbuf", [128, 4 * 128], "float32"), "BI": ("sbuf", [128, 128], "int32"),
+    "VW": ("sbuf", [128, 56], "bfloat16"), "WS": ("sbuf", [128, 512], "bfloat16"),
     "PI": ("sbuf", [128, 8], "int32"), "PF": ("sbuf", [128, 16], "float32"),
-    "LAND": ("sbuf", [128, NH * E], "float32"),
+    "LAND": ("sbuf", [128, NH * 128], "float32"),
 }
 for _b in range(8):
     SCRATCH["P%d" % _b] = ("psum", [128, 512], "float32")
-SEMAPHORES = ["sV", "sS", "sP", "sG", "ld", "st0", "st1", "sent"] + ["arr%d" % t for t in range(RO)] + ["h%d" % k for k in range(NH)]
+SEMAPHORES = ["sV", "sS", "sP", "sG", "ld", "st0", "st1", "st2", "sent"] + ["arr%d" % t for t in range(RO)] + ["h%d" % k for k in range(NH)]
 
 
 def pieces():
-    out = [(0, 0, 0, E, ("far", 0, "all")), (0, 1, 0, E // 2, ("far", 1, "in")), (0, 1, E // 2, E // 2, ("near", 0, "out")), (0, 2, 0, E, None)]
-    h = CHUNKS[0][1] // 2
+    out = []
+    for (s, c0, w, ways) in CFG["START"]:
+        out += [(0, s, c0 + j * (w // len(ways)), w // len(ways), y) for j, y in enumerate(ways)]
     for t in range(RO - 1):
-        out.append((t + 1, t + 3, 0, h, ("far", t % 2, "in")))
-        out.append((t + 1, t + 3, h, h, None))
-        out.append((t + 1, t + 3, CHUNKS[1][0], CHUNKS[1][1], None))
+        for (c0, w), ways in zip(CFG["CH"], CFG["WAY"]):
+            out += [(t + 1, t + 3, c0 + j * (w // len(ways)), w // len(ways), y) for j, y in enumerate(ways)]
     return out
 
 
@@ -105,7 +107,7 @@ def helper_program(g, core, T, topo):
             ds = hs[core]; m = topo.mask(core, ds[0]); col = reg * REG + r * E + c0
             g.wait_ge(T.sem["h%d" % k], ones(inmask(rc, core, way, T, topo)))
             g.remote_dma_fused([RemoteDMATransfer(dst_ids=[dst(d, topo) for d in ds], dma_engine_mask=m, remote_sem=T.sem["arr%d" % arr],
-                                                  src=T.LAND[:, k * E:k * E + w], dsts=[T.TAB[:, col:col + w] for d in ds])], local_sem=T.sem.sent)
+                                                  src=T.LAND[:, k * 128:k * 128 + w], dsts=[T.TAB[:, col:col + w] for d in ds])], local_sem=T.sem.sent)
             sent += ones(m)
         k += 1
     if sent:
@@ -115,6 +117,7 @@ def helper_program(g, core, T, topo):
 def build(g, core, T, topo, r):
     ops = []
     CY = 1.04
+    C = CFG
 
     def ap(x):
         n, a, b, s, pn = x
@@ -122,6 +125,9 @@ def build(g, core, T, topo, r):
 
     def R(n, a, w, s=1, pn=128):
         return (n, a, a + (w - 1) * s + 1, s, pn)
+
+    def RG(a, w):
+        return R("G", 16 * a, 16 * w)
 
     def wd(x):
         return (x[2] - x[1] - 1) // x[3] + 1
@@ -190,7 +196,7 @@ def build(g, core, T, topo, r):
         return add("G", lambda: g.affine_select(ap(o), ap(o), [[0, wd(o)]], A.not_equal, v, -j, 1), [o], [o], 200 + 2 * CY * wd(o))
 
     others = [c for c in T.cores if c != core]
-    sent = [0]; hk = [0]; nets = {}; need = {}
+    sent = [0]; nets = {}; need = {}
     plist = pieces()
     for (arr, reg, c0, w, way) in plist:
         need[arr] = need.get(arr, 0) + sum(ones(topo.mask(c, core)) for c in others)
@@ -204,48 +210,69 @@ def build(g, core, T, topo, r):
                 ds = others; sem = T.sem["arr%d" % arr]; to = src; m = topo.mask(core, ds[0])
             else:
                 k = [x for x in plist if x[4] is not None].index(p)
-                ds = list(helpers(core, way, T, topo)); sem = T.sem["h%d" % k]; to = R("LAND", k * E, w); m = inmask(core, ds[0], way, T, topo)
+                ds = list(helpers(core, way, T, topo)); sem = T.sem["h%d" % k]; to = R("LAND", k * 128, w); m = inmask(core, ds[0], way, T, topo)
             sent[0] += ones(m); tr.append((ds, m, sem, src, to))
         o = add("G", lambda: g.remote_dma_fused([RemoteDMATransfer(dst_ids=[dst(d, topo) for d in ds], dma_engine_mask=m, remote_sem=sem,
                                                                    src=ap(src), dsts=[ap(to) for d in ds]) for (ds, m, sem, src, to) in tr],
                                                 local_sem=T.sem.sent), [x[3] for x in tr], [], 800)
         ops[o]["noinc"] = True
         for (arr, _, a, w, way) in ps_:
-            n = add("N", None, [], [], 600 + w * 512 * 5 / 250.0, [o]) if way is None else o
-            nets.setdefault(arr, []).append(add("N%d" % len(ops), None, [], [], 1200 if way is None else 4000 + w * 512 * 4 / 200.0, [n]))
+            row = 10 + w * 4 / 30.0
+            n = add("N", None, [], [], 300 + 80 * row, [o]) if way is None else o
+            nets.setdefault(arr, []).append(add("N%d" % len(ops), None, [], [], 1200 if way is None else 3600 + 80 * row, [n]))
 
     def gather(q, o, t, off):
         win = R("TAB", t * REG, 3 * REG); n = wd(o); ext = ("arr%d" % t, need[t])
         src = lambda: ap(win).indirect(ap(off))
         if q == "S":
-            return add("S", lambda: g.scalar.activation(ap(o), src(), F.Identity), [win, off], [o], 80 + 1.56 * CY * n, nets[t], ext)
+            return add("S", lambda: g.scalar.activation(ap(o), src(), F.Identity, scale=U10), [win, off], [o], 80 + 1.56 * CY * n, nets[t], ext)
         if q == "V":
-            return add("V", lambda: g.vector.tensor_copy(ap(o), src()), [win, off], [o], 60 + 1.56 * CY * n, nets[t], ext)
-        M2 = 1.5 * 2 ** 24
-        return add("V", lambda: g.vector.tensor_scalar(ap(o), src(), M2, M2 + SHIFT / 2, A.add, A.subtract), [win, off], [o], 60 + 1.56 * CY * n, nets[t], ext)
+            return add("V", lambda: g.vector.tensor_scalar(ap(o), src(), U10, None, A.mult), [win, off], [o], 60 + 1.56 * CY * n, nets[t], ext)
+        M2 = 1.5 * 2 ** 34
+        return add("V", lambda: g.vector.tensor_scalar(ap(o), src(), M2, M2 + 512 * SHIFT, A.add, A.subtract), [win, off], [o],
+                   60 + 1.56 * CY * n, nets[t], ext)
+
+    def rank_up(first, v):
+        for o in ops[first:]:
+            o["up"] = v
 
     o = add("Y", lambda: g.sync.dma_start(T.Z[:], T.kin[:]), [], [R("Z", 0, P)], 3000); ops[o]["dma"] = "ld"
-    iota(R("AE", 0, P), [[6, 3], [18, E]], 6 * (P * r - HALF), 0)
-    act(R("P0", 0, 512), R("AE", 0, 512), F.Identity); act(R("P1", 0, 256), R("AE", 512, 256), F.Identity)
-    AEP = [R("P0", 0, E), R("P0", 256, E), R("P1", 0, E)]
-    ONE = R("ONE", 0, 128); ID = R("ID", 0, 128)
+    first = len(ops)
+    ONE = R("ONE", 0, 128); ID = R("ID", 0, 128); AN = R("AN", 0, E)
+    iota(AN, [[3, E]], P * r, 0)
     ms(ONE, 1.0)
     add("G", lambda: g.affine_select(ap(ID), ap(ONE), [[-1, 128]], A.is_equal, 0.0, 0, 1), [ONE], [ID], 470)
+    AP_ = [R("P0", 0, E), R("P0", 256, E), R("P1", 0, E)]
+    for s in range(3):
+        aff("S", AP_[s], AN, 1.0, float(s))
+    I31, I25 = R("IB", 0, 128), R("IB", 128, 128)
+    ts(I31, ID, 31.0, A.mult); ts(I25, ID, 1024 * SHIFT, A.mult)
+    rank_up(first, 9000)
     IH = {}
-    for j, v in enumerate([1.0 / 1024, SHIFT, 1.0, 4096.0, 1025.0, -1033.0]):
+    for j, v in enumerate([1.0, 4096.0, 1025.0, -1033.0]):
         IH[v] = R("IH", 128 * j, 128); act(IH[v], ID, F.Identity, scale=v)
+    for s in range(3):
+        aff("S", R("AE", s * E, E), AN, 6.0, 6.0 * (s - HALF))
     pi = lambda j: R("PI", j, 1)
     pf = lambda j, pn=128: R("PF", j, 1, 1, pn)
     iota(pi(0), [[0, 1]], 0, 1)
-    ts(pi(1), pi(0), -16, A.bitwise_and); cp(pf(0), pi(1))
+    ts(pi(1), pi(0), -16, A.bitwise_and); cp(pf(0), pi(1)); cp(pf(1), pi(0))
     iota(R("COL", 0, 144), [[1, 144]], -15, 0)
     ts(R("WB", 0, 144), R("COL", 0, 144), pf(0), A.is_equal, 1024.0, A.mult)
     iota(R("BI", 0, 128), [[16, 8], [0, 16]], 0, 0)
-    ts(R("BLK", 0, 128), R("BI", 0, 128), pf(0), A.is_equal, -0.5, A.mult)
-    ZM, ZB = R("ZM", 0, 128), R("ZM", 128, 128)
-    tt(ZM, R("BLK", 0, 128), ID, A.add); act(ZB, ZM, F.Identity, scale=2.0 ** 70)
-    ts(pi(2), pi(0), 15, A.bitwise_and); ts(pf(1), pi(2), 180.0, A.add, -LN2, A.mult)
+    BL = [R("BLK", 128 * j, 128) for j in range(4)]
+    ZM, ZN, ZB, ZC, TH, TN = [R("ZM", 128 * j, 128) for j in range(6)]
+    ts(BL[0], R("BI", 0, 128), pf(0), A.is_equal)
+    ts(BL[1], R("COL", 15, 128), pf(1), A.is_gt, -63.0 / 32, A.mult); ts(BL[1], BL[1], -1.0 / 32, A.add)
+    tt(BL[1], BL[1], BL[0], A.mult); ts(BL[2], ID, 33.0 / 32, A.mult); tt(ZM, BL[1], BL[2], A.add)
+    act(ZN, ZM, F.Identity, scale=-1.0)
+    ts(BL[3], BL[0], -0.5, A.mult); tt(BL[3], BL[3], ID, A.add)
+    act(ZB, BL[3], F.Identity, scale=2.0 ** 76); act(ZC, BL[3], F.Identity, scale=-2.0 ** 76)
     ts(pi(3), pi(0), 7, A.bitwise_and); ts(pi(4), pi(0), 1, A.bitwise_and)
+    ts(pf(9), pi(3), 6.0, A.is_equal, 2.0 ** 28, A.mult)
+    TH, TN = TH[:4] + (8,), TN[:4] + (8,)
+    act(TN, R("ONE", 0, 128, 1, 8), F.Identity, scale=pf(9, 8)); act(TH, TN, F.Identity, scale=-1.0)
+    TH, TN = TH[:4] + (7,), TN[:4] + (7,)
     ts(pf(2), pi(3), 2 * LN2, A.mult, -11 * LN2, A.add)
     ts(pf(3), pi(4), 10 * LN2, A.mult, 10 * LN2, A.add); tt(pf(4), pf(2), pf(3), A.add)
     ts(pf(5), pi(3), 3.0, A.is_ge, -5 * LN2, A.mult); ts(pf(6), pf(5), 10 * LN2, A.add); tt(pf(7), pf(2), pf(6), A.add)
@@ -253,7 +280,8 @@ def build(g, core, T, topo, r):
     for wv, c in ((WX, 4), (WE, 2), (WR, 7)):
         act(wv, R("ONE", 0, 128, 1, 8), F.Exp, scale=pf(c, 8))
     setrow(WE, 6, (682.5 - CEN) / 1024); setrow(WR, 6, 31.5)
-    WX, WE, WR = R("WS", 0, 128, 1, 6), R("WS", 128, 128, 1, 7), R("WS", 256, 128, 1, 7)
+    WX, WE, WR, WK = R("WS", 0, 128, 1, 6), R("WS", 128, 128, 1, 7), R("WS", 256, 128, 1, 7), R("WS", 384, 128, 1, 7)
+    act(WK, WE, F.Identity, scale=1024.0)
     ms(R("VW", 0, 56), 0.0); ms(R("VW", 0, 1), 2.0); ms(R("VW", 48, 1), -3.0); ms(R("VW", 49, 5), -1.0)
     for j in range(1, 6):
         ms(R("VW", 8 * j + j, 1), 2.0 / 4 ** j); ms(R("VW", 8 * j + j - 1, 1), -2.0 / 4 ** (j - 1))
@@ -264,25 +292,24 @@ def build(g, core, T, topo, r):
     setrow(pf(8), 6, 1.0)
     ms(R("SLOT", 0, 128), 0.0); ms(R("SLOT", 384, 128), 0.0); ms(R("COFF", 0, 16 * RO), 0)
 
+    def names(zi, c, w):
+        aff("S", R("NI", c, w), zi, 1.0 / 64, -31.5 / 64); ts(R("I1", c, w), zi, 42, A.bitwise_and)
+
     def split(zi, s, bank):
         c = s * E
-        ts(R("I1", c, E), zi, 42, A.bitwise_and); aff("S", R(bank, 0, E), R("I1", c, E), 31.0, -CEN)
-        ts(R("I2", c, E), zi, 63, A.bitwise_and); tt(R("SK", c, E), R("I2", c, E), R(bank, 0, E), A.add)
-        ts(R("NI", c, E), zi, 6, A.arith_shift_right); aff("S", R("NE", c, E), R("NI", c, E), 6.0, -6.0 * HALF)
-
-    def plain(dr, b64, raw, wo, se):
-        tt(dr, b64, raw, A.subtract); tt(wo, dr, wo, A.add); tt(wo, se, wo, A.mult); tt(raw, raw, wo, A.add)
+        aff("S", bank, R("I1", c, E), 31.0, -CEN)
+        ts(R("I2", c, E), zi, 63, A.bitwise_and); tt(R("SK", c, E), R("I2", c, E), bank, A.add)
+        aff("S", R("NE", c, E), R("NI", c, E), 6.0, -6.0 * HALF)
 
     def behind(first, back=1):
         gate = [i for i in range(first) if ops[i]["wr"] and ops[i]["wr"][0][0] == "TAB"][-back]
         for o in ops[first:]:
             o["after"].append(gate)
 
-    def prep(t):
+    def prep(t, f1):
         s = t % 3; c = s * E
-        n = R("NI", c, E); sl = R("SLOT", 384 * (t % 2) + 128, E); f1, f2, f3 = R("F1", 0, E), R("F2", 0, E), R("F3", 0, E)
-        ts(R("Q1", 0, E), n, 1.0 / 3, A.mult, -1.0 / 3, A.add)
-        f1 = R("P1", 256, E)
+        n = R("NI", c, E); sl = R("SLOT", 384 * (t % 2) + 128, E); f2, f3 = R("F2", 0, E), R("F3", 0, E)
+        aff("S", R("Q1", 0, E), n, 1.0 / 3, -1.0 / 3)
         aff("S", f1, n, float(REG), -float(REG * s)); aff("S", f2, R("Q1", 0, E), 1.0 - 3 * REG, 0.0)
         if s == 0:
             tt(sl, f1, f2, A.add)
@@ -290,80 +317,90 @@ def build(g, core, T, topo, r):
             tt(f3, f1, f2, A.add); act(f2, f3, F.Sign, bias=0.5); aff("S", f1, f2, -1.5 * REG, 1.5 * REG); tt(sl, f3, f1, A.add)
         cp(R("OFF", t * E, E), sl)
 
-    def wrap(t):
+    def wrap(t, bank):
         m = 16 * (t + 1)
-        for h4 in range(0, 16, 2):
-            mm([(R("P5", 496 + h, 1, 1, m), R("SLOT", 384 * (t % 2) + 128 + 16 * h - 16 * t, m), R("ID", 17 * t, 1), True, True)
-                for h in range(h4, h4 + 2)])
-        cp(R("COFF", 16 * t, 16, 1, m), R("P5", 496, 16, 1, m))
-        act(R("SEL", 128 * t, 128), ONE, F.Identity, scale=R("ID", 17 * t + 3, 1))
-        act(R("SELB", 128 * t, 128), R("SEL", 128 * t, 128), F.Identity, scale=-SHIFT / 2)
+        for h4 in range(0, 16, 4):
+            mm([(R(bank, 496 + h, 1, 1, m), R("SLOT", 384 * (t % 2) + 128 + 16 * h - 16 * t, m), R("ID", 17 * t, 1), True, True)
+                for h in range(h4, h4 + 4)])
+        cp(R("COFF", 16 * t, 16, 1, m), R(bank, 496, 16, 1, m))
+        ts(pf(10 + t), R("ID", 17 * t + 3, 1), U10, A.mult)
+        act(R("SEL", 128 * t, 128), ONE, F.Identity, scale=pf(10 + t))
+        act(R("SELB", 128 * t, 128), R("SEL", 128 * t, 128), F.Identity, scale=-512 * SHIFT)
 
-    for s in range(3):
-        c = s * E; bk = "P%d" % (2 + s); b2 = "P%d" % (5 + s)
+    for j, (s, c0, w, ways) in enumerate(C["START"]):
+        c = s * E + c0; zi = R("Z", 3 * c0 + s, w, 3); b1 = R("P%d" % (2 + j % 3), 0, w); b2 = R("P%d" % (5 + j % 3), 0, w)
         first = len(ops)
-        split(R("Z", s, E, 3), s, bk)
-        tt(R("EQ", c, E), R("NE", c, E), AEP[s], A.is_equal)
-        mm([(R(b2, 0, E), IH[1.0 / 1024], R("SK", c, E), True, False), (R(b2, 0, E), IH[SHIFT], R("EQ", c, E), False, True)])
-        tt(R("TAB", s * REG + r * E, E), R("NE", c, E), R(b2, 0, E), A.add)
-        send(s, 0, E)
-        for o in ops[first:]:
-            o["up"] = 6000 - 2000 * s
+        names(zi, c, w)
+        aff("S", R("MF", c, w), R("I1", c, w), 1.0, 0.0)
+        tt(R("EQ", c, w), R("NI", c, w), R(AP_[s][0], AP_[s][1] + c0, w), A.is_equal)
+        aff("S", R("NP", c, w), R("NI", c, w), 6080.0, -6144.0 * HALF - CEN)
+        mm([(b1, I25, R("EQ", c, w), True, False), (b1, I31, R("MF", c, w), False, True)])
+        tt(b2, zi, R("NP", c, w), A.add) if C.get("E2") else tt(b2, R("NP", c, w), b1, A.add)
+        tt(R("TAB", s * REG + r * E + c0, w), zi, b2, A.add)
+        send(s, c0, c0 + w)
+        rank_up(first, 8000 - 1500 * j)
     first = len(ops)
-    prep(0); wrap(0)
+    prep(0, R("P1", 256, E)); wrap(0, "P7")
+    for s in range(3):
+        split(R("Z", s, E, 3), s, R("P%d" % (2 + s), 256, E))
     aff("S", R("RAW", 0, P), R("Z", 0, P), 1.0, 0.0)
-    prep(1)
-    behind(first)
-    late = []
+    prep(1, R("P1", 256, E))
+    behind(first, C.get("BK0", 1))
 
+    BANK = [("P0", "P2", "P3"), ("P1", "P4", "P5"), ("P1", "P6", "P7")]
     for t in range(RO):
         s = t % 3; last = t == RO - 1
-        for ci, (i0, w) in enumerate(CHUNKS):
-            o = gather("B", R("VB", i0, w), t, R("COFF", 16 * t + i0 // 16, w // 16)); ops[o]["up"] = 9000 - UPB * ci
-            ops[o]["after"] += [i for i, x in enumerate(ops) if x.get("up", 0) < 0 and x["q"] == "V"]
-            o = act(R("FL", i0, w), R("VB", i0, w), F.Sign); ops[o]["up"] = 4000
+        CH = C["CHL"] if last else C["CH"]
+        sel, selb = R("SEL", 128 * t, 128), R("SELB", 128 * t, 128)
+        h1 = CH[1][0]
+        for hi, (i0, w) in enumerate([(0, h1), (h1, E - h1)]):
+            o = gather("B", R("VB", i0, w), t, R("COFF", 16 * t + i0 // 16, w // 16)); ops[o]["up"] = 9000
+            ops[o]["after"] += [i for i, x in enumerate(ops) if x.get("up", 0) < -5000 and x["q"] == "V"]
+            if C["FL"][hi] == "S":
+                o = act(R("FL", i0, w), R("VB", i0, w), F.Sign)
+            else:
+                o = ts(R("FL", i0, w), R("VB", i0, w), 1.0, A.min, -1.0, A.max)
+            ops[o]["up"] = 8000
+            first = len(ops); rep = C["REP"][hi]
+            for j in range(rep - 1, -1, -1):
+                B = R("P%d" % hi, j, w, rep)
+                mm([(B, sel, R("VB", i0, w), True, False)])
+                mm([(B, selb, R("FL", i0, w), False, True)])
+            rank_up(first, 8000 - 1000 * hi)
             a = i0
-            if ci == 0 and VG:
-                o2 = gather("V", R("G", 16 * a, 16 * VG), t, R("OFF", t * E + a, VG)); a += VG
+            if hi == 0 and C["VG"]:
+                o2 = gather("V", RG(a, C["VG"]), t, R("OFF", t * E + a, C["VG"])); a += C["VG"]
                 ops[o2]["after"].append(o - 1)
             while a < i0 + w:
-                n = min(SG0 if a == VG else SG, i0 + w - a)
-                if a < SUB:
-                    n = min(n, SUB - a)
-                o3 = gather("S", R("G", 16 * a, 16 * n), t, R("OFF", t * E + a, n)); a += n
+                n = min(C["SG0"] if a == C["VG"] else C["SG"], i0 + w - a)
+                n = min([n] + [c - a for (c, _) in CH if c > a])
+                o3 = gather("S", RG(a, n), t, R("OFF", t * E + a, n)); a += n
                 ops[o3]["up"] = 3900 - 10 * a
-        if not last:
-            mark = len(ops); wrap(t + 1)
-            for o in ops[mark:]:
-                o["after"].append(o2)
-        for ci, (i0, w) in enumerate(CHUNKS):
-            pa, pb, pc, pd = ["P%d" % (4 * ci + j) for j in range(4)]
-            X = lambda n, pn=128: R(n, i0, w, 1, pn)
-            sel, selb = R("SEL", 128 * t, 128), R("SELB", 128 * t, 128)
-            B = R(pa, 0, w); S1 = R(pb, 0, w); XP = R(pb, 256, w); NV = R(pd, 0, w); WO = R(pd, 256, w)
+        late = []
+        for ci, (i0, w) in enumerate(CH):
+            pa, pb, pc = BANK[ci]
+            X = lambda n, pn=128, i0=i0, w=w: R(n, i0, w, 1, pn)
+            rep = C["REP"][min(ci, 1)]; b0 = rep * (i0 - (h1 if ci else 0))
+            B = R(pa, b0, w, rep); BR = R(pa, b0, w * rep)
+            S1, XP, ZP, RB = [R(pb, w * j, w) for j in range(4)]
+            VO, WO, ZQ, BQ = [R(pc, w * j, w) for j in range(4)]
+            VO = VO[:4] + (8,)
             first = len(ops)
-            mm([(B, sel, X("VB"), True, False)])
-            mm([(B, selb, X("FL"), False, True)])
             early = [tt(X("OWN"), R("NE", s * E + i0, w), B, A.is_equal), tt(X("SKIP"), R("AE", s * E + i0, w), B, A.is_equal)]
-            ZZ = R(pa, 256, w); NS = R(pc, 0, w)
-            early.append(mm([(ZZ, ZB, X("OWN"), True, False), (ZZ, ZB, X("SKIP"), False, False)]))
-            subs = [(i0, SUB), (i0 + SUB, w - SUB)] if ci == 0 and SUB else [(i0, w)]
-            for (j0, v) in subs:
-                sv = R(pb, j0 - i0, v); mark = len(ops)
-                mm([(sv, IH[1.0], R("SK", s * E + j0, v), True, False)])
-                for k0, k1 in zip(KCUT, KCUT[1:]):
-                    for k in range(k0, k1):
-                        tt(R("D", 16 * j0 + k * v, v), R("G", 16 * j0 + k, v, 16), R(pa, j0 - i0, v), A.subtract)
-                    d4 = R("D", 16 * j0 + k0 * v, (k1 - k0) * v)
-                    ts(d4, d4, HI, A.min, LO, A.max)
-                    it = [(sv, R("WB", 15 - k, 128), R("D", 16 * j0 + k * v, v), False, k == 15) for k in range(k0, k1)]
-                    if k0 == KCUT[1]:
-                        it = [(sv, IH[4096.0], R("OWN", j0, v), False, False)] + it
-                    for j in range(0, len(it), MMN):
-                        mm(it[j:j + MMN])
-            if not last:
-                mm([(NV, sel, X("VB"), True, False), (NV, selb, X("FL"), False, False)])
-            qs = PLACE[ci]
+            aff("S", X("TB"), B, 32.0 / 3, 64.0 * HALF)
+            mm([(S1, IH[1.0], R("SK", s * E + i0, w), True, False)])
+            KC = C["KCUT"][ci]
+            for k0, k1 in zip(KC, KC[1:]):
+                for k in range(k0, k1, rep):
+                    tt(R("D", 16 * i0 + k * w, w * rep), R("G", 16 * i0 + k // rep, w * rep, 16 // rep), BR, A.subtract)
+                d4 = R("D", 16 * i0 + k0 * w, (k1 - k0) * w)
+                ts(d4, d4, HI, A.min, LO, A.max)
+                it = [(S1, R("WB", 15 - k // rep - 16 // rep * (k % rep), 128), R("D", 16 * i0 + (k - k % rep) * w + k % rep, w, rep), False, k == 15) for k in range(k0, k1)]
+                if k0 == KC[1]:
+                    it = [(S1, IH[4096.0], X("OWN"), False, False)] + it
+                for j in range(0, len(it), C["MMN"]):
+                    mm(it[j:j + C["MMN"]])
+            qs = C["PLACE"][ci]
             aff(qs[0], X("SI"), S1, 1.0, 16 * 4780.0 + CEN)
             ts(X("U"), X("SI"), 0x1555, A.bitwise_and)
             if qs[1] == "S":
@@ -372,9 +409,11 @@ def build(g, core, T, topo, r):
                 ts(X("W"), X("U"), 4095.0, A.subtract, 0.0, A.max)
             if qs[2] == "S":
                 act(X("TES"), X("W"), F.Sign)
-            else:
+            elif qs[2] == "V":
                 ts(X("TES"), X("W"), 1.0, A.min)
-            VO = R(pc, 0, w, 1, 8); vw = lambda j: R("VW", 8 * j, 8)
+            elif qs[2] == "s":
+                act(X("TES"), X("U"), F.Relu, bias=-4095.0 / 2048, scale=1.0 / 2048)
+            vw = lambda j: R("VW", 8 * j, 8)
             for j in range(1, 6):
                 aff(qs[2 + j], X("R%d" % j), X("W"), 1.0, RC[j] - 0.5)
             mm([(VO, vw(0), X("W"), True, False)])
@@ -384,60 +423,69 @@ def build(g, core, T, topo, r):
             mm([(XP, IH[1025.0], X("W"), True, False), (XP, IH[-1033.0], X("TES"), False, False)])
             act(X("SG", 8), VO, F.Sign, bias=pf(8, 8))
             mm([(XP, WX, X("SG", 6), False, True)])
-            it = [(WO, WR, X("SG", 7), True, True)]
-            if not last:
-                it = [(NV, WE, X("SG", 7), False, True)] + it
-            mm(it)
             aff(qs[8], X("SI"), XP, 1.0, 0x111111 / 2.0 + 8)
+            if not last:
+                if C["NVP"][ci] == "P":
+                    NB = R("P%d" % (6 + ci), 0, w)
+                    mm([(NB, sel, X("VB"), True, False), (NB, selb, X("FL"), False, False)])
+                    mm([(NB, WE, X("SG", 7), False, True)])
+                    aff(qs[10], X("NV"), NB, 1024.0, 0.0)
+                else:
+                    NB = R(pc, 0, w)
+                    aff("S", X("NV"), B, 1024.0, 0.0)
+                    mm([(NB, WK, X("SG", 7), True, True)])
+                    tt(X("NV"), X("NV"), NB, A.add)
+            mm([(WO, WR, X("SG", 7), True, True)])
+            for (zz, zb, th) in ((ZQ, ZC, TN), (ZP, ZB, TH)):
+                mm([(zz, zb, X("OWN"), True, False), (zz, zb, X("SKIP"), False, False), (zz, th, X("SG", 7), False, False)])
             ts(X("U"), X("SI"), 0x111119, A.bitwise_and)
             aff(qs[9], X("SI"), X("U"), 0x111111 / 2.0 ** 20, 1.5 * 2 ** 23 + 8)
             ts(X("U"), X("SI"), 15, A.bitwise_and)
-            act(X("EX"), X("U"), F.Exp, bias=pf(1), scale=17 * LN2)
-            mm([(ZZ, ZM, X("EX"), False, True)])
-            ts(X("SE"), ZZ, 1.5 * 2.0 ** -62, A.is_gt)
-            if not last:
-                if qs[10] == "S":
-                    act(NS, X("SE"), F.Identity, bias=1.0, scale=-1.0)
-                else:
-                    ts(NS, ZZ, 1.5 * 2.0 ** -62, A.is_le)
-                tt(NV, X("SE"), NV, A.mult)
-                tt(X("M1"), R("TAB", t * REG + r * E + i0, w), NS, A.mult)
-                tt(R("TAB", (t + 3) * REG + r * E + i0, w), X("M1"), NV, A.add)
-                send(t + 3, i0, i0 + w)
-            for o in ops[first:]:
-                o["up"] = UP[ci]
-            for o in early:
-                ops[o]["up"] += UPO
-            M = 1.5 * 2 ** 23; B64 = R(pc, 256, w); raw = R("RAW", 3 * i0 + s, w, 3)
-            act(X("TB"), B, F.Identity, bias=64.0 * HALF + M, scale=32.0 / 3)
-            act(B64, X("TB"), F.Identity, bias=-M)
-            late.append((X("DR"), B64, raw, WO, X("SE")))
-            if ci == 0 and not last:
-                first = len(ops); plain(*late.pop()); behind(first)
-                for o in ops[first:]:
-                    o["up"] = -20000
+            act(X("EX"), X("U"), F.Exp, bias=-18 * LN2, scale=6 * LN2)
+            raw = R("RAW", 3 * i0 + s, w, 3)
             if last:
-                plain(*late.pop())
+                tt(X("DR"), X("TB"), WO, A.add)
+            mm([(ZP, ZM, X("EX"), False, True)])
+            mm([(ZQ, ZN, X("EX"), False, True)])
+
+            def plain(X=X, WO=WO, ZP=ZP, ZQ=ZQ, RB=RB, raw=raw, last=last):
+                if not last:
+                    tt(X("DR"), X("TB"), WO, A.add)
+                tt(X("DR"), X("DR"), ZP, A.min); tt(RB, raw, ZQ, A.min); tt(raw, X("DR"), RB, A.max)
+            if not last:
+                tt(X("M1"), X("NV"), ZP, A.min)
+                tt(BQ, R("TAB", t * REG + r * E + i0, w), ZQ, A.min)
+                tt(R("TAB", (t + 3) * REG + r * E + i0, w), X("M1"), BQ, A.max)
+                send(t + 3, i0, i0 + w)
+                late.append(plain)
+            else:
+                plain()
                 o = add("Y", lambda i0=i0, w=w: g.sync.dma_start(T.yk[:, 3 * i0:3 * (i0 + w)], T.RAW[:, 3 * i0:3 * (i0 + w)]),
-                        [R("RAW", 3 * i0, 3 * w)], [], 2500)
+                        [R("RAW", 3 * i0, 3 * w)], [], 600)
                 ops[o]["dma"] = "st%d" % ci
+                add("N%d" % len(ops), None, [], [], 2000, [o])
+            rank_up(first, C["UP"][ci])
+            for o in early:
+                ops[o]["up"] += C["UPO"]
         if not last:
             first = len(ops)
-            while late:
-                plain(*late.pop(0))
-            for o in ops[first:]:
-                o["up"] = -20000
-            behind(first)
+            wrap(t + 1, "P0")
+            behind(first, C.get("BKW", 2)); rank_up(first, -8000)
+            first = len(ops)
+            for f in late:
+                f()
+            behind(first); rank_up(first, -20000)
             first = len(ops)
             if t in (1, 2):
-                split(R("ZI", E * (t - 1), E), t - 1, "P1")
+                names(R("ZI", E * (t - 1), E), E * (t - 1), E)
+                split(R("ZI", E * (t - 1), E), t - 1, R("P0", 128, E))
             if t <= 2:
-                prep(t + 2)
-            behind(first, 2)
-            for o in ops[first:]:
-                o["up"] = -10000
+                prep(t + 2, R("P1", 128, E))
+            behind(first, C.get("BKP", 2)); rank_up(first, -10000)
             if t < 2:
+                first = len(ops)
                 aff("S", R("ZI", E * t, E), R("RAW", t, E, 3), 1.0, 0.0)
+                rank_up(first, -30000)
     return ops, sent[0]
 
 
@@ -461,49 +509,49 @@ def order(ops):
     for i in range(n):
         for j in deps[i]:
             succ[j].append(i)
+    banks = [sorted({x[0] for x in o["rd"] + o["wr"] if SCRATCH[x[0]][0] == "psum"}) for o in ops]
+
+    def lay(key, before, after):
+        left = [len(d) for d in before]; ready = [i for i in range(n) if not left[i]]
+        st = [0.0] * n; held = {}
+        while ready:
+            i = min(ready, key=lambda i: (key[i], i)); ready.remove(i)
+            q = ops[i]["q"]; c = ops[i]["cost"]
+            s = max([st[j] + ops[j]["cost"] + (0 if q == ops[j]["q"] == "P" else HOP) for j in before[i]] or [0.0])
+            busy = [(a, b) for (a, b, _) in held.get(q, []) if b > s]
+            for x in banks[i]:
+                busy += [(a - HOP, b + HOP) for (a, b, q2) in held.get(x, []) if q2 != q and b + HOP > s]
+            for (a, b) in sorted(busy):
+                if a >= s + c:
+                    break
+                s = max(s, b)
+            st[i] = s
+            for x in [q] + banks[i]:
+                held.setdefault(x, []).append((s, s + c, q))
+            for j in after[i]:
+                left[j] -= 1
+                if not left[j]:
+                    ready.append(j)
+        return st, max(s + o["cost"] for s, o in zip(st, ops))
+
     pr = [0.0] * n
     for i in range(n - 1, -1, -1):
         pr[i] = ops[i]["cost"] + max([pr[j] + HOP for j in succ[i]] or [0])
-    pr = [p + o.get("up", 0) for p, o in zip(pr, ops)]
-    tie = {}
-    for i, o in enumerate(ops):
-        k = (o["q"],) + tuple(o["wr"][-1][0:1] + (o["wr"][-1][1] % REG % 768,) if o["wr"] else ())
-        if k not in tie:
-            tie[k] = ((len(tie) + 1) * 7919 + SEED * 104729) * 2654435761 % 1000003 / 1000003.0
-        pr[i] += JIT * tie[k]
-        if o.get("up", 0) < 0:
-            pr[i] = o["up"] - i
-    left = [len(d) for d in deps]; ready = [i for i in range(n) if not left[i]]
-    free = {}; end = [0.0] * n; bank = {}; seq = []
-    while ready:
-        st = {}
-        for i in ready:
-            q = ops[i]["q"]; s = free.get(q, 0.0)
-            for j in deps[i]:
-                s = max(s, end[j] + (0 if q == ops[j]["q"] == "P" else HOP))
-            for x in ops[i]["rd"] + ops[i]["wr"]:
-                if SCRATCH[x[0]][0] == "psum":
-                    for q2, j in bank.get(x[0], {}).items():
-                        if q2 != q:
-                            s = max(s, end[j] + HOP)
-            st[i] = s
-        b = min(ready, key=lambda i: (st[i], -pr[i])); q = ops[b]["q"]
-        top = max([i for i in ready if ops[i]["q"] == q and st[i] <= st[b] + (LOOK if ops[b].get("up", 0) >= 0 else BGL) * ops[b]["cost"]], key=lambda i: pr[i])
-        if pr[top] > pr[b] + GAP or st[top] <= st[b] + 40:
-            b = top
-        for x in ops[b]["rd"] + ops[b]["wr"]:
-            if SCRATCH[x[0]][0] == "psum":
-                d = bank.setdefault(x[0], {})
-                for q2, j in d.items():
-                    if q2 != q:
-                        deps[b].add(j)
-                d[q] = b
-        end[b] = st[b] + ops[b]["cost"]; free[q] = end[b]; ops[b]["t"] = st[b]
-        seq.append(b); ready.remove(b)
-        for j in succ[b]:
-            left[j] -= 1
-            if not left[j]:
-                ready.append(j)
+    st, best = lay([-p - CFG["UPW"] * o.get("up", 0) for p, o in zip(pr, ops)], deps, succ); keep = st
+    rng = numpy.random.default_rng(CFG["SEED"])
+    for p in range(CFG["PASSES"]):
+        jit = rng.normal(0.0, CFG["JIT"] if p else 0.0, n) * (rng.random(n) < CFG["JP"])
+        back, _t = lay([-s - o["cost"] + float(e) for s, o, e in zip(keep, ops, jit)], succ, deps)
+        st, span = lay([-s - o["cost"] for s, o in zip(back, ops)], deps, succ)
+        if span <= best:
+            best, keep = span, st
+    seq = sorted(range(n), key=lambda i: (keep[i], i)); bank = {}
+    for i in seq:
+        ops[i]["t"] = keep[i]
+        for x in banks[i]:
+            d = bank.setdefault(x, {})
+            deps[i].update(j for q2, j in d.items() if q2 != ops[i]["q"])
+            d[ops[i]["q"]] = i
     return seq, deps
 
 
@@ -514,7 +562,7 @@ def rank_program(g, core, T, topo):
     ops, sent = build(g, core, T, topo, r)
     seq, deps = order(ops)
     Q = {"V": g.vector, "S": g.scalar, "P": g.tensor, "G": g, "Y": g.sync}
-    used = set()
+    used = set(); place = {i: k for k, i in enumerate(seq)}
     for i in seq:
         for j in deps[i]:
             if not (ops[i]["q"] == ops[j]["q"] == "P"):
@@ -532,7 +580,7 @@ def rank_program(g, core, T, topo):
                     want[s] = (v, j)
         if o["ext"]:
             want[o["ext"][0]] = (o["ext"][1], None)
-        for s, (v, j) in sorted(want.items(), key=lambda z: -(seq.index(z[1][1]) if z[1][1] is not None else 10 ** 9)):
+        for s, (v, j) in sorted(want.items(), key=lambda z: -(place[z[1][1]] if z[1][1] is not None else 10 ** 9)):
             if kn.get(s, 0) < v:
                 Q[q].wait_ge(T.sem[s], v); kn[s] = v
                 for s2, v2 in clock.get(j, {}).items():

@@ -1,88 +1,74 @@
 import math
-import numpy
 from concourse.bass import DstId, RemoteDMATransfer
 from concourse.mybir import AluOpType as A, ActivationFunctionType as F
 
 P, E, RO, NR = 768, 256, 5, 6
 REG = NR * E
-HALF = NR * P // 2
+HALF = 2280
 CEN = 684.0
 U10 = 1.0 / 1024
 HI, LO = 3412.0 * U10, -4780.0 * U10
 SHIFT = 32768.0
 LN2 = math.log(2.0)
 RC = [0, 4096.0, 2048.0, 8192.0, 32768.0, 131072.0, 0.0]
-NH = 20
-HOP, PEC = 120, 0.7
+NH, LW = 16, 160
 FAR0, FAR1, NEAR0, NEAR1 = ("far", 0), ("far", 1), ("near", 0), ("near", 1)
 CFG = {
-    "CH": [(0, 128), (128, 128)],
-    "CHL": [(0, 128), (128, 128)],
-    "WAY": [[FAR0 + ("in",), FAR1 + ("out",)], [None]],
-    "START": [(0, 0, 256, [FAR0 + ("in",), FAR1 + ("out",)]), (1, 0, 256, [NEAR0 + ("out",), FAR0 + ("in",)]),
-              (2, 0, 256, [NEAR1 + ("in",), None])],
-    "VG": 56, "SG0": 8, "SG": 40,
-    "KCUT": [[0, 4, 8, 12, 16]] * 3, "MMN": 8,
-    "UP": [1500, 0, -500], "UPO": 0, "UPW": 1.0, "PASSES": 3, "SEED": 0, "JIT": 500.0, "JP": 0.1,
-    "PLACE": ["SSSSSSSSSSS", "VVSVSVSVVVS", "VVSVSVSVVVS"],
-    "FL": "VV", "REP": [1, 1],
+    "LOAD": [0, 384, 768],
+    "ENC": [(0, 0, 128), (1, 0, 128), (2, 0, 128), (0, 128, 128), (1, 128, 128), (2, 128, 128)],
+    "START": [[(0, 0, 128, ("fwd", "nf"))], [(1, 0, 128, FAR0 + ("in",)), (2, 0, 128, ("fwd", "nf"))],
+              [(0, 128, 128, FAR1 + ("in",)), (1, 128, 128, None)], [(2, 128, 128, NEAR0 + ("in",))]],
+    "TURN": [1, 2, 3, 4, 5],
+    "PARTS": [(0, 128), (128, 128)],
+    "SEND": [[(0, 64, FAR0 + ("in",)), (64, 64, FAR1 + ("out",))], [(128, 128, None)]], "FOLD": [0, 0],
+    "VB": [(0, 128), (128, 128)],
+    "GATH": [("V", 48), ("S", 80), ("S", 64), ("S", 64)],
+    "REP": [2, 4],
+    "SUB": [[2] * 8, [4, 4, 4, 2, 2]],
+    "KCUT": [[0, 6, 12, 14, 16], [0, 8, 12, 14, 16]], "MMN": 2,
+    "VO": [[(1, 2), (3, 4), (5,)], [(1, 3), (2, 5), (4,)]],
+    "NV": "VV", "OWNBANK": [{"ZP": "P6", "ZQ": "P7"}, {}],
+    "PLACE": ['SSSSSSSSV', 'SVSSVSVVV'],
+    "ORDER": """sel vb0 g1 vb1 fl0 g0 fl1 g3 sk0 sk1 b01 b13 B01 b00 B00 B13 b12 B12 b11 B11 b10 B10
+        d02 d00 d04 d08 d06 c00 d0a own0 c06 d0c d0e c0c c0e m00 m02 m04 m06 so0 m08 m0a m0c m0e sx1 g2 own1
+        d14 sx0 si0 na0 u0 d10 w0 te0 qa0 x1 pa0 x0 c10 d18 d1c c18 d1e r20 r10 r40 r30 r50 xa0 va0 ve0 m10 vf0 vg0 m12 m14 m16
+        ni sg0 xb0 sj0 tb0 so1 m18 m1a c1c c1e m1c m1e uj0 tb1 si1 sm0 uk0 u1 ex0 te1 w1 nb0 pt0 qt0 wo0 qb0 pb0
+        va1 r11 r21 r41 nv0 r31 r51 bq0 mi0 ve1 vf1 vg1 mx0 na1 sg1 xa1 xb1 sj1 uj1 sm1 uk1 nb1 wo1 qa1 qt1 pa1 pt1 ex1
+        q1 f1 f2 mf ne nv1 pb1 qb1 mi1 bq1 mx1 send0 send1
+        wr0 wr1 wr2 wr3 f3 rb0 dr0 rb1 dr1 ds0 f4 f5 i2 rw0 sl ds1 off i1 skm co rw1 zi""",
 }
-CFG.update({"VG": 48, "SG0": 40, "SG": 48, "KCUT": [[0, 6, 12, 14, 16], [0, 4, 8, 12, 16], [0, 4, 8, 12, 16]], "MMN": 4,
-            "PLACE": ["SSSSSSSSSSS", "VVSVSVSVSVS", "VVSVSVSVVVS"], "REP": [2, 4], "BKW": 1, "BK0": 3, "BKP": 2, "PASSES": 150,
-            "NVP": "PPV"})
 
 SCRATCH = {
     "TAB": ("sbuf", [128, 7 * REG], "float32"), "Z": ("sbuf", [128, P], "int32"), "RAW": ("sbuf", [128, P], "float32"),
     "G": ("sbuf", [128, 16 * E], "float32"), "D": ("sbuf", [128, 16 * E], "float16"),
-    "NE": ("sbuf", [128, P], "float32"), "SK": ("sbuf", [128, P], "float16"), "AE": ("sbuf", [128, P], "float32"),
+    "NE": ("sbuf", [128, P], "float32"), "SK": ("sbuf", [128, P], "float16"),
     "NI": ("sbuf", [128, P], "int32"), "OFF": ("sbuf", [128, RO * E], "uint16"), "COFF": ("sbuf", [128, RO * 16], "uint16"),
-    "SEL": ("sbuf", [128, RO * 128], "float32"), "SELB": ("sbuf", [128, RO * 128], "bfloat16"),
-    "SLOT": ("sbuf", [128, 768], "float32"), "ZI": ("sbuf", [128, 2 * E], "int32"), "AN": ("sbuf", [128, E], "float32"),
+    "SEL": ("sbuf", [128, (RO + 1) * 128], "float32"), "SELB": ("sbuf", [128, (RO + 1) * 128], "bfloat16"),
+    "SP": ("sbuf", [128, E], "float16"),
+    "IOT": ("sbuf", [128, E + 16], "float16"), "KS": ("sbuf", [128, 256], "bfloat16"),
+    "SLOT": ("sbuf", [128, 3 * 384], "float32"), "ZI": ("sbuf", [128, 2 * E], "int32"), "AN": ("sbuf", [128, E], "float32"),
     "I1": ("sbuf", [128, P], "int32"), "I2": ("sbuf", [128, P], "int32"), "EQ": ("sbuf", [128, P], "bfloat16"),
-    "MF": ("sbuf", [128, P], "bfloat16"), "NP": ("sbuf", [128, P], "float32"),
+    "MF": ("sbuf", [128, P], "float16"), "NP": ("sbuf", [128, P], "float32"),
     "Q1": ("sbuf", [128, E], "int32"), "F2": ("sbuf", [128, E], "float32"), "F3": ("sbuf", [128, E], "float32"),
-    "VB": ("sbuf", [128, E], "float32"), "FL": ("sbuf", [128, E], "bfloat16"),
-    "OWN": ("sbuf", [128, E], "float16"), "SKIP": ("sbuf", [128, E], "float16"),
+    "VB": ("sbuf", [128, E], "float32"), "FL": ("sbuf", [128, E], "bfloat16"), "OWN": ("sbuf", [128, E], "float16"),
     "SI": ("sbuf", [128, E], "int32"), "U": ("sbuf", [128, E], "int32"), "W": ("sbuf", [128, E], "float16"),
+    "SJ": ("sbuf", [128, E], "int32"), "UJ": ("sbuf", [128, E], "int32"),
     "TES": ("sbuf", [128, E], "float16"), "R1": ("sbuf", [128, E], "float16"), "R2": ("sbuf", [128, E], "bfloat16"),
     "R3": ("sbuf", [128, E], "bfloat16"), "R4": ("sbuf", [128, E], "bfloat16"), "R5": ("sbuf", [128, E], "bfloat16"),
     "SG": ("sbuf", [128, E], "bfloat16"), "EX": ("sbuf", [128, E], "bfloat16"),
-    "NV": ("sbuf", [128, E], "float32"), "M1": ("sbuf", [128, E], "float32"), "TB": ("sbuf", [128, E], "int32"),
-    "DR": ("sbuf", [128, E], "float32"),
-    "ONE": ("sbuf", [128, 128], "float32"), "ID": ("sbuf", [128, 128], "float32"), "COL": ("sbuf", [128, 144], "float32"),
-    "WB": ("sbuf", [128, 144], "float16"), "IH": ("sbuf", [128, 4 * 128], "float16"), "IB": ("sbuf", [128, 256], "bfloat16"),
+    "NV": ("sbuf", [128, E], "float32"), "M1": ("sbuf", [128, RO * E], "float32"), "M2": ("sbuf", [128, RO * E], "float32"),
+    "TB": ("sbuf", [128, E], "int32"), "DR": ("sbuf", [128, E], "float32"),
+    "ONE": ("sbuf", [128, 128], "float32"), "ID": ("sbuf", [128, 256], "float32"), "COL": ("sbuf", [128, 144], "float32"),
+    "WB": ("sbuf", [128, 144], "float16"), "IH": ("sbuf", [128, 4 * 128], "float16"), "IB": ("sbuf", [128, 128], "bfloat16"),
     "ZM": ("sbuf", [128, 6 * 128], "bfloat16"), "BLK": ("sbuf", [128, 4 * 128], "float32"), "BI": ("sbuf", [128, 128], "int32"),
-    "VW": ("sbuf", [128, 56], "bfloat16"), "WS": ("sbuf", [128, 512], "bfloat16"),
-    "PI": ("sbuf", [128, 8], "int32"), "PF": ("sbuf", [128, 16], "float32"),
-    "LAND": ("sbuf", [128, NH * 128], "float32"),
+    "VW": ("sbuf", [128, 96], "bfloat16"), "WS": ("sbuf", [128, 512], "bfloat16"),
+    "PI": ("sbuf", [128, 8], "int32"), "PF": ("sbuf", [128, 24], "float32"),
+    "LAND": ("sbuf", [128, NH * LW], "float32"),
 }
 for _b in range(8):
     SCRATCH["P%d" % _b] = ("psum", [128, 512], "float32")
-SEMAPHORES = ["sV", "sS", "sP", "sG", "ld", "st0", "st1", "st2", "sent"] + ["arr%d" % t for t in range(RO)] + ["h%d" % k for k in range(NH)]
-
-
-def pieces():
-    out = []
-    for (s, c0, w, ways) in CFG["START"]:
-        out += [(0, s, c0 + j * (w // len(ways)), w // len(ways), y) for j, y in enumerate(ways)]
-    for t in range(RO - 1):
-        for (c0, w), ways in zip(CFG["CH"], CFG["WAY"]):
-            out += [(t + 1, t + 3, c0 + j * (w // len(ways)), w // len(ways), y) for j, y in enumerate(ways)]
-    return out
-
-
-def helpers(rc, way, T, topo):
-    dsts = [c for c in T.cores if c != rc]
-    side = [h for h in topo.cores_of(rc) if T.rank_of(h) is None and (topo.die(h) != topo.die(rc)) == (way[0] == "far")]
-    full = [h for h in side if all(topo.may_write(h, d) for d in dsts)]
-    part = [h for h in side if h not in full]
-    a, b = full[way[1] % len(full)], part[way[1] % len(part)]
-    return {b: [d for d in dsts if topo.may_write(b, d)], a: [d for d in dsts if not topo.may_write(b, d)]}
-
-
-def inmask(rc, h, way, T, topo):
-    full = topo.mask(rc, h); out = topo.mask(rc, [c for c in T.cores if c != rc][0])
-    return {"all": full, "out": out, "in": full & ~out}[way[2]]
+SEMAPHORES = (["sV", "sS", "sP", "sG", "ld0", "ld1", "ld2", "st0", "st1", "sent"] + ["arr%d" % t for t in range(RO)]
+              + ["h%d_%d" % (k, j) for k in range(2 * NH) for j in range(3)])
 
 
 def ones(m):
@@ -94,30 +80,73 @@ def dst(c, topo):
     return DstId(rid=rid, pnc=pid)
 
 
+def calls():
+    out = [[(0, s, c0, w, way) for (s, c0, w, way) in call] for call in CFG["START"]]
+    for t in range(RO - 1):
+        out += [[(t + 1, t + 3, c0, w, way) for (c0, w, way) in call] for call in CFG["SEND"]]
+    return out
+
+
+def route(rc, way, T, topo):
+    r = T.rank_of(rc); dsts = [T.cores[(r + j) % NR] for j in CFG["TURN"]]
+    out = topo.mask(rc, dsts[0])
+    free = lambda c: [h for h in topo.cores_of(c) if T.rank_of(h) is None]
+    inner = [e for e in topo.engines(rc, free(rc)[0]) if not out >> e & 1]
+    part_of = {"out": out, "in": sum(1 << e for e in inner), "in0": sum(1 << e for e in inner[:len(inner) // 2]),
+               "in1": sum(1 << e for e in inner[len(inner) // 2:])}
+
+    def pick(d, es, letter):
+        side = [h for h in free(d) if all(topo.may_write(h, e) for e in es)]
+        near = [h for h in side if topo.die(h) == topo.die(d)]; far = [h for h in side if h not in near]
+        return {"n": near[0], "f": far[-1], "g": far[0]}[letter]
+    if way is None:
+        return [(out, dsts, {})]
+    if way[0] == "fwd":
+        on = {}
+        for d in [d for d in dsts if topo.same_plane(topo.chip(rc), topo.chip(d))]:
+            mate = [e for e in dsts if topo.mates(topo.chip(d), topo.chip(e))]
+            src = [c for c in T.cores if topo.same_plane(topo.chip(c), topo.chip(d))].index(rc)
+            on[pick(d, mate, way[1][src])] = [d] + mate
+        mate = [d for d in dsts if topo.mates(topo.chip(rc), topo.chip(d))]
+        if len(way) == 2:
+            return [(out, mate, on)]
+        return [(out, [], on), (part_of[way[3]], [], {pick(rc, mate, way[2]): mate})]
+    side = [h for h in free(rc) if (topo.die(h) != topo.die(rc)) == (way[0] == "far")]
+    full = [h for h in side if all(topo.may_write(h, d) for d in dsts)]
+    part = [h for h in side if h not in full]
+    a, b = full[way[1] % len(full)], part[way[1] % len(part)]
+    return [(part_of[way[2]], [], {b: [d for d in dsts if topo.may_write(b, d)], a: [d for d in dsts if not topo.may_write(b, d)]})]
+
+
+def signal(p, rc, T, topo):
+    if p[4] is None:
+        return "arr%d" % p[0]
+    k = [x for call in calls() for x in call if x[4] is not None].index(p)
+    plane = [c for c in T.cores if c == rc or topo.same_plane(topo.chip(c), topo.chip(rc))]
+    return "h%d_%d" % (k, plane.index(rc))
+
+
+def landings(core, T, topo):
+    return [(p, rc, m, on[core]) for call in calls() for p in call for rc in T.cores for (m, _, on) in route(rc, p[4], T, topo) if core in on]
+
+
 def helper_program(g, core, T, topo):
-    home = [c for c in topo.cores_of(core) if T.rank_of(c) is not None]
-    if not home:
-        return
-    rc = home[0]; r = T.rank_of(rc); sent = 0; k = 0
-    for (arr, reg, c0, w, way) in pieces():
-        if way is None:
-            continue
-        hs = helpers(rc, way, T, topo)
-        if core in hs:
-            ds = hs[core]; m = topo.mask(core, ds[0]); col = reg * REG + r * E + c0
-            g.wait_ge(T.sem["h%d" % k], ones(inmask(rc, core, way, T, topo)))
-            g.remote_dma_fused([RemoteDMATransfer(dst_ids=[dst(d, topo) for d in ds], dma_engine_mask=m, remote_sem=T.sem["arr%d" % arr],
-                                                  src=T.LAND[:, k * 128:k * 128 + w], dsts=[T.TAB[:, col:col + w] for d in ds])], local_sem=T.sem.sent)
-            sent += ones(m)
-        k += 1
+    sent = 0
+    for k, ((arr, reg, c0, w, way), rc, m0, ds) in enumerate(landings(core, T, topo)):
+        col = reg * REG + T.rank_of(rc) * E + c0
+        off = [d for d in ds if topo.chip(d) != topo.chip(core)]; here = [d for d in ds if d not in off]
+        m = topo.mask(core, off[0]); tr = [(off, m)] + [([d], topo.mask(core, d) & ~m) for d in here]
+        g.wait_ge(T.sem[signal((arr, reg, c0, w, way), rc, T, topo)], ones(m0))
+        g.remote_dma_fused([RemoteDMATransfer(dst_ids=[dst(d, topo) for d in dd], dma_engine_mask=mm, remote_sem=T.sem["arr%d" % arr],
+                                              src=T.LAND[:, k * LW:k * LW + w], dsts=[T.TAB[:, col:col + w] for d in dd]) for (dd, mm) in tr],
+                           local_sem=T.sem.sent)
+        sent += sum(ones(mm) for (dd, mm) in tr)
     if sent:
         g.wait_ge(T.sem.sent, sent)
 
 
 def build(g, core, T, topo, r):
-    ops = []
-    CY = 1.04
-    C = CFG
+    ops = []; C = CFG; now = [-1, ""]
 
     def ap(x):
         n, a, b, s, pn = x
@@ -126,21 +155,15 @@ def build(g, core, T, topo, r):
     def R(n, a, w, s=1, pn=128):
         return (n, a, a + (w - 1) * s + 1, s, pn)
 
-    def RG(a, w):
-        return R("G", 16 * a, 16 * w)
-
     def wd(x):
         return (x[2] - x[1] - 1) // x[3] + 1
 
-    def two(x):
-        return SCRATCH[x[0]][2] in ("float16", "bfloat16", "uint16")
-
-    def ps(x):
-        return SCRATCH[x[0]][0] == "psum"
-
-    def add(q, fn, rd, wr, cost, after=(), ext=None):
-        ops.append({"q": q, "fn": fn, "rd": list(rd), "wr": list(wr), "cost": cost, "after": list(after), "ext": ext})
+    def add(q, fn, rd, wr, after=(), ext=None):
+        ops.append({"q": q, "fn": fn, "rd": list(rd), "wr": list(wr), "after": list(after), "ext": ext, "t": now[0], "name": now[1]})
         return len(ops) - 1
+
+    def name(n):
+        now[1] = n
 
     def col(s):
         return [s] if isinstance(s, tuple) else []
@@ -149,24 +172,21 @@ def build(g, core, T, topo, r):
         return ap(s) if isinstance(s, tuple) else s
 
     def ts(o, i, s1, op0, s2=None, op1=None):
-        c = 60 + CY * max(64, wd(o) * (0.5 if two(o) and two(i) else 1))
         if op1 is None:
-            return add("V", lambda: g.vector.tensor_scalar(ap(o), ap(i), sc(s1), None, op0), [i] + col(s1), [o], c)
-        return add("V", lambda: g.vector.tensor_scalar(ap(o), ap(i), sc(s1), sc(s2), op0, op1), [i] + col(s1) + col(s2), [o], c)
+            return add("V", lambda: g.vector.tensor_scalar(ap(o), ap(i), sc(s1), None, op0), [i] + col(s1), [o])
+        return add("V", lambda: g.vector.tensor_scalar(ap(o), ap(i), sc(s1), sc(s2), op0, op1), [i] + col(s1) + col(s2), [o])
 
     def tt(o, a, b, op):
-        c = 60 + CY * max(64, wd(o) * (1 if ps(a) or ps(b) else 2))
-        return add("V", lambda: g.vector.tensor_tensor(ap(o), ap(a), ap(b), op), [a, b], [o], c)
+        return add("V", lambda: g.vector.tensor_tensor(ap(o), ap(a), ap(b), op), [a, b], [o])
 
     def cp(o, i):
-        return add("V", lambda: g.vector.tensor_copy(ap(o), ap(i)), [i], [o], 60 + CY * max(64, wd(o)))
+        return add("V", lambda: g.vector.tensor_copy(ap(o), ap(i)), [i], [o])
 
     def ms(o, v):
-        return add("V", lambda: g.vector.memset(ap(o), v), [], [o], 60 + CY * max(64, wd(o)))
+        return add("V", lambda: g.vector.memset(ap(o), v), [], [o])
 
     def act(o, i, f, bias=0.0, scale=1.0):
-        return add("S", lambda: g.scalar.activation(ap(o), ap(i), f, bias=sc(bias), scale=sc(scale)), [i] + col(bias) + col(scale), [o],
-                   80 + CY * max(64, wd(o)))
+        return add("S", lambda: g.scalar.activation(ap(o), ap(i), f, bias=sc(bias), scale=sc(scale)), [i] + col(bias) + col(scale), [o])
 
     def aff(q, o, i, scale, bias):
         if q == "S":
@@ -180,99 +200,148 @@ def build(g, core, T, topo, r):
             for (o, l, x, s0, s1) in items:
                 ins = g.tensor.matmul(ap(o), ap(l), ap(x), s0, s1)
             return ins
-        c = 60 + sum(PEC * max(min(64, wd(l)), wd(x)) * (1 if two(x) else 4) for (o, l, x, s0, s1) in items)
         banks = {it[0][0] for it in items}
-        o = add("P", fn, [y for it in items for y in it[1:3]], [it[0] for it in items], c, [lastmm[b] for b in banks if b in lastmm])
+        o = add("P", fn, [y for it in items for y in it[1:3]], [it[0] for it in items], [lastmm[b] for b in banks if b in lastmm])
         lastmm.update({b: o for b in banks})
         return o
 
     def iota(o, pat, base, cm):
-        fl = SCRATCH[o[0]][2] != "int32"
-        if fl:
-            return add("G", lambda: g.iota(ap(o), pat, base, cm, allow_small_or_imprecise_dtypes=True), [], [o], 160 + 2 * CY * wd(o))
-        return add("G", lambda: g.iota(ap(o), pat, base, cm), [], [o], 160 + 2 * CY * wd(o))
+        if SCRATCH[o[0]][2] != "int32":
+            return add("G", lambda: g.iota(ap(o), pat, base, cm, allow_small_or_imprecise_dtypes=True), [], [o])
+        return add("G", lambda: g.iota(ap(o), pat, base, cm), [], [o])
 
     def setrow(o, j, v):
-        return add("G", lambda: g.affine_select(ap(o), ap(o), [[0, wd(o)]], A.not_equal, v, -j, 1), [o], [o], 200 + 2 * CY * wd(o))
+        return add("G", lambda: g.affine_select(ap(o), ap(o), [[0, wd(o)]], A.not_equal, v, -j, 1), [o], [o])
 
-    others = [c for c in T.cores if c != core]
-    sent = [0]; nets = {}; need = {}
-    plist = pieces()
-    for (arr, reg, c0, w, way) in plist:
-        need[arr] = need.get(arr, 0) + sum(ones(topo.mask(c, core)) for c in others)
+    sent = [0]; need = {}; todo = calls()
+    for call in todo:
+        for p in call:
+            for c in T.cores:
+                if c != core:
+                    sem = signal(p, c, T, topo) if core in route(c, p[4], T, topo)[0][1] else "arr%d" % p[0]
+                    x = need.setdefault(p[0], {}); x[sem] = x.get(sem, 0) + ones(topo.mask(c, core))
 
-    def send(reg, c0, c1):
-        tr = []; ps_ = [p for p in plist if p[1] == reg and c0 <= p[2] < c1]
-        for p in ps_:
-            arr, _, a, w, way = p
-            src = R("TAB", reg * REG + r * E + a, w)
-            if way is None:
-                ds = others; sem = T.sem["arr%d" % arr]; to = src; m = topo.mask(core, ds[0])
-            else:
-                k = [x for x in plist if x[4] is not None].index(p)
-                ds = list(helpers(core, way, T, topo)); sem = T.sem["h%d" % k]; to = R("LAND", k * 128, w); m = inmask(core, ds[0], way, T, topo)
-            sent[0] += ones(m); tr.append((ds, m, sem, src, to))
-        o = add("G", lambda: g.remote_dma_fused([RemoteDMATransfer(dst_ids=[dst(d, topo) for d in ds], dma_engine_mask=m, remote_sem=sem,
-                                                                   src=ap(src), dsts=[ap(to) for d in ds]) for (ds, m, sem, src, to) in tr],
-                                                local_sem=T.sem.sent), [x[3] for x in tr], [], 800)
+    def send(fold=None):
+        tr = []
+        for p in todo.pop(0):
+            arr, reg, a, w, way = p
+            to = R("TAB", reg * REG + r * E + a, w)
+            src = [to] if fold is None else [R("M1", fold + a, w), R("M2", fold + a, w)]
+            for (m, ds, on) in route(core, way, T, topo):
+                at = [R("LAND", LW * [x[:2] for x in landings(h, T, topo)].index((p, core)), w) for h in on]
+                tr.append((m, src, signal(p, core, T, topo), list(on) + ds, at + [to for d in ds])); sent[0] += ones(m)
+        o = add("G", lambda: g.remote_dma_fused(
+            [RemoteDMATransfer(dst_ids=[dst(d, topo) for d in ds], dma_engine_mask=m, remote_sem=T.sem[sem], srcs=[ap(y) for y in src],
+                               dsts=[ap(y) for y in at], alu_op=0 if fold is None else 2) for (m, src, sem, ds, at) in tr],
+            local_sem=T.sem.sent), [y for x in tr for y in x[1]], [])
         ops[o]["noinc"] = True
-        for (arr, _, a, w, way) in ps_:
-            row = 10 + w * 4 / 30.0
-            n = add("N", None, [], [], 300 + 80 * row, [o]) if way is None else o
-            nets.setdefault(arr, []).append(add("N%d" % len(ops), None, [], [], 1200 if way is None else 3600 + 80 * row, [n]))
 
     def gather(q, o, t, off):
-        win = R("TAB", t * REG, 3 * REG); n = wd(o); ext = ("arr%d" % t, need[t])
+        win = R("TAB", t * REG, 3 * REG); ext = need[t]
         src = lambda: ap(win).indirect(ap(off))
         if q == "S":
-            return add("S", lambda: g.scalar.activation(ap(o), src(), F.Identity, scale=U10), [win, off], [o], 80 + 1.56 * CY * n, nets[t], ext)
+            return add("S", lambda: g.scalar.activation(ap(o), src(), F.Identity, scale=U10), [win, off], [o], [], ext)
         if q == "V":
-            return add("V", lambda: g.vector.tensor_scalar(ap(o), src(), U10, None, A.mult), [win, off], [o], 60 + 1.56 * CY * n, nets[t], ext)
+            return add("V", lambda: g.vector.tensor_scalar(ap(o), src(), U10, None, A.mult), [win, off], [o], [], ext)
         M2 = 1.5 * 2 ** 34
-        return add("V", lambda: g.vector.tensor_scalar(ap(o), src(), M2, M2 + 512 * SHIFT, A.add, A.subtract), [win, off], [o],
-                   60 + 1.56 * CY * n, nets[t], ext)
+        return add("V", lambda: g.vector.tensor_scalar(ap(o), src(), M2, M2 + 512 * SHIFT, A.add, A.subtract), [win, off], [o], [], ext)
 
-    def rank_up(first, v):
-        for o in ops[first:]:
-            o["up"] = v
-
-    o = add("Y", lambda: g.sync.dma_start(T.Z[:], T.kin[:]), [], [R("Z", 0, P)], 3000); ops[o]["dma"] = "ld"
-    first = len(ops)
-    ONE = R("ONE", 0, 128); ID = R("ID", 0, 128); AN = R("AN", 0, E)
-    iota(AN, [[3, E]], P * r, 0)
+    for j, (a, b) in enumerate(zip(C["LOAD"], C["LOAD"][1:])):
+        o = add("Y", lambda a=a, b=b: g.sync.dma_start(T.Z[:, a:b], T.kin[:, a:b]), [], [R("Z", a, b - a)])
+        ops[o]["dma"] = "ld%d" % j
+    ONE = R("ONE", 0, 128); ID = R("ID", 0, 128); IN = R("ID", 128, 128); AN = R("AN", 0, E); I25 = R("IB", 0, 128)
+    pi = lambda j: R("PI", j, 1)
+    pf = lambda j, pn=128: R("PF", j, 1, 1, pn)
     ms(ONE, 1.0)
-    add("G", lambda: g.affine_select(ap(ID), ap(ONE), [[-1, 128]], A.is_equal, 0.0, 0, 1), [ONE], [ID], 470)
+    add("G", lambda: g.affine_select(ap(ID), ap(ONE), [[-1, 128]], A.is_equal, 0.0, 0, 1), [ONE], [ID])
+    iota(AN, [[3, E]], P * r, 0)
+    iota(pi(0), [[0, 1]], 0, 1)
+    iota(R("COL", 0, 144), [[1, 144]], -15, 0)
+    iota(R("BI", 0, 128), [[16, 8], [0, 16]], 0, 0)
+    IH = {v: R("IH", 128 * j, 128) for j, v in enumerate([1.0, 4096.0, 1025.0, -516.5])}
+    for v in IH:
+        act(IH[v], ID, F.Identity, scale=v)
     AP_ = [R("P0", 0, E), R("P0", 256, E), R("P1", 0, E)]
     for s in range(3):
         aff("S", AP_[s], AN, 1.0, float(s))
-    I31, I25 = R("IB", 0, 128), R("IB", 128, 128)
-    ts(I31, ID, 31.0, A.mult); ts(I25, ID, 1024 * SHIFT, A.mult)
-    rank_up(first, 9000)
-    IH = {}
-    for j, v in enumerate([1.0, 4096.0, 1025.0, -1033.0]):
-        IH[v] = R("IH", 128 * j, 128); act(IH[v], ID, F.Identity, scale=v)
-    for s in range(3):
-        aff("S", R("AE", s * E, E), AN, 6.0, 6.0 * (s - HALF))
-    pi = lambda j: R("PI", j, 1)
-    pf = lambda j, pn=128: R("PF", j, 1, 1, pn)
-    iota(pi(0), [[0, 1]], 0, 1)
+    vw = lambda j, a=0, w=9: R("VW", 10 * j + a, w)
+    ms(R("VW", 0, 90), 0.0); ms(R("COFF", 0, 16 * RO), 0)
+    for j in range(3):
+        ms(R("SLOT", 384 * j + 64, 64), 0.0)
+    ts(IN, ID, 6080.0, A.mult); ts(I25, ID, 1024 * SHIFT, A.mult)
+    ms(vw(0, 0, 1), 2.0); ms(vw(6, 0, 1), -1.5); ms(vw(6, 1, 5), -0.5)
+    ms(R("SEL", 128 * RO, 128), U10); ms(R("SELB", 128 * RO, 128), -SHIFT / 2)
+    for j in range(1, 4):
+        ms(vw(j, j, 1), 2.0 / 4 ** j); ms(vw(j, j - 1, 1), -2.0 / 4 ** (j - 1))
+
+    def names(zi, c, w):
+        name("ni"); aff("S", R("NI", c, w), zi, 1.0 / 64, -31.5 / 64)
+        name("i1"); ts(R("I1", c, w), zi, 42, A.bitwise_and)
+
+    def split(zi, s, bank):
+        c = s * E
+        name("mf"); aff("S", bank, R("I1", c, E), 31.0, -CEN)
+        name("i2"); ts(R("I2", c, E), zi, 63, A.bitwise_and)
+        name("skm"); tt(R("SK", c, E), R("I2", c, E), bank, A.add)
+        name("ne"); aff("S", R("NE", c, E), R("NI", c, E), 6.0, -6.0 * HALF)
+
+    def prep(t, f1):
+        s = t % 3; c = s * E
+        n = R("NI", c, E); sl = R("SLOT", 384 * s + 128, E); f2, f3 = R("F2", 0, E), R("F3", 0, E)
+        name("q1"); aff("S", R("Q1", 0, E), n, 1.0 / 3, -1.0 / 3)
+        name("f1"); aff("S", f1, n, float(REG), -float(REG * s))
+        name("f2"); aff("S", f2, R("Q1", 0, E), 1.0 - 3 * REG, 0.0)
+        if s == 0:
+            name("sl"); tt(sl, f1, f2, A.add)
+        else:
+            name("f3"); tt(f3, f1, f2, A.add)
+            name("f4"); act(f2, f3, F.Sign, bias=0.5)
+            name("f5"); aff("S", f1, f2, -1.5 * REG, 1.5 * REG)
+            name("sl"); tt(sl, f3, f1, A.add)
+        name("off"); cp(R("OFF", t * E, E), sl)
+
+    def wrap(t, bank):
+        m = 16 * (t + 1)
+        for h4 in range(0, 16, 4):
+            name("wr%d" % (h4 // 4))
+            mm([(R(bank, 496 + h, 1, 1, m), R("SLOT", 384 * (t % 3) + 128 + 16 * h - 16 * t, m), R("ID", 17 * t, 1), True, True)
+                for h in range(h4, h4 + 4)])
+        name("co"); cp(R("COFF", 16 * t, 16, 1, m), R(bank, 496, 16, 1, m))
+
+    def select(t):
+        for n in ("SEL", "SELB"):
+            o, i = R(n, 128 * t, 128), R(n, 128 * RO, 128)
+            add("G", lambda o=o, i=i: g.affine_select(ap(o), ap(i), [[0, 128]], A.is_equal, 0.0, -17 * t - 3, 1), [i], [o])
+
+    have = set(); pend = []; waiting = [[(p[0], p[1] + j) for p in call for j in range(p[2])] for call in C["START"]]
+    for j, (s, c0, w) in enumerate(C["ENC"]):
+        c = s * E + c0; zi = R("Z", 3 * c0 + s, w, 3); b1 = R("P%d" % (2 + j % 6), 0, w)
+        names(zi, c, w)
+        aff("S", R("NP", c, w), R("NI", c, w), 1.0, -2304.0)
+        tt(R("EQ", c, w), R("NI", c, w), R(AP_[s][0], AP_[s][1] + c0, w), A.is_equal)
+        aff("S" if j else "V", R("MF", c, w), R("I1", c, w), 31.0, -CEN)
+        mm([(b1, IN, R("NP", c, w), True, False)])
+        mm([(b1, I25, R("EQ", c, w), False, False), (b1, IH[1.0], R("MF", c, w), False, True)])
+
+        def fin(s=s, c0=c0, w=w, zi=zi, b1=b1):
+            tt(R("TAB", s * REG + r * E + c0, w), zi, b1, A.add)
+            have.update((s, c0 + i) for i in range(w))
+            while waiting and all(x in have for x in waiting[0]):
+                waiting.pop(0); send()
+        pend.append(fin)
+        if len(pend) > 1:
+            pend.pop(0)()
+    for f in pend:
+        f()
+
+    name(""); now[0] = -0.5
+    for j in range(4, 6):
+        ms(vw(j, j, 1), 2.0 / 4 ** j); ms(vw(j, j - 1, 1), -2.0 / 4 ** (j - 1))
     ts(pi(1), pi(0), -16, A.bitwise_and); cp(pf(0), pi(1)); cp(pf(1), pi(0))
-    iota(R("COL", 0, 144), [[1, 144]], -15, 0)
     ts(R("WB", 0, 144), R("COL", 0, 144), pf(0), A.is_equal, 1024.0, A.mult)
-    iota(R("BI", 0, 128), [[16, 8], [0, 16]], 0, 0)
-    BL = [R("BLK", 128 * j, 128) for j in range(4)]
-    ZM, ZN, ZB, ZC, TH, TN = [R("ZM", 128 * j, 128) for j in range(6)]
-    ts(BL[0], R("BI", 0, 128), pf(0), A.is_equal)
-    ts(BL[1], R("COL", 15, 128), pf(1), A.is_gt, -63.0 / 32, A.mult); ts(BL[1], BL[1], -1.0 / 32, A.add)
-    tt(BL[1], BL[1], BL[0], A.mult); ts(BL[2], ID, 33.0 / 32, A.mult); tt(ZM, BL[1], BL[2], A.add)
-    act(ZN, ZM, F.Identity, scale=-1.0)
-    ts(BL[3], BL[0], -0.5, A.mult); tt(BL[3], BL[3], ID, A.add)
-    act(ZB, BL[3], F.Identity, scale=2.0 ** 76); act(ZC, BL[3], F.Identity, scale=-2.0 ** 76)
+    select(0)
+    prep(0, R("P1", 256, E)); wrap(0, "P7"); split(R("Z", 0, E, 3), 0, R("P2", 256, E))
     ts(pi(3), pi(0), 7, A.bitwise_and); ts(pi(4), pi(0), 1, A.bitwise_and)
-    ts(pf(9), pi(3), 6.0, A.is_equal, 2.0 ** 28, A.mult)
-    TH, TN = TH[:4] + (8,), TN[:4] + (8,)
-    act(TN, R("ONE", 0, 128, 1, 8), F.Identity, scale=pf(9, 8)); act(TH, TN, F.Identity, scale=-1.0)
-    TH, TN = TH[:4] + (7,), TN[:4] + (7,)
     ts(pf(2), pi(3), 2 * LN2, A.mult, -11 * LN2, A.add)
     ts(pf(3), pi(4), 10 * LN2, A.mult, 10 * LN2, A.add); tt(pf(4), pf(2), pf(3), A.add)
     ts(pf(5), pi(3), 3.0, A.is_ge, -5 * LN2, A.mult); ts(pf(6), pf(5), 10 * LN2, A.add); tt(pf(7), pf(2), pf(6), A.add)
@@ -280,217 +349,155 @@ def build(g, core, T, topo, r):
     for wv, c in ((WX, 4), (WE, 2), (WR, 7)):
         act(wv, R("ONE", 0, 128, 1, 8), F.Exp, scale=pf(c, 8))
     setrow(WE, 6, (682.5 - CEN) / 1024); setrow(WR, 6, 31.5)
-    WX, WE, WR, WK = R("WS", 0, 128, 1, 6), R("WS", 128, 128, 1, 7), R("WS", 256, 128, 1, 7), R("WS", 384, 128, 1, 7)
-    act(WK, WE, F.Identity, scale=1024.0)
-    ms(R("VW", 0, 56), 0.0); ms(R("VW", 0, 1), 2.0); ms(R("VW", 48, 1), -3.0); ms(R("VW", 49, 5), -1.0)
-    for j in range(1, 6):
-        ms(R("VW", 8 * j + j, 1), 2.0 / 4 ** j); ms(R("VW", 8 * j + j - 1, 1), -2.0 / 4 ** (j - 1))
-    KJ = [256.0 / 4 ** j * (RC[j] - RC[j + 1]) for j in range(6)]
+    WX, WE, WR = R("WS", 0, 128, 1, 6), R("WS", 128, 128, 1, 7), R("WS", 256, 128, 1, 7)
+    BL = [R("BLK", 128 * j, 128) for j in range(4)]
+    ZM, ZN, ZB, ZC, TH, TN = [R("ZM", 128 * j, 128) for j in range(6)]
+    ts(BL[0], R("BI", 0, 128), pf(0), A.is_equal)
+    ts(BL[1], R("COL", 15, 128), pf(1), A.is_gt, -63.0 / 32, A.mult); aff("S", BL[1], BL[1], 1.0, -1.0 / 32)
+    tt(BL[1], BL[1], BL[0], A.mult); aff("S", BL[2], ID, 33.0 / 32, 0.0); tt(ZM, BL[1], BL[2], A.add)
+    act(ZN, ZM, F.Identity, scale=-1.0)
+    aff("S", BL[3], BL[0], -0.5, 0.0); tt(BL[3], BL[3], ID, A.add)
+    act(ZB, BL[3], F.Identity, scale=2.0 ** 76); act(ZC, BL[3], F.Identity, scale=-2.0 ** 76)
+    ts(pf(9), pi(3), 6.0, A.is_equal, 2.0 ** 28, A.mult)
+    act(TN[:4] + (8,), R("ONE", 0, 128, 1, 8), F.Identity, scale=pf(9, 8)); act(TH[:4] + (8,), TN[:4] + (8,), F.Identity, scale=-1.0)
+    TH, TN = TH[:4] + (7,), TN[:4] + (7,)
+    KP, KN = R("KS", 0, 128, 1, 9), R("KS", 128, 128, 1, 9)
+    tt(pf(15), R("ID", 8, 1), R("ID", 7, 1), A.subtract); ts(pf(16), pf(15), 2.0 ** 77, A.mult)
+    act(KP, R("ONE", 0, 128, 1, 9), F.Identity, scale=pf(16, 9)); act(KN, KP, F.Identity, scale=-1.0)
+    aff("S", R("IOT", 0, E), AN, 1.0, -P * r - 384.0); ms(vw(7, 7, 2), 1.0); ms(vw(8, 7, 2), -1.0)
+    WK = R("WS", 384, 128, 1, 7); act(WK, WE, F.Identity, scale=1024.0)
+    KJ = [256.0 / 4 ** j * (RC[j] - RC[j + 1]) + (192.0 if j == 0 else 64.0) for j in range(6)]
     ms(pf(8), -KJ[2] - 0.5)
     for j in (0, 1, 5):
         setrow(pf(8), j, -KJ[j] - 0.5)
-    setrow(pf(8), 6, 1.0)
-    ms(R("SLOT", 0, 128), 0.0); ms(R("SLOT", 384, 128), 0.0); ms(R("COFF", 0, 16 * RO), 0)
-
-    def names(zi, c, w):
-        aff("S", R("NI", c, w), zi, 1.0 / 64, -31.5 / 64); ts(R("I1", c, w), zi, 42, A.bitwise_and)
-
-    def split(zi, s, bank):
-        c = s * E
-        aff("S", bank, R("I1", c, E), 31.0, -CEN)
-        ts(R("I2", c, E), zi, 63, A.bitwise_and); tt(R("SK", c, E), R("I2", c, E), bank, A.add)
-        aff("S", R("NE", c, E), R("NI", c, E), 6.0, -6.0 * HALF)
-
-    def behind(first, back=1):
-        gate = [i for i in range(first) if ops[i]["wr"] and ops[i]["wr"][0][0] == "TAB"][-back]
-        for o in ops[first:]:
-            o["after"].append(gate)
-
-    def prep(t, f1):
-        s = t % 3; c = s * E
-        n = R("NI", c, E); sl = R("SLOT", 384 * (t % 2) + 128, E); f2, f3 = R("F2", 0, E), R("F3", 0, E)
-        aff("S", R("Q1", 0, E), n, 1.0 / 3, -1.0 / 3)
-        aff("S", f1, n, float(REG), -float(REG * s)); aff("S", f2, R("Q1", 0, E), 1.0 - 3 * REG, 0.0)
-        if s == 0:
-            tt(sl, f1, f2, A.add)
-        else:
-            tt(f3, f1, f2, A.add); act(f2, f3, F.Sign, bias=0.5); aff("S", f1, f2, -1.5 * REG, 1.5 * REG); tt(sl, f3, f1, A.add)
-        cp(R("OFF", t * E, E), sl)
-
-    def wrap(t, bank):
-        m = 16 * (t + 1)
-        for h4 in range(0, 16, 4):
-            mm([(R(bank, 496 + h, 1, 1, m), R("SLOT", 384 * (t % 2) + 128 + 16 * h - 16 * t, m), R("ID", 17 * t, 1), True, True)
-                for h in range(h4, h4 + 4)])
-        cp(R("COFF", 16 * t, 16, 1, m), R(bank, 496, 16, 1, m))
-        ts(pf(10 + t), R("ID", 17 * t + 3, 1), U10, A.mult)
-        act(R("SEL", 128 * t, 128), ONE, F.Identity, scale=pf(10 + t))
-        act(R("SELB", 128 * t, 128), R("SEL", 128 * t, 128), F.Identity, scale=-512 * SHIFT)
-
-    for j, (s, c0, w, ways) in enumerate(C["START"]):
-        c = s * E + c0; zi = R("Z", 3 * c0 + s, w, 3); b1 = R("P%d" % (2 + j % 3), 0, w); b2 = R("P%d" % (5 + j % 3), 0, w)
-        first = len(ops)
-        names(zi, c, w)
-        aff("S", R("MF", c, w), R("I1", c, w), 1.0, 0.0)
-        tt(R("EQ", c, w), R("NI", c, w), R(AP_[s][0], AP_[s][1] + c0, w), A.is_equal)
-        aff("S", R("NP", c, w), R("NI", c, w), 6080.0, -6144.0 * HALF - CEN)
-        mm([(b1, I25, R("EQ", c, w), True, False), (b1, I31, R("MF", c, w), False, True)])
-        tt(b2, zi, R("NP", c, w), A.add) if C.get("E2") else tt(b2, R("NP", c, w), b1, A.add)
-        tt(R("TAB", s * REG + r * E + c0, w), zi, b2, A.add)
-        send(s, c0, c0 + w)
-        rank_up(first, 8000 - 1500 * j)
-    first = len(ops)
-    prep(0, R("P1", 256, E)); wrap(0, "P7")
-    for s in range(3):
-        split(R("Z", s, E, 3), s, R("P%d" % (2 + s), 256, E))
+    setrow(pf(8), 6, 1.0); setrow(pf(8), 7, 0.5); setrow(pf(8), 8, -0.5)
+    prep(1, R("P3", 256, E)); split(R("Z", 1, E, 3), 1, R("P4", 256, E))
     aff("S", R("RAW", 0, P), R("Z", 0, P), 1.0, 0.0)
-    prep(1, R("P1", 256, E))
-    behind(first, C.get("BK0", 1))
 
-    BANK = [("P0", "P2", "P3"), ("P1", "P4", "P5"), ("P1", "P6", "P7")]
     for t in range(RO):
-        s = t % 3; last = t == RO - 1
-        CH = C["CHL"] if last else C["CH"]
+        s = t % 3; last = t == RO - 1; now[0] = t
         sel, selb = R("SEL", 128 * t, 128), R("SELB", 128 * t, 128)
-        h1 = CH[1][0]
-        for hi, (i0, w) in enumerate([(0, h1), (h1, E - h1)]):
-            o = gather("B", R("VB", i0, w), t, R("COFF", 16 * t + i0 // 16, w // 16)); ops[o]["up"] = 9000
-            ops[o]["after"] += [i for i, x in enumerate(ops) if x.get("up", 0) < -5000 and x["q"] == "V"]
-            if C["FL"][hi] == "S":
-                o = act(R("FL", i0, w), R("VB", i0, w), F.Sign)
-            else:
-                o = ts(R("FL", i0, w), R("VB", i0, w), 1.0, A.min, -1.0, A.max)
-            ops[o]["up"] = 8000
-            first = len(ops); rep = C["REP"][hi]
-            for j in range(rep - 1, -1, -1):
-                B = R("P%d" % hi, j, w, rep)
-                mm([(B, sel, R("VB", i0, w), True, False)])
-                mm([(B, selb, R("FL", i0, w), False, True)])
-            rank_up(first, 8000 - 1000 * hi)
-            a = i0
-            if hi == 0 and C["VG"]:
-                o2 = gather("V", RG(a, C["VG"]), t, R("OFF", t * E + a, C["VG"])); a += C["VG"]
-                ops[o2]["after"].append(o - 1)
-            while a < i0 + w:
-                n = min(C["SG0"] if a == C["VG"] else C["SG"], i0 + w - a)
-                n = min([n] + [c - a for (c, _) in CH if c > a])
-                o3 = gather("S", RG(a, n), t, R("OFF", t * E + a, n)); a += n
-                ops[o3]["up"] = 3900 - 10 * a
+        if not last:
+            name("sel"); select(t + 1)
+        for h, (i0, w) in enumerate(C["VB"]):
+            name("vb%d" % h); gather("B", R("VB", i0, w), t, R("COFF", 16 * t + i0 // 16, w // 16))
+            name("fl%d" % h); ts(R("FL", i0, w), R("VB", i0, w), 1.0, A.min, -1.0, A.max)
+        a = 0
+        for j, (q, n) in enumerate(C["GATH"]):
+            name("g%d" % j); gather(q, R("G", 16 * a, 16 * n), t, R("OFF", t * E + a, n)); a += n
         late = []
-        for ci, (i0, w) in enumerate(CH):
-            pa, pb, pc = BANK[ci]
+        for c, (i0, w) in enumerate(C["PARTS"]):
+            pa, pb, pc = "P%d" % c, "P%d" % (2 + 2 * c), "P%d" % (3 + 2 * c)
             X = lambda n, pn=128, i0=i0, w=w: R(n, i0, w, 1, pn)
-            rep = C["REP"][min(ci, 1)]; b0 = rep * (i0 - (h1 if ci else 0))
-            B = R(pa, b0, w, rep); BR = R(pa, b0, w * rep)
-            S1, XP, ZP, RB = [R(pb, w * j, w) for j in range(4)]
-            VO, WO, ZQ, BQ = [R(pc, w * j, w) for j in range(4)]
-            VO = VO[:4] + (8,)
-            first = len(ops)
-            early = [tt(X("OWN"), R("NE", s * E + i0, w), B, A.is_equal), tt(X("SKIP"), R("AE", s * E + i0, w), B, A.is_equal)]
-            aff("S", X("TB"), B, 32.0 / 3, 64.0 * HALF)
-            mm([(S1, IH[1.0], R("SK", s * E + i0, w), True, False)])
-            KC = C["KCUT"][ci]
-            for k0, k1 in zip(KC, KC[1:]):
-                for k in range(k0, k1, rep):
-                    tt(R("D", 16 * i0 + k * w, w * rep), R("G", 16 * i0 + k // rep, w * rep, 16 // rep), BR, A.subtract)
+            nm = lambda n, c=c: name("%s%d" % (n, c))
+            nk = lambda n, k, c=c: name("%s%d%x" % (n, c, k))
+            S1, XP, ZP = [R(pb, w * j, w) for j in range(3)]
+            BQ, WO, ZQ = [R(pc, w * j, w) for j in range(3)]
+            VO = BQ[:4] + (9,); RB = S1; NB = BQ
+            for n, bank in C["OWNBANK"][c].items():
+                if n == "ZP":
+                    ZP = R(bank, 0, w)
+                elif n == "ZQ":
+                    ZQ, BQ, RB = [R(bank, w * j, w) for j in range(3)]
+                else:
+                    NB = R(bank, 0, w)
+            rep = C["REP"][c]; B = R(pa, 0, w, rep); qs = C["PLACE"][c]
+            for j in range(rep - 1, -1, -1):
+                nk("b", j); mm([(R(pa, j, w, rep), sel, X("VB"), True, False)])
+                nk("B", j); mm([(R(pa, j, w, rep), selb, X("FL"), False, True)])
+            nm("own"); tt(X("OWN"), R("NE", s * E + i0, w), B, A.is_equal)
+            nm("tb"); aff("S", X("TB"), B, 32.0 / 3, 64.0 * HALF)
+            nm("sk"); mm([(S1, IH[1.0], R("SK", s * E + i0, w), True, False)])
+            k = 0; rows = []; free = list(range(16))
+            for n in C["SUB"][c]:
+                q = free[0]; mine = [q + 16 // n * j for j in range(n)]; free = [x for x in free if x not in mine]
+                nk("d", k); tt(R("D", 16 * i0 + k * w, w * n), R("G", 16 * i0 + q, w * n, 16 // n), R(pa, 0, w * n, rep // n), A.subtract)
+                rows += [(x, R("D", 16 * i0 + k * w + j, w, n)) for j, x in enumerate(mine)]; k += n
+            for k0, k1 in zip(C["KCUT"][c], C["KCUT"][c][1:]):
                 d4 = R("D", 16 * i0 + k0 * w, (k1 - k0) * w)
-                ts(d4, d4, HI, A.min, LO, A.max)
-                it = [(S1, R("WB", 15 - k // rep - 16 // rep * (k % rep), 128), R("D", 16 * i0 + (k - k % rep) * w + k % rep, w, rep), False, k == 15) for k in range(k0, k1)]
-                if k0 == KC[1]:
-                    it = [(S1, IH[4096.0], X("OWN"), False, False)] + it
-                for j in range(0, len(it), C["MMN"]):
-                    mm(it[j:j + C["MMN"]])
-            qs = C["PLACE"][ci]
-            aff(qs[0], X("SI"), S1, 1.0, 16 * 4780.0 + CEN)
-            ts(X("U"), X("SI"), 0x1555, A.bitwise_and)
+                nk("c", k0); ts(d4, d4, HI, A.min, LO, A.max)
+            for k0 in range(0, 16, C["MMN"]):
+                if k0 == 8:
+                    nm("so"); mm([(S1, IH[4096.0], X("OWN"), False, False)])
+                nk("m", k0); mm([(S1, R("WB", 15 - rows[k][0], 128), rows[k][1], False, k == 15) for k in range(k0, k0 + C["MMN"])])
+            nm("sx"); aff("S", X("SP", 1), B[:4] + (1,), 1.0 / 6, HALF - P * r - s - 384.0)
+            nm("x"); mm([(VO, vw(7)[:4] + (1,), X("SP", 1), True, False), (VO, vw(8)[:4] + (1,), X("IOT", 1), False, False)])
+            nm("si"); aff(qs[0], X("SI"), S1, 1.0, 16 * 4780.0 + CEN)
+            nm("u"); ts(X("U"), X("SI"), 0x1555, A.bitwise_and)
+            nm("w")
             if qs[1] == "S":
                 act(X("W"), X("U"), F.Relu, bias=-4095.0)
             else:
                 ts(X("W"), X("U"), 4095.0, A.subtract, 0.0, A.max)
-            if qs[2] == "S":
-                act(X("TES"), X("W"), F.Sign)
-            elif qs[2] == "V":
-                ts(X("TES"), X("W"), 1.0, A.min)
-            elif qs[2] == "s":
-                act(X("TES"), X("U"), F.Relu, bias=-4095.0 / 2048, scale=1.0 / 2048)
-            vw = lambda j: R("VW", 8 * j, 8)
+            nm("te"); act(X("TES"), X("U"), F.Sign, bias=-4095.5)
             for j in range(1, 6):
-                aff(qs[2 + j], X("R%d" % j), X("W"), 1.0, RC[j] - 0.5)
-            mm([(VO, vw(0), X("W"), True, False)])
-            mm([(VO, vw(6), X("TES"), False, False), (VO, vw(1), X("R1"), False, False)])
-            mm([(VO, vw(j), X("R%d" % j), False, False) for j in (2, 3)])
-            mm([(VO, vw(j), X("R%d" % j), False, j == 5) for j in (4, 5)])
-            mm([(XP, IH[1025.0], X("W"), True, False), (XP, IH[-1033.0], X("TES"), False, False)])
-            act(X("SG", 8), VO, F.Sign, bias=pf(8, 8))
-            mm([(XP, WX, X("SG", 6), False, True)])
-            aff(qs[8], X("SI"), XP, 1.0, 0x111111 / 2.0 + 8)
+                nm("r%d" % j); aff(qs[1 + j], X("R%d" % j), X("W"), 1.0, RC[j] - 0.5)
+            nm("va"); mm([(VO, vw(6), X("TES"), False, False), (VO, vw(0), X("W"), False, False)])
+            for j, js in enumerate(C["VO"][c]):
+                nm("v" + "efg"[j]); mm([(VO, vw(i), X("R%d" % i), False, i == C["VO"][c][-1][-1]) for i in js])
+            nm("xa"); mm([(XP, IH[1025.0], X("W"), True, False), (XP, IH[-516.5], X("TES"), False, False)])
+            nm("sg"); act(X("SG", 9), VO, F.Sign, bias=pf(8, 9))
+            nm("xb"); mm([(XP, WX, X("SG", 6), False, True)])
+            nm("sj"); aff(qs[7], X("SJ"), XP, 1.0, 0x111111 / 2.0 + 8 - 516.5)
             if not last:
-                if C["NVP"][ci] == "P":
-                    NB = R("P%d" % (6 + ci), 0, w)
-                    mm([(NB, sel, X("VB"), True, False), (NB, selb, X("FL"), False, False)])
-                    mm([(NB, WE, X("SG", 7), False, True)])
-                    aff(qs[10], X("NV"), NB, 1024.0, 0.0)
+                if C["NV"][c] == "V":
+                    nm("na"); aff("S", X("NV"), B, 1024.0, 0.0)
+                    nm("nb"); mm([(NB, WK, X("SG", 7), True, True)])
+                    nm("nv"); tt(X("NV"), X("NV"), NB, A.add)
                 else:
-                    NB = R(pc, 0, w)
-                    aff("S", X("NV"), B, 1024.0, 0.0)
-                    mm([(NB, WK, X("SG", 7), True, True)])
-                    tt(X("NV"), X("NV"), NB, A.add)
-            mm([(WO, WR, X("SG", 7), True, True)])
-            for (zz, zb, th) in ((ZQ, ZC, TN), (ZP, ZB, TH)):
-                mm([(zz, zb, X("OWN"), True, False), (zz, zb, X("SKIP"), False, False), (zz, th, X("SG", 7), False, False)])
-            ts(X("U"), X("SI"), 0x111119, A.bitwise_and)
-            aff(qs[9], X("SI"), X("U"), 0x111111 / 2.0 ** 20, 1.5 * 2 ** 23 + 8)
-            ts(X("U"), X("SI"), 15, A.bitwise_and)
-            act(X("EX"), X("U"), F.Exp, bias=-18 * LN2, scale=6 * LN2)
-            raw = R("RAW", 3 * i0 + s, w, 3)
+                    nm("na"); mm([(NB, sel, X("VB"), True, False), (NB, selb, X("FL"), False, False)])
+                    nm("nb"); mm([(NB, WE, X("SG", 7), False, True)])
+                    nm("nv"); aff("S", X("NV"), NB, 1024.0, 0.0)
+            nm("wo"); mm([(WO, WR, X("SG", 7), True, True)])
             if last:
-                tt(X("DR"), X("TB"), WO, A.add)
-            mm([(ZP, ZM, X("EX"), False, True)])
-            mm([(ZQ, ZN, X("EX"), False, True)])
-
-            def plain(X=X, WO=WO, ZP=ZP, ZQ=ZQ, RB=RB, raw=raw, last=last):
-                if not last:
-                    tt(X("DR"), X("TB"), WO, A.add)
-                tt(X("DR"), X("DR"), ZP, A.min); tt(RB, raw, ZQ, A.min); tt(raw, X("DR"), RB, A.max)
+                nm("nv"); tt(X("DR"), X("TB"), WO, A.add)
+            for (zz, zb, th, ks, n) in ((ZQ, ZC, TN, KN, "q"), (ZP, ZB, TH, KP, "p")):
+                nm(n + "a"); mm([(zz, zb, X("OWN"), True, False)])
+                nm(n + "t"); mm([(zz, ks, X("SG", 9), False, False), (zz, th, X("SG", 7), False, False)])
+            nm("uj"); ts(X("UJ"), X("SJ"), 0x111119, A.bitwise_and)
+            nm("sm"); aff(qs[8], X("SJ"), X("UJ"), 0x111111 / 2.0 ** 20, 1.5 * 2 ** 23 + 8)
+            nm("uk"); ts(X("UJ"), X("SJ"), 15, A.bitwise_and)
+            nm("ex"); act(X("EX"), X("UJ"), F.Exp, bias=-18 * LN2, scale=6 * LN2)
+            nm("pb"); mm([(ZP, ZM, X("EX"), False, True)])
+            nm("qb"); mm([(ZQ, ZN, X("EX"), False, True)])
+            raw = R("RAW", 3 * i0 + s, w, 3)
             if not last:
-                tt(X("M1"), X("NV"), ZP, A.min)
-                tt(BQ, R("TAB", t * REG + r * E + i0, w), ZQ, A.min)
-                tt(R("TAB", (t + 3) * REG + r * E + i0, w), X("M1"), BQ, A.max)
-                send(t + 3, i0, i0 + w)
+                m1, m2 = R("M1", t * E + i0, w), R("M2", t * E + i0, w) if C["FOLD"][c] else BQ
+                nm("mi"); tt(m1, X("NV"), ZP, A.min)
+                nm("bq"); tt(m2, R("TAB", t * REG + r * E + i0, w), ZQ, A.min)
+                nm("mx"); tt(R("TAB", (t + 3) * REG + r * E + i0, w), m1, m2, A.max)
+                nm("send"); send(t * E if C["FOLD"][c] else None)
+
+                def plain(X=X, nm=nm, WO=WO, ZP=ZP, ZQ=ZQ, RB=RB, raw=raw):
+                    nm("dr"); tt(X("DR"), X("TB"), WO, A.add)
+                    nm("ds"); tt(X("DR"), X("DR"), ZP, A.min)
+                    nm("rb"); tt(RB, raw, ZQ, A.min)
+                    nm("rw"); tt(raw, X("DR"), RB, A.max)
                 late.append(plain)
             else:
-                plain()
-                o = add("Y", lambda i0=i0, w=w: g.sync.dma_start(T.yk[:, 3 * i0:3 * (i0 + w)], T.RAW[:, 3 * i0:3 * (i0 + w)]),
-                        [R("RAW", 3 * i0, 3 * w)], [], 600)
-                ops[o]["dma"] = "st%d" % ci
-                add("N%d" % len(ops), None, [], [], 2000, [o])
-            rank_up(first, C["UP"][ci])
-            for o in early:
-                ops[o]["up"] += C["UPO"]
-        if not last:
-            first = len(ops)
+                nm("mi"); tt(X("DR"), X("DR"), ZP, A.min)
+                nm("bq"); tt(BQ, raw, ZQ, A.min)
+                nm("mx"); tt(raw, X("DR"), BQ, A.max)
+                nm("send")
+                o = add("Y", lambda i0=i0, w=w: g.sync.dma_start(T.yk[:, 3 * i0:3 * (i0 + w)], T.RAW[:, 3 * i0:3 * (i0 + w)]), [R("RAW", 3 * i0, 3 * w)], [])
+                ops[o]["dma"] = "st%d" % c
+        for f in late:
+            f()
+        if t in (0, 1):
+            name("zi"); aff("S", R("ZI", E * t, E), R("RAW", t, E, 3), 1.0, 0.0)
+        if t in (1, 2):
+            names(R("ZI", E * (t - 1), E), E * (t - 1), E)
+        if t <= 2:
+            prep(t + 2, R("P1", 128, E))
+        if t <= 3:
             wrap(t + 1, "P0")
-            behind(first, C.get("BKW", 2)); rank_up(first, -8000)
-            first = len(ops)
-            for f in late:
-                f()
-            behind(first); rank_up(first, -20000)
-            first = len(ops)
-            if t in (1, 2):
-                names(R("ZI", E * (t - 1), E), E * (t - 1), E)
-                split(R("ZI", E * (t - 1), E), t - 1, R("P0", 128, E))
-            if t <= 2:
-                prep(t + 2, R("P1", 128, E))
-            behind(first, C.get("BKP", 2)); rank_up(first, -10000)
-            if t < 2:
-                first = len(ops)
-                aff("S", R("ZI", E * t, E), R("RAW", t, E, 3), 1.0, 0.0)
-                rank_up(first, -30000)
+        if t in (0, 2, 3):
+            split(R("ZI", E * (t - 2), E) if t else R("Z", 2, E, 3), (t + 1) % 3 if t else 2, R("P0", 128, E))
     return ops, sent[0]
 
 
-def order(ops):
-    n = len(ops); deps = [set(o["after"]) for o in ops]; acc = {}
+def depend(ops):
+    deps = [set(o["after"]) for o in ops]; acc = {}
     for i, o in enumerate(ops):
         for kind, lst in (("r", o["rd"]), ("w", o["wr"])):
             for x in lst:
@@ -505,50 +512,30 @@ def order(ops):
                 if kind == "w" and x[3] == 1 and x[4] == 128:
                     l[:] = [z for z in l if not (x[1] <= z[2][1] and z[2][2] <= x[2])]
                 l.append((i, kind, x))
-    succ = [[] for _ in ops]
-    for i in range(n):
-        for j in deps[i]:
-            succ[j].append(i)
-    banks = [sorted({x[0] for x in o["rd"] + o["wr"] if SCRATCH[x[0]][0] == "psum"}) for o in ops]
+    return deps
 
-    def lay(key, before, after):
-        left = [len(d) for d in before]; ready = [i for i in range(n) if not left[i]]
-        st = [0.0] * n; held = {}
-        while ready:
-            i = min(ready, key=lambda i: (key[i], i)); ready.remove(i)
-            q = ops[i]["q"]; c = ops[i]["cost"]
-            s = max([st[j] + ops[j]["cost"] + (0 if q == ops[j]["q"] == "P" else HOP) for j in before[i]] or [0.0])
-            busy = [(a, b) for (a, b, _) in held.get(q, []) if b > s]
-            for x in banks[i]:
-                busy += [(a - HOP, b + HOP) for (a, b, q2) in held.get(x, []) if q2 != q and b + HOP > s]
-            for (a, b) in sorted(busy):
-                if a >= s + c:
-                    break
-                s = max(s, b)
-            st[i] = s
-            for x in [q] + banks[i]:
-                held.setdefault(x, []).append((s, s + c, q))
-            for j in after[i]:
-                left[j] -= 1
-                if not left[j]:
-                    ready.append(j)
-        return st, max(s + o["cost"] for s, o in zip(st, ops))
 
-    pr = [0.0] * n
-    for i in range(n - 1, -1, -1):
-        pr[i] = ops[i]["cost"] + max([pr[j] + HOP for j in succ[i]] or [0])
-    st, best = lay([-p - CFG["UPW"] * o.get("up", 0) for p, o in zip(pr, ops)], deps, succ); keep = st
-    rng = numpy.random.default_rng(CFG["SEED"])
-    for p in range(CFG["PASSES"]):
-        jit = rng.normal(0.0, CFG["JIT"] if p else 0.0, n) * (rng.random(n) < CFG["JP"])
-        back, _t = lay([-s - o["cost"] + float(e) for s, o, e in zip(keep, ops, jit)], succ, deps)
-        st, span = lay([-s - o["cost"] for s, o in zip(back, ops)], deps, succ)
-        if span <= best:
-            best, keep = span, st
-    seq = sorted(range(n), key=lambda i: (keep[i], i)); bank = {}
+def order(ops, deps, names):
+    at = {n: k for k, n in enumerate(names)}
+    key = [(o["t"], at.get(o["name"], len(names)) if o["t"] >= 0 else 0, i) for i, o in enumerate(ops)]
+    left = [i for i, o in enumerate(ops) if -1 < o["t"] < 0]; end = {}; free = {}
+    while left:
+        can = [(max([free.get(ops[i]["q"], 0)] + [end.get(j, 0) + 100 for j in deps[i]]), i) for i in left if not deps[i] & set(left)]
+        s, i = min(can); x = ops[i]["wr"][0]; left.remove(i); key[i] = (-0.5, s, i)
+        end[i] = free[ops[i]["q"]] = s + (600 if ops[i]["q"] == "P" else 60 + max(64, (x[2] - x[1]) // x[3]) * (2 if ops[i]["q"] == "G" else 1))
+    seq = []; seen = set()
+
+    def put(i):
+        if i not in seen:
+            seen.add(i)
+            for j in sorted(deps[i], key=lambda j: key[j]):
+                put(j)
+            seq.append(i)
+    for i in sorted(range(len(ops)), key=lambda i: key[i]):
+        put(i)
+    deps = [set(d) for d in deps]; bank = {}
     for i in seq:
-        ops[i]["t"] = keep[i]
-        for x in banks[i]:
+        for x in {x[0] for x in ops[i]["rd"] + ops[i]["wr"] if SCRATCH[x[0]][0] == "psum"}:
             d = bank.setdefault(x, {})
             deps[i].update(j for q2, j in d.items() if q2 != ops[i]["q"])
             d[ops[i]["q"]] = i
@@ -560,7 +547,7 @@ def rank_program(g, core, T, topo):
     if r is None:
         return helper_program(g, core, T, topo)
     ops, sent = build(g, core, T, topo, r)
-    seq, deps = order(ops)
+    seq, deps = order(ops, depend(ops), CFG["ORDER"].split())
     Q = {"V": g.vector, "S": g.scalar, "P": g.tensor, "G": g, "Y": g.sync}
     used = set(); place = {i: k for k, i in enumerate(seq)}
     for i in seq:
@@ -570,16 +557,14 @@ def rank_program(g, core, T, topo):
     cnt = {}; sig = {}; known = {}; clock = {}
     for i in seq:
         o = ops[i]; q = o["q"]
-        if o["fn"] is None:
-            continue
         kn = known.setdefault(q, {}); want = {}
         for j in deps[i]:
             if j in sig and not (q == ops[j]["q"] == "P"):
                 s, v = sig[j]
                 if v > want.get(s, (0, 0))[0]:
                     want[s] = (v, j)
-        if o["ext"]:
-            want[o["ext"][0]] = (o["ext"][1], None)
+        for s, v in (o["ext"] or {}).items():
+            want[s] = (v, None)
         for s, (v, j) in sorted(want.items(), key=lambda z: -(place[z[1][1]] if z[1][1] is not None else 10 ** 9)):
             if kn.get(s, 0) < v:
                 Q[q].wait_ge(T.sem[s], v); kn[s] = v

@@ -10,46 +10,44 @@ U10 = 1.0 / 1024
 HI, LO = 3412.0 * U10, -4780.0 * U10
 SHIFT = 32768.0
 LN2 = math.log(2.0)
-RC = [0, 4096.0, 2048.0, 8192.0, 32768.0, 131072.0, 0.0]
-NH, LW = 16, 160
+RC = [0, 4096.0, 2064.0, 8192.0, 32768.0, 131072.0, 0.0]
+NH, LW = 24, 160
 FAR0, FAR1, NEAR0, NEAR1 = ("far", 0), ("far", 1), ("near", 0), ("near", 1)
 CFG = {
     "LOAD": [0, 384, 768],
     "ENC": [(0, 0, 128), (1, 0, 128), (2, 0, 128), (0, 128, 128), (1, 128, 128), (2, 128, 128)],
     "START": [[(0, 0, 128, ("fwd", "nf"))], [(1, 0, 128, FAR0 + ("in",)), (2, 0, 128, ("fwd", "nf"))],
               [(0, 128, 128, FAR1 + ("in",)), (1, 128, 128, None)], [(2, 128, 128, NEAR0 + ("in",))]],
+    "LAG": 2.5, "PIPE": "a0 a1 b0 a2 b1 a3 c0 b2 a4 c1 b3 a5 c2 b4 b5 c3 c4 c5",
     "TURN": [1, 2, 3, 4, 5],
-    "PARTS": [(0, 128), (128, 128)],
-    "SEND": [[(0, 64, FAR0 + ("in",)), (64, 64, FAR1 + ("out",))], [(128, 128, None)]], "FOLD": [0, 0],
+    "PARTS": [(0, 128), (128, 64), (192, 64)],
+    "SEND": [[(0, 64, ("fwd", "nf")), (64, 64, FAR0 + ("in",))], [(128, 128, None)]], "FOLD": [0, 0, 0],
     "VB": [(0, 128), (128, 128)],
-    "GATH": [("V", 48), ("S", 80), ("S", 64), ("S", 64)],
+    "GATH": [("S", 32), ("V", 24), ("S", 40), ("S", 32), ("S", 32), ("S", 32), ("S", 32), ("S", 16), ("S", 16)],
     "REP": [2, 4],
     "SUB": [[2] * 8, [4, 4, 4, 2, 2]],
-    "KCUT": [[0, 6, 12, 14, 16], [0, 8, 12, 14, 16]], "MMN": 2,
-    "VO": [[(1, 2), (3, 4), (5,)], [(1, 3), (2, 5), (4,)]],
-    "NV": "VV", "OWNBANK": [{"ZP": "P6", "ZQ": "P7"}, {}],
-    "PLACE": ['SSSSSSSSV', 'SVSSVSVVV'],
-    "ORDER": """sel vb0 g1 vb1 fl0 g0 fl1 g3 sk0 sk1 b01 b13 B01 b00 B00 B13 b12 B12 b11 B11 b10 B10
-        d02 d00 d04 d08 d06 c00 d0a own0 c06 d0c d0e c0c c0e m00 m02 m04 m06 so0 m08 m0a m0c m0e sx1 g2 own1
-        d14 sx0 si0 na0 u0 d10 w0 te0 qa0 x1 pa0 x0 c10 d18 d1c c18 d1e r20 r10 r40 r30 r50 xa0 va0 ve0 m10 vf0 vg0 m12 m14 m16
-        ni sg0 xb0 sj0 tb0 so1 m18 m1a c1c c1e m1c m1e uj0 tb1 si1 sm0 uk0 u1 ex0 te1 w1 nb0 pt0 qt0 wo0 qb0 pb0
-        va1 r11 r21 r41 nv0 r31 r51 bq0 mi0 ve1 vf1 vg1 mx0 na1 sg1 xa1 xb1 sj1 uj1 sm1 uk1 nb1 wo1 qa1 qt1 pa1 pt1 ex1
-        q1 f1 f2 mf ne nv1 pb1 qb1 mi1 bq1 mx1 send0 send1
-        wr0 wr1 wr2 wr3 f3 rb0 dr0 rb1 dr1 ds0 f4 f5 i2 rw0 sl ds1 off i1 skm co rw1 zi""",
+    "KCUT": [[0, 4, 10, 14, 16], [0, 4, 8, 12, 14, 16]], "MMN": 2, "SO": [4, 0, 0],
+    "VO": [[(1, 2), (3, 4), (5,)], [(1, 3), (2, 5), (4,)], [(1, 3), (2, 5), (4,)]],
+    "HALVES": [(0, 128), (128, 128)],
+    "OWNBANK": [{}, {}, {}],
+    "PLACE": ['SSVSSSSSV', 'VVVSSVVSS', 'VVVSVSVVS'],
+    "ORDER": """sel vb0 vb1 fl0 g1 fl1 b01 B01 b00 B00 g0 g2 d00 d02 d04 d06 d08 d0a g3 g4 g5 own0 c00 c04 b13 sk1 B13 b12 sk0 sk2 B12 b11 B11 b10 B10 m00 m02 so0 m04 m06 d0c d0e own1 c0e c0a so1 m08 m0a m0c m0e so2 d10 d14 c10 c14 g6 g8 si0 sx0 g7 na0 u0 w0 te0 d18 d1e r10 c18 d1c r20 r40 r30 r50 tb0 zi m20 m10 x0 m22 m24 m26 m12 m14 m16 xa0 va0 ve0 c1e c1c i2 m18 m28 m2a vf0 vg0 m1a m2c m2e m1c m1e si2 si1 u2 u1 w2 w1 sx1 sg0 xb0 ni na1 pa0 x1 x2 nb0 xa1 sj0 te2 te1 r31 r21 r42 tb1 r22 q1 r12 r51 r11 r32 uj0 r41 r52 va2 va1 ve2 ve1 vf1 vg1 sm0 nv0 uk0 i1 vf2 vg2 sg1 xa2 pt0 qa0 xb1 sg2 ex0 xb2 sj2 sj1 uj1 nb1 qt0 pb0 qb0 qa1 q2 sm1 uj2 mi0 bq0 sm2 mf uk1 ex1 mx0 uk2 nb2 pa2 pa1 pt2 pt1 qa2 qt1 nv2 nv1 skm ex2 ne f1 f2 wo0 pb1 qt2 qb1 wo1 pb2 qb2 wo2 mi1 bq1 mi2 bq2 mx1 mx2 send0 send1 rb2 dr1 f3 dr2 rb1 sl ds2 dr0 ds1 ds0 rw1 rb0 ta rw0 tb rw2 off""",
+    "PLACEL": ['SSSSSSSSS', 'SVVVVVSVV', 'VSSSVVSVS'],
+    "LAST": """vb0 vb1 fl0 fl1 g1 g0 g2 g4 g3 g5 g6 b01 B01 b00 B00 sk0 b13 B13 b12 B12 b11 B11 b10 B10 sk2 d00 d02 d0a d08 d04 c00 own0 d06 own1 d0c c04 d0e c0a d10 c0e m00 m02 so0 m04 so2 m06 sk1 m08 m0a so1 m0c m0e c10 d14 sx0 g7 m10 x0 m20 m22 m12 si0 g8 u0 c14 w0 te0 d18 d1c c18 d1e c1c c1e r20 r10 r40 r30 m14 m24 va0 m26 m16 ve0 vf0 r50 m28 vg0 m18 m1a xa0 tb0 sg0 sx1 m1c m1e xb0 m2a m2c m2e si1 u1 si2 w1 u2 sj0 te1 r51 w2 te2 r52 r12 r22 r11 r31 r21 r41 uj0 r32 r42 sm0 uk0 pa0 x1 x2 nb0 qa0 qt0 va1 ve1 vf1 xa1 vg1 va2 ve2 vf2 vg2 sg1 xb1 tb1 sg2 ex0 sj1 nv0 uj1 nb1 xa2 qa1 xb2 pt0 pb0 qt1 pa1 nb2 pt1 qb0 qa2 qt2 sj2 sm1 uj2 sm2 uk1 mi0 nv1 ex1 uk2 ex2 bq0 nv2 qb1 pa2 pt2 pb1 qb2 pb2 mx0 bq1 bq2 mi2 mi1 mx2 mx1 send0 send1""",
 }
 
 SCRATCH = {
     "TAB": ("sbuf", [128, 7 * REG], "float32"), "Z": ("sbuf", [128, P], "int32"), "RAW": ("sbuf", [128, P], "float32"),
     "G": ("sbuf", [128, 16 * E], "float32"), "D": ("sbuf", [128, 16 * E], "float16"),
     "NE": ("sbuf", [128, P], "float32"), "SK": ("sbuf", [128, P], "float16"),
-    "NI": ("sbuf", [128, P], "int32"), "OFF": ("sbuf", [128, RO * E], "uint16"), "COFF": ("sbuf", [128, RO * 16], "uint16"),
+    "NI": ("sbuf", [128, P], "int32"), "OFF": ("sbuf", [128, RO * E], "uint16"), "PERM": ("sbuf", [128, 16], "uint16"),
+    "TT": ("sbuf", [128, 2 * E + 32], "float32"), "PC": ("sbuf", [128, 16], "float32"),
     "SEL": ("sbuf", [128, (RO + 1) * 128], "float32"), "SELB": ("sbuf", [128, (RO + 1) * 128], "bfloat16"),
     "SP": ("sbuf", [128, E], "float16"),
-    "IOT": ("sbuf", [128, E + 16], "float16"), "KS": ("sbuf", [128, 256], "bfloat16"),
-    "SLOT": ("sbuf", [128, 3 * 384], "float32"), "ZI": ("sbuf", [128, 2 * E], "int32"), "AN": ("sbuf", [128, E], "float32"),
+    "SLOT": ("sbuf", [128, E + 64], "float32"), "ZI": ("sbuf", [128, 2 * E], "int32"), "AN": ("sbuf", [128, E], "float32"),
     "I1": ("sbuf", [128, P], "int32"), "I2": ("sbuf", [128, P], "int32"), "EQ": ("sbuf", [128, P], "bfloat16"),
     "MF": ("sbuf", [128, P], "float16"), "NP": ("sbuf", [128, P], "float32"),
-    "Q1": ("sbuf", [128, E], "int32"), "F2": ("sbuf", [128, E], "float32"), "F3": ("sbuf", [128, E], "float32"),
+    "Q1": ("sbuf", [128, 2 * E], "int32"), "F2": ("sbuf", [128, E], "float32"),
     "VB": ("sbuf", [128, E], "float32"), "FL": ("sbuf", [128, E], "bfloat16"), "OWN": ("sbuf", [128, E], "float16"),
     "SI": ("sbuf", [128, E], "int32"), "U": ("sbuf", [128, E], "int32"), "W": ("sbuf", [128, E], "float16"),
     "SJ": ("sbuf", [128, E], "int32"), "UJ": ("sbuf", [128, E], "int32"),
@@ -60,15 +58,15 @@ SCRATCH = {
     "TB": ("sbuf", [128, E], "int32"), "DR": ("sbuf", [128, E], "float32"),
     "ONE": ("sbuf", [128, 128], "float32"), "ID": ("sbuf", [128, 256], "float32"), "COL": ("sbuf", [128, 144], "float32"),
     "WB": ("sbuf", [128, 144], "float16"), "IH": ("sbuf", [128, 4 * 128], "float16"), "IB": ("sbuf", [128, 128], "bfloat16"),
-    "ZM": ("sbuf", [128, 6 * 128], "bfloat16"), "BLK": ("sbuf", [128, 4 * 128], "float32"), "BI": ("sbuf", [128, 128], "int32"),
-    "VW": ("sbuf", [128, 96], "bfloat16"), "WS": ("sbuf", [128, 512], "bfloat16"),
+    "ZM": ("sbuf", [128, 6 * 128], "bfloat16"),
+    "VW": ("sbuf", [128, 40], "bfloat16"), "WS": ("sbuf", [128, 384], "bfloat16"),
     "PI": ("sbuf", [128, 8], "int32"), "PF": ("sbuf", [128, 24], "float32"),
     "LAND": ("sbuf", [128, NH * LW], "float32"),
 }
 for _b in range(8):
     SCRATCH["P%d" % _b] = ("psum", [128, 512], "float32")
-SEMAPHORES = (["sV", "sS", "sP", "sG", "ld0", "ld1", "ld2", "st0", "st1", "sent"] + ["arr%d" % t for t in range(RO)]
-              + ["h%d_%d" % (k, j) for k in range(2 * NH) for j in range(3)])
+SEMAPHORES = (["sV", "sS", "sP", "sG", "ld0", "ld1", "ld2", "st0", "st1", "st2", "sent"] + ["arr%d" % t for t in range(RO)]
+              + ["h%d_%d_%d" % (k, hop, j) for k in range(20) for hop in range(2) for j in range(3)])
 
 
 def ones(m):
@@ -100,47 +98,56 @@ def route(rc, way, T, topo):
         near = [h for h in side if topo.die(h) == topo.die(d)]; far = [h for h in side if h not in near]
         return {"n": near[0], "f": far[-1], "g": far[0]}[letter]
     if way is None:
-        return [(out, dsts, {})]
+        return [(0, rc, out, dsts)]
     if way[0] == "fwd":
-        on = {}
-        for d in [d for d in dsts if topo.same_plane(topo.chip(rc), topo.chip(d))]:
-            mate = [e for e in dsts if topo.mates(topo.chip(d), topo.chip(e))]
-            src = [c for c in T.cores if topo.same_plane(topo.chip(c), topo.chip(d))].index(rc)
-            on[pick(d, mate, way[1][src])] = [d] + mate
+        first = []; src = rc; on = []; hop = 0
         mate = [d for d in dsts if topo.mates(topo.chip(rc), topo.chip(d))]
-        if len(way) == 2:
-            return [(out, mate, on)]
-        return [(out, [], on), (part_of[way[3]], [], {pick(rc, mate, way[2]): mate})]
+        if len(way) > 2:
+            src = pick(rc, mate, way[2]); first = [(0, rc, part_of[way[3]], [src])]; hop = 1
+        for d in [d for d in dsts if topo.same_plane(topo.chip(rc), topo.chip(d))]:
+            j = [c for c in T.cores if topo.same_plane(topo.chip(c), topo.chip(d))].index(rc)
+            e = [e for e in dsts if topo.mates(topo.chip(d), topo.chip(e))]; h = pick(d, e, way[1][j])
+            on += [(hop + 1, h, out, e), (hop + 1, h, part_of["in"], [d])]
+        return first + [(hop, src, out, [x[1] for x in on[::2]] + mate)] + on
     side = [h for h in free(rc) if (topo.die(h) != topo.die(rc)) == (way[0] == "far")]
     full = [h for h in side if all(topo.may_write(h, d) for d in dsts)]
     part = [h for h in side if h not in full]
     a, b = full[way[1] % len(full)], part[way[1] % len(part)]
-    return [(part_of[way[2]], [], {b: [d for d in dsts if topo.may_write(b, d)], a: [d for d in dsts if not topo.may_write(b, d)]})]
+    return [(0, rc, part_of[way[2]], [b, a]), (1, b, out, [d for d in dsts if topo.may_write(b, d)]),
+            (1, a, out, [d for d in dsts if not topo.may_write(b, d)])]
 
 
-def signal(p, rc, T, topo):
-    if p[4] is None:
-        return "arr%d" % p[0]
-    k = [x for call in calls() for x in call if x[4] is not None].index(p)
-    plane = [c for c in T.cores if c == rc or topo.same_plane(topo.chip(c), topo.chip(rc))]
-    return "h%d_%d" % (k, plane.index(rc))
+def plan(T, topo):
+    trs = []; land = {}; k = 0
+    for j, call in enumerate(calls()):
+        for p in call:
+            for rc in T.cores:
+                plane = [c for c in T.cores if c == rc or topo.same_plane(topo.chip(c), topo.chip(rc))]
+                for (hop, src, m, ds) in route(rc, p[4], T, topo):
+                    on = [d for d in ds if T.rank_of(d) is None]
+                    trs.append((j, p, rc, hop, src, m, ds, "h%d_%d_%d" % (k, hop, plane.index(rc)) if on else "arr%d" % p[0]))
+                    for d in on:
+                        land.setdefault(d, []).append(trs[-1])
+            k += p[4] is not None
+    for d in land:
+        land[d].sort(key=lambda x: (x[1][0], x[0] + CFG["LAG"] * x[3]))
+    return trs, land
 
 
-def landings(core, T, topo):
-    return [(p, rc, m, on[core]) for call in calls() for p in call for rc in T.cores for (m, _, on) in route(rc, p[4], T, topo) if core in on]
+def transfer(x, srcs, land, T, topo, fold=False):
+    j, (arr, reg, c0, w, way), rc, hop, src, m, ds, sem = x
+    col = reg * REG + T.rank_of(rc) * E + c0
+    at = [T.TAB[:, col:col + w] if d not in land else T.LAND[:, LW * land[d].index(x):LW * land[d].index(x) + w] for d in ds]
+    return RemoteDMATransfer(dst_ids=[dst(d, topo) for d in ds], dma_engine_mask=m, remote_sem=T.sem[sem], srcs=srcs, dsts=at, alu_op=2 if fold else 0)
 
 
 def helper_program(g, core, T, topo):
-    sent = 0
-    for k, ((arr, reg, c0, w, way), rc, m0, ds) in enumerate(landings(core, T, topo)):
-        col = reg * REG + T.rank_of(rc) * E + c0
-        off = [d for d in ds if topo.chip(d) != topo.chip(core)]; here = [d for d in ds if d not in off]
-        m = topo.mask(core, off[0]); tr = [(off, m)] + [([d], topo.mask(core, d) & ~m) for d in here]
-        g.wait_ge(T.sem[signal((arr, reg, c0, w, way), rc, T, topo)], ones(m0))
-        g.remote_dma_fused([RemoteDMATransfer(dst_ids=[dst(d, topo) for d in dd], dma_engine_mask=mm, remote_sem=T.sem["arr%d" % arr],
-                                              src=T.LAND[:, k * LW:k * LW + w], dsts=[T.TAB[:, col:col + w] for d in dd]) for (dd, mm) in tr],
-                           local_sem=T.sem.sent)
-        sent += sum(ones(mm) for (dd, mm) in tr)
+    trs, land = plan(T, topo); sent = 0
+    for k, x in enumerate(land.get(core, [])):
+        mine = [y for y in trs if y[1:3] == x[1:3] and y[4] == core and y[3] == x[3] + 1]
+        g.wait_ge(T.sem[x[7]], ones(x[5]))
+        g.remote_dma_fused([transfer(y, [T.LAND[:, k * LW:k * LW + x[1][3]]], land, T, topo) for y in mine], local_sem=T.sem.sent)
+        sent += sum(ones(y[5]) for y in mine)
     if sent:
         g.wait_ge(T.sem.sent, sent)
 
@@ -210,30 +217,26 @@ def build(g, core, T, topo, r):
             return add("G", lambda: g.iota(ap(o), pat, base, cm, allow_small_or_imprecise_dtypes=True), [], [o])
         return add("G", lambda: g.iota(ap(o), pat, base, cm), [], [o])
 
-    def setrow(o, j, v):
-        return add("G", lambda: g.affine_select(ap(o), ap(o), [[0, wd(o)]], A.not_equal, v, -j, 1), [o], [o])
+    def keep(o, i, pat, op, fill, base=0, cm=1):
+        return add("G", lambda: g.affine_select(ap(o), ap(i), pat, op, fill, base, cm), [i], [o])
 
-    sent = [0]; need = {}; todo = calls()
-    for call in todo:
-        for p in call:
-            for c in T.cores:
-                if c != core:
-                    sem = signal(p, c, T, topo) if core in route(c, p[4], T, topo)[0][1] else "arr%d" % p[0]
-                    x = need.setdefault(p[0], {}); x[sem] = x.get(sem, 0) + ones(topo.mask(c, core))
+    def setrow(o, j, v):
+        return keep(o, o, [[0, wd(o)]], A.not_equal, v, -j)
+
+    sent = [0]; need = {}; trs, land = plan(T, topo); ncall = [0]
+    for x in trs:
+        if core in x[6]:
+            n = need.setdefault(x[1][0], {}); n[x[7]] = n.get(x[7], 0) + ones(x[5])
 
     def send(fold=None):
         tr = []
-        for p in todo.pop(0):
-            arr, reg, a, w, way = p
-            to = R("TAB", reg * REG + r * E + a, w)
-            src = [to] if fold is None else [R("M1", fold + a, w), R("M2", fold + a, w)]
-            for (m, ds, on) in route(core, way, T, topo):
-                at = [R("LAND", LW * [x[:2] for x in landings(h, T, topo)].index((p, core)), w) for h in on]
-                tr.append((m, src, signal(p, core, T, topo), list(on) + ds, at + [to for d in ds])); sent[0] += ones(m)
-        o = add("G", lambda: g.remote_dma_fused(
-            [RemoteDMATransfer(dst_ids=[dst(d, topo) for d in ds], dma_engine_mask=m, remote_sem=T.sem[sem], srcs=[ap(y) for y in src],
-                               dsts=[ap(y) for y in at], alu_op=0 if fold is None else 2) for (m, src, sem, ds, at) in tr],
-            local_sem=T.sem.sent), [y for x in tr for y in x[1]], [])
+        for x in trs:
+            if x[0] == ncall[0] and x[4] == core:
+                arr, reg, a, w, way = x[1]
+                tr.append((x, [R("TAB", reg * REG + r * E + a, w)] if fold is None else [R("M1", fold + a, w), R("M2", fold + a, w)])); sent[0] += ones(x[5])
+        ncall[0] += 1
+        o = add("G", lambda: g.remote_dma_fused([transfer(x, [ap(y) for y in src], land, T, topo, fold is not None) for (x, src) in tr],
+                                                local_sem=T.sem.sent), [y for x in tr for y in x[1]], [])
         ops[o]["noinc"] = True
 
     def gather(q, o, t, off):
@@ -253,26 +256,27 @@ def build(g, core, T, topo, r):
     pi = lambda j: R("PI", j, 1)
     pf = lambda j, pn=128: R("PF", j, 1, 1, pn)
     ms(ONE, 1.0)
-    add("G", lambda: g.affine_select(ap(ID), ap(ONE), [[-1, 128]], A.is_equal, 0.0, 0, 1), [ONE], [ID])
-    iota(AN, [[3, E]], P * r, 0)
     iota(pi(0), [[0, 1]], 0, 1)
+    keep(ID, ONE, [[-1, 128]], A.is_equal, 0.0)
+    iota(AN, [[3, E]], P * r, 0)
     iota(R("COL", 0, 144), [[1, 144]], -15, 0)
-    iota(R("BI", 0, 128), [[16, 8], [0, 16]], 0, 0)
-    IH = {v: R("IH", 128 * j, 128) for j, v in enumerate([1.0, 4096.0, 1025.0, -516.5])}
+    iota(R("PC", 0, 16), [[128, 2], [2, 8]], 0, 0)
+    IH = {v: R("IH", 128 * j, 128) for j, v in enumerate([1.0, 4096.0, 1025.0])}
     for v in IH:
         act(IH[v], ID, F.Identity, scale=v)
     AP_ = [R("P0", 0, E), R("P0", 256, E), R("P1", 0, E)]
     for s in range(3):
         aff("S", AP_[s], AN, 1.0, float(s))
-    vw = lambda j, a=0, w=9: R("VW", 10 * j + a, w)
-    ms(R("VW", 0, 90), 0.0); ms(R("COFF", 0, 16 * RO), 0)
-    for j in range(3):
-        ms(R("SLOT", 384 * j + 64, 64), 0.0)
+    vw = lambda j: R("VW", 8 - j, 9)
+    VT, VX = R("VW", 20, 9), R("VW", 30, 9, 1, 2)
+    ZM, ZB, TH, ZN, ZC, TN = [R("ZM", 128 * j, 128) for j in range(6)]
+    ms(R("VW", 0, 40), 0.0); ms(R("SLOT", 0, 32), 0.0); ms(R("SLOT", 32 + E, 32), 0.0)
+    ts(pi(1), pi(0), -16, A.bitwise_and); ts(pi(3), pi(0), 7, A.bitwise_and); ts(pi(4), pi(0), 1, A.bitwise_and)
     ts(IN, ID, 6080.0, A.mult); ts(I25, ID, 1024 * SHIFT, A.mult)
-    ms(vw(0, 0, 1), 2.0); ms(vw(6, 0, 1), -1.5); ms(vw(6, 1, 5), -0.5)
+    ts(pi(5), pi(0), 4, A.logical_shift_right, 1, A.bitwise_and); ts(pi(6), pi(0), 3, A.logical_shift_right, 1, A.bitwise_and)
+    ms(R("VW", 7, 1), -1.0); ms(R("VW", 8, 1), 1.0); ms(R("VW", 36, 2), 1.0); cp(pf(0), pi(1))
     ms(R("SEL", 128 * RO, 128), U10); ms(R("SELB", 128 * RO, 128), -SHIFT / 2)
-    for j in range(1, 4):
-        ms(vw(j, j, 1), 2.0 / 4 ** j); ms(vw(j, j - 1, 1), -2.0 / 4 ** (j - 1))
+    ms(ZM, -1.0 / 32); ms(ZB, -2.0 ** 75); ms(TH, 0.0); ms(pf(8), 1.0)
 
     def names(zi, c, w):
         name("ni"); aff("S", R("NI", c, w), zi, 1.0 / 64, -31.5 / 64)
@@ -287,91 +291,66 @@ def build(g, core, T, topo, r):
 
     def prep(t, f1):
         s = t % 3; c = s * E
-        n = R("NI", c, E); sl = R("SLOT", 384 * s + 128, E); f2, f3 = R("F2", 0, E), R("F3", 0, E)
+        n = R("NI", c, E); f2 = R("F2", 0, E)
         name("q1"); aff("S", R("Q1", 0, E), n, 1.0 / 3, -1.0 / 3)
-        name("f1"); aff("S", f1, n, float(REG), -float(REG * s))
-        name("f2"); aff("S", f2, R("Q1", 0, E), 1.0 - 3 * REG, 0.0)
-        if s == 0:
-            name("sl"); tt(sl, f1, f2, A.add)
-        else:
-            name("f3"); tt(f3, f1, f2, A.add)
-            name("f4"); act(f2, f3, F.Sign, bias=0.5)
-            name("f5"); aff("S", f1, f2, -1.5 * REG, 1.5 * REG)
-            name("sl"); tt(sl, f3, f1, A.add)
-        name("off"); cp(R("OFF", t * E, E), sl)
+        name("q2"); aff("S", R("Q1", E, E), n, 1.0 / 3, (2.0 - s) / 3)
+        name("f1"); aff("S", f1, n, float(REG), float(REG * (3 - s)))
+        name("f2"); aff("S", f2, R("Q1", E, E), -3.0 * REG, 0.0)
+        name("f3"); tt(f1, f1, f2, A.add)
+        name("sl"); tt(R("SLOT", 32, E), f1, R("Q1", 0, E), A.add)
 
-    def wrap(t, bank):
-        m = 16 * (t + 1)
-        for h4 in range(0, 16, 4):
-            name("wr%d" % (h4 // 4))
-            mm([(R(bank, 496 + h, 1, 1, m), R("SLOT", 384 * (t % 3) + 128 + 16 * h - 16 * t, m), R("ID", 17 * t, 1), True, True)
-                for h in range(h4, h4 + 4)])
-        name("co"); cp(R("COFF", 16 * t, 16, 1, m), R(bank, 496, 16, 1, m))
+    def wrap(t):
+        for (n, o, i) in (("ta", R("TT", 0, E), R("SLOT", 32, E)), ("tb", R("TT", E, E + 32), R("SLOT", 16, E + 32))):
+            name(n); add("V", lambda o=o, i=i: g.vector.transpose(ap(o), ap(i)), [i], [o])
+        o, win, off = R("OFF", t * E, E), R("TT", 0, 2 * E + 32), R("PERM", 0, 16)
+        name("off"); add("V", lambda: g.vector.tensor_copy(ap(o), ap(win).indirect(ap(off))), [win, off], [o])
 
     def select(t):
         for n in ("SEL", "SELB"):
             o, i = R(n, 128 * t, 128), R(n, 128 * RO, 128)
             add("G", lambda o=o, i=i: g.affine_select(ap(o), ap(i), [[0, 128]], A.is_equal, 0.0, -17 * t - 3, 1), [i], [o])
 
-    have = set(); pend = []; waiting = [[(p[0], p[1] + j) for p in call for j in range(p[2])] for call in C["START"]]
-    for j, (s, c0, w) in enumerate(C["ENC"]):
+    have = set(); waiting = [[(p[0], p[1] + j) for p in call for j in range(p[2])] for call in C["START"]]
+    for step in C["PIPE"].split():
+        j = int(step[1]); s, c0, w = C["ENC"][j]
         c = s * E + c0; zi = R("Z", 3 * c0 + s, w, 3); b1 = R("P%d" % (2 + j % 6), 0, w)
-        names(zi, c, w)
-        aff("S", R("NP", c, w), R("NI", c, w), 1.0, -2304.0)
-        tt(R("EQ", c, w), R("NI", c, w), R(AP_[s][0], AP_[s][1] + c0, w), A.is_equal)
-        aff("S" if j else "V", R("MF", c, w), R("I1", c, w), 31.0, -CEN)
-        mm([(b1, IN, R("NP", c, w), True, False)])
-        mm([(b1, I25, R("EQ", c, w), False, False), (b1, IH[1.0], R("MF", c, w), False, True)])
-
-        def fin(s=s, c0=c0, w=w, zi=zi, b1=b1):
+        if step[0] == "a":
+            names(zi, c, w)
+        elif step[0] == "b":
+            aff("S", R("NP", c, w), R("NI", c, w), 1.0, -2304.0)
+            tt(R("EQ", c, w), R("NI", c, w), R(AP_[s][0], AP_[s][1] + c0, w), A.is_equal)
+            aff("S" if j else "V", R("MF", c, w), R("I1", c, w), 31.0, -CEN)
+            mm([(b1, IN, R("NP", c, w), True, False)])
+            mm([(b1, I25, R("EQ", c, w), False, False), (b1, IH[1.0], R("MF", c, w), False, True)])
+        else:
             tt(R("TAB", s * REG + r * E + c0, w), zi, b1, A.add)
             have.update((s, c0 + i) for i in range(w))
             while waiting and all(x in have for x in waiting[0]):
                 waiting.pop(0); send()
-        pend.append(fin)
-        if len(pend) > 1:
-            pend.pop(0)()
-    for f in pend:
-        f()
 
     name(""); now[0] = -0.5
-    for j in range(4, 6):
-        ms(vw(j, j, 1), 2.0 / 4 ** j); ms(vw(j, j - 1, 1), -2.0 / 4 ** (j - 1))
-    ts(pi(1), pi(0), -16, A.bitwise_and); cp(pf(0), pi(1)); cp(pf(1), pi(0))
-    ts(R("WB", 0, 144), R("COL", 0, 144), pf(0), A.is_equal, 1024.0, A.mult)
+    tt(pf(10), pi(4), pi(5), A.not_equal); ts(pf(11), pi(3), 16.0, A.mult); ts(pf(12), pf(10), E + 16.0, A.mult, pf(11), A.add)
+    tt(pf(13), pf(12), pi(6), A.add); ts(R("PERM", 0, 16), R("PC", 0, 16), pf(13), A.add)
     select(0)
-    prep(0, R("P1", 256, E)); wrap(0, "P7"); split(R("Z", 0, E, 3), 0, R("P2", 256, E))
-    ts(pi(3), pi(0), 7, A.bitwise_and); ts(pi(4), pi(0), 1, A.bitwise_and)
+    prep(0, R("P1", 256, E)); wrap(0); split(R("Z", 0, E, 3), 0, R("P2", 256, E))
+    ts(R("WB", 0, 144), R("COL", 0, 144), pf(0), A.is_equal, 1024.0, A.mult)
     ts(pf(2), pi(3), 2 * LN2, A.mult, -11 * LN2, A.add)
-    ts(pf(3), pi(4), 10 * LN2, A.mult, 10 * LN2, A.add); tt(pf(4), pf(2), pf(3), A.add)
-    ts(pf(5), pi(3), 3.0, A.is_ge, -5 * LN2, A.mult); ts(pf(6), pf(5), 10 * LN2, A.add); tt(pf(7), pf(2), pf(6), A.add)
-    WX, WE, WR = R("WS", 0, 128, 1, 8), R("WS", 128, 128, 1, 8), R("WS", 256, 128, 1, 8)
-    for wv, c in ((WX, 4), (WE, 2), (WR, 7)):
-        act(wv, R("ONE", 0, 128, 1, 8), F.Exp, scale=pf(c, 8))
-    setrow(WE, 6, (682.5 - CEN) / 1024); setrow(WR, 6, 31.5)
-    WX, WE, WR = R("WS", 0, 128, 1, 6), R("WS", 128, 128, 1, 7), R("WS", 256, 128, 1, 7)
-    BL = [R("BLK", 128 * j, 128) for j in range(4)]
-    ZM, ZN, ZB, ZC, TH, TN = [R("ZM", 128 * j, 128) for j in range(6)]
-    ts(BL[0], R("BI", 0, 128), pf(0), A.is_equal)
-    ts(BL[1], R("COL", 15, 128), pf(1), A.is_gt, -63.0 / 32, A.mult); aff("S", BL[1], BL[1], 1.0, -1.0 / 32)
-    tt(BL[1], BL[1], BL[0], A.mult); aff("S", BL[2], ID, 33.0 / 32, 0.0); tt(ZM, BL[1], BL[2], A.add)
-    act(ZN, ZM, F.Identity, scale=-1.0)
-    aff("S", BL[3], BL[0], -0.5, 0.0); tt(BL[3], BL[3], ID, A.add)
-    act(ZB, BL[3], F.Identity, scale=2.0 ** 76); act(ZC, BL[3], F.Identity, scale=-2.0 ** 76)
-    ts(pf(9), pi(3), 6.0, A.is_equal, 2.0 ** 28, A.mult)
-    act(TN[:4] + (8,), R("ONE", 0, 128, 1, 8), F.Identity, scale=pf(9, 8)); act(TH[:4] + (8,), TN[:4] + (8,), F.Identity, scale=-1.0)
-    TH, TN = TH[:4] + (7,), TN[:4] + (7,)
-    KP, KN = R("KS", 0, 128, 1, 9), R("KS", 128, 128, 1, 9)
-    tt(pf(15), R("ID", 8, 1), R("ID", 7, 1), A.subtract); ts(pf(16), pf(15), 2.0 ** 77, A.mult)
-    act(KP, R("ONE", 0, 128, 1, 9), F.Identity, scale=pf(16, 9)); act(KN, KP, F.Identity, scale=-1.0)
-    aff("S", R("IOT", 0, E), AN, 1.0, -P * r - 384.0); ms(vw(7, 7, 2), 1.0); ms(vw(8, 7, 2), -1.0)
-    WK = R("WS", 384, 128, 1, 7); act(WK, WE, F.Identity, scale=1024.0)
-    KJ = [256.0 / 4 ** j * (RC[j] - RC[j + 1]) + (192.0 if j == 0 else 64.0) for j in range(6)]
-    ms(pf(8), -KJ[2] - 0.5)
-    for j in (0, 1, 5):
-        setrow(pf(8), j, -KJ[j] - 0.5)
-    setrow(pf(8), 6, 1.0); setrow(pf(8), 7, 0.5); setrow(pf(8), 8, -0.5)
-    prep(1, R("P3", 256, E)); split(R("Z", 1, E, 3), 1, R("P4", 256, E))
+    ts(pf(3), pi(4), 10 * LN2, A.mult, pf(2), A.add); ts(pf(5), pi(3), 3.0, A.is_ge, -5 * LN2, A.mult); tt(pf(7), pf(2), pf(5), A.add)
+    WX, WK, WR = R("WS", 0, 128, 1, 6), R("WS", 128, 128, 1, 9), R("WS", 256, 128, 1, 9)
+    ms(R("WS", 128, 256, 1, 9), 0.0); setrow(WK, 8, 682.5 - CEN); setrow(WR, 8, 31.5)
+    for wv, c in ((WX, 3), (WK, 2), (WR, 7)):
+        act(wv[:4] + (6,), R("ONE", 0, 128, 1, 6), F.Exp, scale=pf(c, 6), bias=10 * LN2)
+    act(R("VW", 20, 6), R("COL", 15, 6), F.Exp, scale=2 * LN2, bias=-2 * LN2); ms(R("VW", 21, 1), 5.0)
+    keep(ZM, ZM, [[-1, 128]], A.is_ge, -2.0); keep(ZM, ZM, [[-1, 128]], A.not_equal, 1.0); keep(ZB, ZB, [[-1, 128]], A.not_equal, 2.0 ** 75)
+    both = R("ZM", 0, 256)
+    keep(both, both, [[0, 2], [-16, 8], [0, 16]], A.is_ge, 0.0); keep(both, both, [[0, 2], [16, 8], [0, 16]], A.is_ge, 0.0, 15, -1)
+    setrow(TH, 6, -2.0 ** 77); setrow(TH, 7, 2.0 ** 77); setrow(TH, 8, -2.0 ** 28); setrow(R("VW", 36, 2), 1, -1.0)
+    act(R("ZM", 384, 384), R("ZM", 0, 384), F.Identity, scale=-1.0)
+    TH, TN = TH[:4] + (9,), TN[:4] + (9,)
+    aff("S", R("SP", 0, E), AN, 1.0, -P * r - 384.0)
+    for j in range(6):
+        setrow(pf(8), j, -128.0 * (RC[j] - RC[j + 1]) - (640.0 if j == 1 else 32.0 * 4 ** j) - 4 ** j / 4.0)
+    setrow(pf(8), 6, 0.5); setrow(pf(8), 7, -0.5)
     aff("S", R("RAW", 0, P), R("Z", 0, P), 1.0, 0.0)
 
     for t in range(RO):
@@ -379,85 +358,87 @@ def build(g, core, T, topo, r):
         sel, selb = R("SEL", 128 * t, 128), R("SELB", 128 * t, 128)
         if not last:
             name("sel"); select(t + 1)
+            zi = R("Z", t + 1, E, 3) if t < 2 else R("ZI", 0, E)
+            if t >= 2:
+                name("zi"); aff("S", zi, R("RAW", t - 2, E, 3), 1.0, 0.0)
+                names(zi, E * (t - 2), E)
+            split(zi, (t + 1) % 3, R("P0", E, E)); prep(t + 1, R("P0", E, E)); wrap(t + 1)
         for h, (i0, w) in enumerate(C["VB"]):
-            name("vb%d" % h); gather("B", R("VB", i0, w), t, R("COFF", 16 * t + i0 // 16, w // 16))
+            name("vb%d" % h); gather("B", R("VB", i0, w), t, R("OFF", t * E + i0 + t * w // 16, w // 16))
             name("fl%d" % h); ts(R("FL", i0, w), R("VB", i0, w), 1.0, A.min, -1.0, A.max)
         a = 0
         for j, (q, n) in enumerate(C["GATH"]):
             name("g%d" % j); gather(q, R("G", 16 * a, 16 * n), t, R("OFF", t * E + a, n)); a += n
-        late = []
+        late = []; sends = [max(a + n for (a, n, way) in call) for call in C["SEND"]]
+        for h, (i0, w) in enumerate(C["HALVES"]):
+            X = lambda n, pn=128, i0=i0, w=w: R(n, i0, w, 1, pn)
+            rep = C["REP"][h]; B = R("P%d" % h, 0, w)
+            for j in range(rep - 1, -1, -1):
+                name("b%d%d" % (h, j)); mm([(R("P%d" % h, j * w, w), sel, X("VB"), True, False)])
+                name("B%d%d" % (h, j)); mm([(R("P%d" % h, j * w, w), selb, X("FL"), False, True)])
+            name("own%d" % h); tt(X("OWN"), R("NE", s * E + i0, w), B, A.is_equal)
+            name("tb%d" % h); aff("S", X("TB"), B, 32.0 / 3, 64.0 * HALF)
+            name("sx%d" % h); aff("S", X("SP", 1), B[:4] + (1,), 1.0 / 6, HALF - P * r - s - 384.0)
+            if not last:
+                name("na%d" % h); aff("S", X("NV"), B, 1024.0, 0.0)
+            k = 0
+            for n in C["SUB"][h]:
+                name("d%d%x" % (h, k)); tt(R("D", 16 * i0 + k * w, w * n), R("G", 16 * i0 + k * w, w * n), R("P%d" % h, 0, w * n), A.subtract)
+                k += n
+            for k0, k1 in zip(C["KCUT"][h], C["KCUT"][h][1:]):
+                d4 = R("D", 16 * i0 + k0 * w, (k1 - k0) * w)
+                name("c%d%x" % (h, k0)); ts(d4, d4, HI, A.min, LO, A.max)
         for c, (i0, w) in enumerate(C["PARTS"]):
-            pa, pb, pc = "P%d" % c, "P%d" % (2 + 2 * c), "P%d" % (3 + 2 * c)
+            h0, hw = [x for x in C["HALVES"] if x[0] <= i0][-1]
+            pb, pc = "P%d" % (2 + 2 * c), "P%d" % (3 + 2 * c)
             X = lambda n, pn=128, i0=i0, w=w: R(n, i0, w, 1, pn)
             nm = lambda n, c=c: name("%s%d" % (n, c))
             nk = lambda n, k, c=c: name("%s%d%x" % (n, c, k))
             S1, XP, ZP = [R(pb, w * j, w) for j in range(3)]
             BQ, WO, ZQ = [R(pc, w * j, w) for j in range(3)]
             VO = BQ[:4] + (9,); RB = S1; NB = BQ
-            for n, bank in C["OWNBANK"][c].items():
+            for n, (bank, a) in C["OWNBANK"][c].items():
                 if n == "ZP":
-                    ZP = R(bank, 0, w)
-                elif n == "ZQ":
-                    ZQ, BQ, RB = [R(bank, w * j, w) for j in range(3)]
+                    ZP = R(bank, a, w)
                 else:
-                    NB = R(bank, 0, w)
-            rep = C["REP"][c]; B = R(pa, 0, w, rep); qs = C["PLACE"][c]
-            for j in range(rep - 1, -1, -1):
-                nk("b", j); mm([(R(pa, j, w, rep), sel, X("VB"), True, False)])
-                nk("B", j); mm([(R(pa, j, w, rep), selb, X("FL"), False, True)])
-            nm("own"); tt(X("OWN"), R("NE", s * E + i0, w), B, A.is_equal)
-            nm("tb"); aff("S", X("TB"), B, 32.0 / 3, 64.0 * HALF)
+                    ZQ, BQ, RB = [R(bank, a + w * j, w) for j in range(3)]
+            qs = C["PLACEL" if last else "PLACE"][c]
             nm("sk"); mm([(S1, IH[1.0], R("SK", s * E + i0, w), True, False)])
-            k = 0; rows = []; free = list(range(16))
-            for n in C["SUB"][c]:
-                q = free[0]; mine = [q + 16 // n * j for j in range(n)]; free = [x for x in free if x not in mine]
-                nk("d", k); tt(R("D", 16 * i0 + k * w, w * n), R("G", 16 * i0 + q, w * n, 16 // n), R(pa, 0, w * n, rep // n), A.subtract)
-                rows += [(x, R("D", 16 * i0 + k * w + j, w, n)) for j, x in enumerate(mine)]; k += n
-            for k0, k1 in zip(C["KCUT"][c], C["KCUT"][c][1:]):
-                d4 = R("D", 16 * i0 + k0 * w, (k1 - k0) * w)
-                nk("c", k0); ts(d4, d4, HI, A.min, LO, A.max)
             for k0 in range(0, 16, C["MMN"]):
-                if k0 == 8:
+                if k0 == C["SO"][c]:
                     nm("so"); mm([(S1, IH[4096.0], X("OWN"), False, False)])
-                nk("m", k0); mm([(S1, R("WB", 15 - rows[k][0], 128), rows[k][1], False, k == 15) for k in range(k0, k0 + C["MMN"])])
-            nm("sx"); aff("S", X("SP", 1), B[:4] + (1,), 1.0 / 6, HALF - P * r - s - 384.0)
-            nm("x"); mm([(VO, vw(7)[:4] + (1,), X("SP", 1), True, False), (VO, vw(8)[:4] + (1,), X("IOT", 1), False, False)])
+                nk("m", k0); mm([(S1, R("WB", 15 - k, 128), R("D", 16 * h0 + k * hw + i0 - h0, w), False, k == 15) for k in range(k0, k0 + C["MMN"])])
+            nm("x"); mm([(VO, VX, X("SP", 2), True, False)])
             nm("si"); aff(qs[0], X("SI"), S1, 1.0, 16 * 4780.0 + CEN)
             nm("u"); ts(X("U"), X("SI"), 0x1555, A.bitwise_and)
             nm("w")
             if qs[1] == "S":
-                act(X("W"), X("U"), F.Relu, bias=-4095.0)
+                act(X("W"), X("U"), F.Relu, bias=-4088.0)
             else:
-                ts(X("W"), X("U"), 4095.0, A.subtract, 0.0, A.max)
-            nm("te"); act(X("TES"), X("U"), F.Sign, bias=-4095.5)
+                ts(X("W"), X("U"), 4088.0, A.subtract, 0.0, A.max)
+            nm("te"); act(X("TES"), X("U"), F.Sign, bias=4095.5, scale=-1.0)
             for j in range(1, 6):
-                nm("r%d" % j); aff(qs[1 + j], X("R%d" % j), X("W"), 1.0, RC[j] - 0.5)
-            nm("va"); mm([(VO, vw(6), X("TES"), False, False), (VO, vw(0), X("W"), False, False)])
+                nm("r%d" % j); aff(qs[1 + j], X("R%d" % j), X("W"), 1.0, RC[j] + (-6.5 if j == 2 else 0.5))
+            nm("va"); mm([(VO, VT, X("TES"), False, False), (VO, vw(0), X("W"), False, False)])
             for j, js in enumerate(C["VO"][c]):
                 nm("v" + "efg"[j]); mm([(VO, vw(i), X("R%d" % i), False, i == C["VO"][c][-1][-1]) for i in js])
-            nm("xa"); mm([(XP, IH[1025.0], X("W"), True, False), (XP, IH[-516.5], X("TES"), False, False)])
+            nm("xa"); mm([(XP, IH[1025.0], X("W"), True, False)])
             nm("sg"); act(X("SG", 9), VO, F.Sign, bias=pf(8, 9))
             nm("xb"); mm([(XP, WX, X("SG", 6), False, True)])
-            nm("sj"); aff(qs[7], X("SJ"), XP, 1.0, 0x111111 / 2.0 + 8 - 516.5)
+            nm("sj"); aff(qs[7], X("SJ"), XP, 1.0, 0x111111 / 2.0)
             if not last:
-                if C["NV"][c] == "V":
-                    nm("na"); aff("S", X("NV"), B, 1024.0, 0.0)
-                    nm("nb"); mm([(NB, WK, X("SG", 7), True, True)])
-                    nm("nv"); tt(X("NV"), X("NV"), NB, A.add)
-                else:
-                    nm("na"); mm([(NB, sel, X("VB"), True, False), (NB, selb, X("FL"), False, False)])
-                    nm("nb"); mm([(NB, WE, X("SG", 7), False, True)])
-                    nm("nv"); aff("S", X("NV"), NB, 1024.0, 0.0)
-            nm("wo"); mm([(WO, WR, X("SG", 7), True, True)])
+                nm("nb"); mm([(NB, WK, X("SG", 9), True, True)])
+                nm("nv"); tt(X("NV"), X("NV"), NB, A.add)
             if last:
+                nm("nb"); mm([(WO, WR, X("SG", 9), True, True)])
                 nm("nv"); tt(X("DR"), X("TB"), WO, A.add)
-            for (zz, zb, th, ks, n) in ((ZQ, ZC, TN, KN, "q"), (ZP, ZB, TH, KP, "p")):
+            for (zz, zb, th, n) in ((ZQ, ZC, TN, "q"), (ZP, ZB, TH, "p")):
                 nm(n + "a"); mm([(zz, zb, X("OWN"), True, False)])
-                nm(n + "t"); mm([(zz, ks, X("SG", 9), False, False), (zz, th, X("SG", 7), False, False)])
+                nm(n + "t"); mm([(zz, th, X("SG", 9), False, False)])
             nm("uj"); ts(X("UJ"), X("SJ"), 0x111119, A.bitwise_and)
-            nm("sm"); aff(qs[8], X("SJ"), X("UJ"), 0x111111 / 2.0 ** 20, 1.5 * 2 ** 23 + 8)
+            nm("sm"); aff(qs[8], X("SJ"), X("UJ"), 0x111111 / 2.0 ** 20, 1.5 * 2 ** 23)
             nm("uk"); ts(X("UJ"), X("SJ"), 15, A.bitwise_and)
-            nm("ex"); act(X("EX"), X("UJ"), F.Exp, bias=-18 * LN2, scale=6 * LN2)
+            nm("ex"); act(X("EX"), X("UJ"), F.Exp, bias=-24 * LN2, scale=6 * LN2)
             nm("pb"); mm([(ZP, ZM, X("EX"), False, True)])
             nm("qb"); mm([(ZQ, ZN, X("EX"), False, True)])
             raw = R("RAW", 3 * i0 + s, w, 3)
@@ -466,9 +447,11 @@ def build(g, core, T, topo, r):
                 nm("mi"); tt(m1, X("NV"), ZP, A.min)
                 nm("bq"); tt(m2, R("TAB", t * REG + r * E + i0, w), ZQ, A.min)
                 nm("mx"); tt(R("TAB", (t + 3) * REG + r * E + i0, w), m1, m2, A.max)
-                nm("send"); send(t * E if C["FOLD"][c] else None)
+                if i0 + w in sends:
+                    name("send%d" % sends.index(i0 + w)); send(t * E if C["FOLD"][c] else None)
 
                 def plain(X=X, nm=nm, WO=WO, ZP=ZP, ZQ=ZQ, RB=RB, raw=raw):
+                    nm("wo"); mm([(WO, WR, X("SG", 9), True, True)])
                     nm("dr"); tt(X("DR"), X("TB"), WO, A.add)
                     nm("ds"); tt(X("DR"), X("DR"), ZP, A.min)
                     nm("rb"); tt(RB, raw, ZQ, A.min)
@@ -478,21 +461,12 @@ def build(g, core, T, topo, r):
                 nm("mi"); tt(X("DR"), X("DR"), ZP, A.min)
                 nm("bq"); tt(BQ, raw, ZQ, A.min)
                 nm("mx"); tt(raw, X("DR"), BQ, A.max)
-                nm("send")
-                o = add("Y", lambda i0=i0, w=w: g.sync.dma_start(T.yk[:, 3 * i0:3 * (i0 + w)], T.RAW[:, 3 * i0:3 * (i0 + w)]), [R("RAW", 3 * i0, 3 * w)], [])
-                ops[o]["dma"] = "st%d" % c
+                if i0 + w in sends:
+                    j = sends.index(i0 + w); a, b = 3 * ([0] + sends)[j], 3 * (i0 + w); name("send%d" % j)
+                    o = add("Y", lambda a=a, b=b: g.sync.dma_start(T.yk[:, a:b], T.RAW[:, a:b]), [R("RAW", a, b - a)], [])
+                    ops[o]["dma"] = "st%d" % j
         for f in late:
             f()
-        if t in (0, 1):
-            name("zi"); aff("S", R("ZI", E * t, E), R("RAW", t, E, 3), 1.0, 0.0)
-        if t in (1, 2):
-            names(R("ZI", E * (t - 1), E), E * (t - 1), E)
-        if t <= 2:
-            prep(t + 2, R("P1", 128, E))
-        if t <= 3:
-            wrap(t + 1, "P0")
-        if t in (0, 2, 3):
-            split(R("ZI", E * (t - 2), E) if t else R("Z", 2, E, 3), (t + 1) % 3 if t else 2, R("P0", 128, E))
     return ops, sent[0]
 
 
@@ -516,13 +490,13 @@ def depend(ops):
 
 
 def order(ops, deps, names):
-    at = {n: k for k, n in enumerate(names)}
-    key = [(o["t"], at.get(o["name"], len(names)) if o["t"] >= 0 else 0, i) for i, o in enumerate(ops)]
-    left = [i for i, o in enumerate(ops) if -1 < o["t"] < 0]; end = {}; free = {}
+    at = [{n: k for k, n in enumerate(x)} for x in names]
+    key = [(o["t"], at[o["t"]][o["name"]] if o["t"] >= 0 else 0, i) for i, o in enumerate(ops)]
+    left = [i for i, o in enumerate(ops) if -1 < o["t"] < 0]; end = {}; free = {"G": 1500, "V": 600}
     while left:
         can = [(max([free.get(ops[i]["q"], 0)] + [end.get(j, 0) + 100 for j in deps[i]]), i) for i in left if not deps[i] & set(left)]
         s, i = min(can); x = ops[i]["wr"][0]; left.remove(i); key[i] = (-0.5, s, i)
-        end[i] = free[ops[i]["q"]] = s + (600 if ops[i]["q"] == "P" else 60 + max(64, (x[2] - x[1]) // x[3]) * (2 if ops[i]["q"] == "G" else 1))
+        end[i] = free[ops[i]["q"]] = s + (200 + 2 * (x[2] - x[1]) if ops[i]["q"] == "G" else 60 + max(64, (x[2] - x[1]) // x[3]))
     seq = []; seen = set()
 
     def put(i):
@@ -547,7 +521,7 @@ def rank_program(g, core, T, topo):
     if r is None:
         return helper_program(g, core, T, topo)
     ops, sent = build(g, core, T, topo, r)
-    seq, deps = order(ops, depend(ops), CFG["ORDER"].split())
+    seq, deps = order(ops, depend(ops), [CFG["ORDER"].split()] * (RO - 1) + [CFG["LAST"].split()])
     Q = {"V": g.vector, "S": g.scalar, "P": g.tensor, "G": g, "Y": g.sync}
     used = set(); place = {i: k for k, i in enumerate(seq)}
     for i in seq:

import math
from concourse.bass import DstId, RemoteDMATransfer
from concourse.mybir import AluOpType as A, ActivationFunctionType as F

P, E, RO, NR = 768, 256, 5, 6
REG = NR * E
HALF = 2280
CEN = 684.0
U10 = 1.0 / 1024
HI, LO = 3412.0 * U10, -4780.0 * U10
SHIFT = 32768.0
LN2 = math.log(2.0)
RC = [0, 4096.0, 2064.0, 8192.0, 32768.0, 131072.0, 0.0]
NH, LW = 24, 160
FAR0, FAR1, NEAR0, NEAR1 = ("far", 0), ("far", 1), ("near", 0), ("near", 1)
CFG = {
    "LOAD": [0, 384, 768],
    "ENC": [(0, 0, 128), (1, 0, 128), (2, 0, 128), (0, 128, 128), (1, 128, 128), (2, 128, 128)],
    "START": [[(0, 0, 128, ("fwd", "nf"))], [(1, 0, 128, FAR0 + ("in",)), (2, 0, 128, ("fwd", "nf"))],
              [(0, 128, 128, FAR1 + ("in",)), (1, 128, 128, None)], [(2, 128, 128, NEAR0 + ("in",))]],
    "LAG": 2.5, "PIPE": "a0 a1 b0 a2 b1 a3 c0 b2 a4 c1 b3 a5 c2 b4 b5 c3 c4 c5",
    "TURN": [1, 2, 3, 4, 5],
    "PARTS": [(0, 128), (128, 64), (192, 64)],
    "SEND": [[(0, 64, ("fwd", "nf")), (64, 64, FAR0 + ("in",))], [(128, 128, None)]], "FOLD": [0, 0, 0],
    "VB": [(0, 128), (128, 128)],
    "GATH": [("S", 32), ("V", 24), ("S", 40), ("S", 32), ("S", 32), ("S", 32), ("S", 32), ("S", 16), ("S", 16)],
    "REP": [2, 4],
    "SUB": [[2] * 8, [4, 4, 4, 2, 2]],
    "KCUT": [[0, 4, 10, 14, 16], [0, 4, 8, 12, 14, 16]], "MMN": 2, "SO": [4, 0, 0],
    "VO": [[(1, 2), (3, 4), (5,)], [(1, 3), (2, 5), (4,)], [(1, 3), (2, 5), (4,)]],
    "HALVES": [(0, 128), (128, 128)],
    "OWNBANK": [{}, {}, {}],
    "PLACE": ['SSVSSSSSV', 'VVVSSVVSS', 'VVVSVSVVS'],
    "ORDER": """sel vb0 vb1 fl0 g1 fl1 b01 B01 b00 B00 g0 g2 d00 d02 d04 d06 d08 d0a g3 g4 g5 own0 c00 c04 b13 sk1 B13 b12 sk0 sk2 B12 b11 B11 b10 B10 m00 m02 so0 m04 m06 d0c d0e own1 c0e c0a so1 m08 m0a m0c m0e so2 d10 d14 c10 c14 g6 g8 si0 sx0 g7 na0 u0 w0 te0 d18 d1e r10 c18 d1c r20 r40 r30 r50 tb0 zi m20 m10 x0 m22 m24 m26 m12 m14 m16 xa0 va0 ve0 c1e c1c i2 m18 m28 m2a vf0 vg0 m1a m2c m2e m1c m1e si2 si1 u2 u1 w2 w1 sx1 sg0 xb0 ni na1 pa0 x1 x2 nb0 xa1 sj0 te2 te1 r31 r21 r42 tb1 r22 q1 r12 r51 r11 r32 uj0 r41 r52 va2 va1 ve2 ve1 vf1 vg1 sm0 nv0 uk0 i1 vf2 vg2 sg1 xa2 pt0 qa0 xb1 sg2 ex0 xb2 sj2 sj1 uj1 nb1 qt0 pb0 qb0 qa1 q2 sm1 uj2 mi0 bq0 sm2 mf uk1 ex1 mx0 uk2 nb2 pa2 pa1 pt2 pt1 qa2 qt1 nv2 nv1 skm ex2 ne f1 f2 wo0 pb1 qt2 qb1 wo1 pb2 qb2 wo2 mi1 bq1 mi2 bq2 mx1 mx2 send0 send1 rb2 dr1 f3 dr2 rb1 sl ds2 dr0 ds1 ds0 rw1 rb0 ta rw0 tb rw2 off""",
    "PLACEL": ['SSSSSSSSS', 'SVVVVVSVV', 'VSSSVVSVS'],
    "LAST": """vb0 vb1 fl0 fl1 g1 g0 g2 g4 g3 g5 g6 b01 B01 b00 B00 sk0 b13 B13 b12 B12 b11 B11 b10 B10 sk2 d00 d02 d0a d08 d04 c00 own0 d06 own1 d0c c04 d0e c0a d10 c0e m00 m02 so0 m04 so2 m06 sk1 m08 m0a so1 m0c m0e c10 d14 sx0 g7 m10 x0 m20 m22 m12 si0 g8 u0 c14 w0 te0 d18 d1c c18 d1e c1c c1e r20 r10 r40 r30 m14 m24 va0 m26 m16 ve0 vf0 r50 m28 vg0 m18 m1a xa0 tb0 sg0 sx1 m1c m1e xb0 m2a m2c m2e si1 u1 si2 w1 u2 sj0 te1 r51 w2 te2 r52 r12 r22 r11 r31 r21 r41 uj0 r32 r42 sm0 uk0 pa0 x1 x2 nb0 qa0 qt0 va1 ve1 vf1 xa1 vg1 va2 ve2 vf2 vg2 sg1 xb1 tb1 sg2 ex0 sj1 nv0 uj1 nb1 xa2 qa1 xb2 pt0 pb0 qt1 pa1 nb2 pt1 qb0 qa2 qt2 sj2 sm1 uj2 sm2 uk1 mi0 nv1 ex1 uk2 ex2 bq0 nv2 qb1 pa2 pt2 pb1 qb2 pb2 mx0 bq1 bq2 mi2 mi1 mx2 mx1 send0 send1""",
}

SCRATCH = {
    "TAB": ("sbuf", [128, 7 * REG], "float32"), "Z": ("sbuf", [128, P], "int32"), "RAW": ("sbuf", [128, P], "float32"),
    "G": ("sbuf", [128, 16 * E], "float32"), "D": ("sbuf", [128, 16 * E], "float16"),
    "NE": ("sbuf", [128, P], "float32"), "SK": ("sbuf", [128, P], "float16"),
    "NI": ("sbuf", [128, P], "int32"), "OFF": ("sbuf", [128, RO * E], "uint16"), "PERM": ("sbuf", [128, 16], "uint16"),
    "TT": ("sbuf", [128, 2 * E + 32], "float32"), "PC": ("sbuf", [128, 16], "float32"),
    "SEL": ("sbuf", [128, (RO + 1) * 128], "float32"), "SELB": ("sbuf", [128, (RO + 1) * 128], "bfloat16"),
    "SP": ("sbuf", [128, E], "float16"),
    "SLOT": ("sbuf", [128, E + 64], "float32"), "ZI": ("sbuf", [128, 2 * E], "int32"), "AN": ("sbuf", [128, E], "float32"),
    "I1": ("sbuf", [128, P], "int32"), "I2": ("sbuf", [128, P], "int32"), "EQ": ("sbuf", [128, P], "bfloat16"),
    "MF": ("sbuf", [128, P], "float16"), "NP": ("sbuf", [128, P], "float32"),
    "Q1": ("sbuf", [128, 2 * E], "int32"), "F2": ("sbuf", [128, E], "float32"),
    "VB": ("sbuf", [128, E], "float32"), "FL": ("sbuf", [128, E], "bfloat16"), "OWN": ("sbuf", [128, E], "float16"),
    "SI": ("sbuf", [128, E], "int32"), "U": ("sbuf", [128, E], "int32"), "W": ("sbuf", [128, E], "float16"),
    "SJ": ("sbuf", [128, E], "int32"), "UJ": ("sbuf", [128, E], "int32"),
    "TES": ("sbuf", [128, E], "float16"), "R1": ("sbuf", [128, E], "float16"), "R2": ("sbuf", [128, E], "bfloat16"),
    "R3": ("sbuf", [128, E], "bfloat16"), "R4": ("sbuf", [128, E], "bfloat16"), "R5": ("sbuf", [128, E], "bfloat16"),
    "SG": ("sbuf", [128, E], "bfloat16"), "EX": ("sbuf", [128, E], "bfloat16"),
    "NV": ("sbuf", [128, E], "float32"), "M1": ("sbuf", [128, RO * E], "float32"), "M2": ("sbuf", [128, RO * E], "float32"),
    "TB": ("sbuf", [128, E], "int32"), "DR": ("sbuf", [128, E], "float32"),
    "ONE": ("sbuf", [128, 128], "float32"), "ID": ("sbuf", [128, 256], "float32"), "COL": ("sbuf", [128, 144], "float32"),
    "WB": ("sbuf", [128, 144], "float16"), "IH": ("sbuf", [128, 4 * 128], "float16"), "IB": ("sbuf", [128, 128], "bfloat16"),
    "ZM": ("sbuf", [128, 6 * 128], "bfloat16"),
    "VW": ("sbuf", [128, 40], "bfloat16"), "WS": ("sbuf", [128, 384], "bfloat16"),
    "PI": ("sbuf", [128, 8], "int32"), "PF": ("sbuf", [128, 24], "float32"),
    "LAND": ("sbuf", [128, NH * LW], "float32"),
}
for _b in range(8):
    SCRATCH["P%d" % _b] = ("psum", [128, 512], "float32")
SEMAPHORES = (["sV", "sS", "sP", "sG", "ld0", "ld1", "ld2", "st0", "st1", "st2", "sent"] + ["arr%d" % t for t in range(RO)]
              + ["h%d_%d_%d" % (k, hop, j) for k in range(20) for hop in range(2) for j in range(3)])


def ones(m):
    return bin(m).count("1")


def dst(c, topo):
    rid, pid, _ = topo.addr(c)
    return DstId(rid=rid, pnc=pid)


def calls():
    out = [[(0, s, c0, w, way) for (s, c0, w, way) in call] for call in CFG["START"]]
    for t in range(RO - 1):
        out += [[(t + 1, t + 3, c0, w, way) for (c0, w, way) in call] for call in CFG["SEND"]]
    return out


def route(rc, way, T, topo):
    r = T.rank_of(rc); dsts = [T.cores[(r + j) % NR] for j in CFG["TURN"]]
    out = topo.mask(rc, dsts[0])
    free = lambda c: [h for h in topo.cores_of(c) if T.rank_of(h) is None]
    inner = [e for e in topo.engines(rc, free(rc)[0]) if not out >> e & 1]
    part_of = {"out": out, "in": sum(1 << e for e in inner), "in0": sum(1 << e for e in inner[:len(inner) // 2]),
               "in1": sum(1 << e for e in inner[len(inner) // 2:])}

    def pick(d, es, letter):
        side = [h for h in free(d) if all(topo.may_write(h, e) for e in es)]
        near = [h for h in side if topo.die(h) == topo.die(d)]; far = [h for h in side if h not in near]
        return {"n": near[0], "f": far[-1], "g": far[0]}[letter]
    if way is None:
        return [(0, rc, out, dsts)]
    if way[0] == "fwd":
        first = []; src = rc; on = []; hop = 0
        mate = [d for d in dsts if topo.mates(topo.chip(rc), topo.chip(d))]
        if len(way) > 2:
            src = pick(rc, mate, way[2]); first = [(0, rc, part_of[way[3]], [src])]; hop = 1
        for d in [d for d in dsts if topo.same_plane(topo.chip(rc), topo.chip(d))]:
            j = [c for c in T.cores if topo.same_plane(topo.chip(c), topo.chip(d))].index(rc)
            e = [e for e in dsts if topo.mates(topo.chip(d), topo.chip(e))]; h = pick(d, e, way[1][j])
            on += [(hop + 1, h, out, e), (hop + 1, h, part_of["in"], [d])]
        return first + [(hop, src, out, [x[1] for x in on[::2]] + mate)] + on
    side = [h for h in free(rc) if (topo.die(h) != topo.die(rc)) == (way[0] == "far")]
    full = [h for h in side if all(topo.may_write(h, d) for d in dsts)]
    part = [h for h in side if h not in full]
    a, b = full[way[1] % len(full)], part[way[1] % len(part)]
    return [(0, rc, part_of[way[2]], [b, a]), (1, b, out, [d for d in dsts if topo.may_write(b, d)]),
            (1, a, out, [d for d in dsts if not topo.may_write(b, d)])]


def plan(T, topo):
    trs = []; land = {}; k = 0
    for j, call in enumerate(calls()):
        for p in call:
            for rc in T.cores:
                plane = [c for c in T.cores if c == rc or topo.same_plane(topo.chip(c), topo.chip(rc))]
                for (hop, src, m, ds) in route(rc, p[4], T, topo):
                    on = [d for d in ds if T.rank_of(d) is None]
                    trs.append((j, p, rc, hop, src, m, ds, "h%d_%d_%d" % (k, hop, plane.index(rc)) if on else "arr%d" % p[0]))
                    for d in on:
                        land.setdefault(d, []).append(trs[-1])
            k += p[4] is not None
    for d in land:
        land[d].sort(key=lambda x: (x[1][0], x[0] + CFG["LAG"] * x[3]))
    return trs, land


def transfer(x, srcs, land, T, topo, fold=False):
    j, (arr, reg, c0, w, way), rc, hop, src, m, ds, sem = x
    col = reg * REG + T.rank_of(rc) * E + c0
    at = [T.TAB[:, col:col + w] if d not in land else T.LAND[:, LW * land[d].index(x):LW * land[d].index(x) + w] for d in ds]
    return RemoteDMATransfer(dst_ids=[dst(d, topo) for d in ds], dma_engine_mask=m, remote_sem=T.sem[sem], srcs=srcs, dsts=at, alu_op=2 if fold else 0)


def helper_program(g, core, T, topo):
    trs, land = plan(T, topo); sent = 0
    for k, x in enumerate(land.get(core, [])):
        mine = [y for y in trs if y[1:3] == x[1:3] and y[4] == core and y[3] == x[3] + 1]
        g.wait_ge(T.sem[x[7]], ones(x[5]))
        g.remote_dma_fused([transfer(y, [T.LAND[:, k * LW:k * LW + x[1][3]]], land, T, topo) for y in mine], local_sem=T.sem.sent)
        sent += sum(ones(y[5]) for y in mine)
    if sent:
        g.wait_ge(T.sem.sent, sent)


def build(g, core, T, topo, r):
    ops = []; C = CFG; now = [-1, ""]

    def ap(x):
        n, a, b, s, pn = x
        return T[n][0:pn, a:b:s] if s != 1 else T[n][0:pn, a:b]

    def R(n, a, w, s=1, pn=128):
        return (n, a, a + (w - 1) * s + 1, s, pn)

    def wd(x):
        return (x[2] - x[1] - 1) // x[3] + 1

    def add(q, fn, rd, wr, after=(), ext=None):
        ops.append({"q": q, "fn": fn, "rd": list(rd), "wr": list(wr), "after": list(after), "ext": ext, "t": now[0], "name": now[1]})
        return len(ops) - 1

    def name(n):
        now[1] = n

    def col(s):
        return [s] if isinstance(s, tuple) else []

    def sc(s):
        return ap(s) if isinstance(s, tuple) else s

    def ts(o, i, s1, op0, s2=None, op1=None):
        if op1 is None:
            return add("V", lambda: g.vector.tensor_scalar(ap(o), ap(i), sc(s1), None, op0), [i] + col(s1), [o])
        return add("V", lambda: g.vector.tensor_scalar(ap(o), ap(i), sc(s1), sc(s2), op0, op1), [i] + col(s1) + col(s2), [o])

    def tt(o, a, b, op):
        return add("V", lambda: g.vector.tensor_tensor(ap(o), ap(a), ap(b), op), [a, b], [o])

    def cp(o, i):
        return add("V", lambda: g.vector.tensor_copy(ap(o), ap(i)), [i], [o])

    def ms(o, v):
        return add("V", lambda: g.vector.memset(ap(o), v), [], [o])

    def act(o, i, f, bias=0.0, scale=1.0):
        return add("S", lambda: g.scalar.activation(ap(o), ap(i), f, bias=sc(bias), scale=sc(scale)), [i] + col(bias) + col(scale), [o])

    def aff(q, o, i, scale, bias):
        if q == "S":
            return act(o, i, F.Identity, bias=bias, scale=scale)
        return ts(o, i, bias, A.add) if scale == 1.0 else ts(o, i, scale, A.mult, bias, A.add)

    lastmm = {}

    def mm(items):
        def fn():
            for (o, l, x, s0, s1) in items:
                ins = g.tensor.matmul(ap(o), ap(l), ap(x), s0, s1)
            return ins
        banks = {it[0][0] for it in items}
        o = add("P", fn, [y for it in items for y in it[1:3]], [it[0] for it in items], [lastmm[b] for b in banks if b in lastmm])
        lastmm.update({b: o for b in banks})
        return o

    def iota(o, pat, base, cm):
        if SCRATCH[o[0]][2] != "int32":
            return add("G", lambda: g.iota(ap(o), pat, base, cm, allow_small_or_imprecise_dtypes=True), [], [o])
        return add("G", lambda: g.iota(ap(o), pat, base, cm), [], [o])

    def keep(o, i, pat, op, fill, base=0, cm=1):
        return add("G", lambda: g.affine_select(ap(o), ap(i), pat, op, fill, base, cm), [i], [o])

    def setrow(o, j, v):
        return keep(o, o, [[0, wd(o)]], A.not_equal, v, -j)

    sent = [0]; need = {}; trs, land = plan(T, topo); ncall = [0]
    for x in trs:
        if core in x[6]:
            n = need.setdefault(x[1][0], {}); n[x[7]] = n.get(x[7], 0) + ones(x[5])

    def send(fold=None):
        tr = []
        for x in trs:
            if x[0] == ncall[0] and x[4] == core:
                arr, reg, a, w, way = x[1]
                tr.append((x, [R("TAB", reg * REG + r * E + a, w)] if fold is None else [R("M1", fold + a, w), R("M2", fold + a, w)])); sent[0] += ones(x[5])
        ncall[0] += 1
        o = add("G", lambda: g.remote_dma_fused([transfer(x, [ap(y) for y in src], land, T, topo, fold is not None) for (x, src) in tr],
                                                local_sem=T.sem.sent), [y for x in tr for y in x[1]], [])
        ops[o]["noinc"] = True

    def gather(q, o, t, off):
        win = R("TAB", t * REG, 3 * REG); ext = need[t]
        src = lambda: ap(win).indirect(ap(off))
        if q == "S":
            return add("S", lambda: g.scalar.activation(ap(o), src(), F.Identity, scale=U10), [win, off], [o], [], ext)
        if q == "V":
            return add("V", lambda: g.vector.tensor_scalar(ap(o), src(), U10, None, A.mult), [win, off], [o], [], ext)
        M2 = 1.5 * 2 ** 34
        return add("V", lambda: g.vector.tensor_scalar(ap(o), src(), M2, M2 + 512 * SHIFT, A.add, A.subtract), [win, off], [o], [], ext)

    for j, (a, b) in enumerate(zip(C["LOAD"], C["LOAD"][1:])):
        o = add("Y", lambda a=a, b=b: g.sync.dma_start(T.Z[:, a:b], T.kin[:, a:b]), [], [R("Z", a, b - a)])
        ops[o]["dma"] = "ld%d" % j
    ONE = R("ONE", 0, 128); ID = R("ID", 0, 128); IN = R("ID", 128, 128); AN = R("AN", 0, E); I25 = R("IB", 0, 128)
    pi = lambda j: R("PI", j, 1)
    pf = lambda j, pn=128: R("PF", j, 1, 1, pn)
    ms(ONE, 1.0)
    iota(pi(0), [[0, 1]], 0, 1)
    keep(ID, ONE, [[-1, 128]], A.is_equal, 0.0)
    iota(AN, [[3, E]], P * r, 0)
    iota(R("COL", 0, 144), [[1, 144]], -15, 0)
    iota(R("PC", 0, 16), [[128, 2], [2, 8]], 0, 0)
    IH = {v: R("IH", 128 * j, 128) for j, v in enumerate([1.0, 4096.0, 1025.0])}
    for v in IH:
        act(IH[v], ID, F.Identity, scale=v)
    AP_ = [R("P0", 0, E), R("P0", 256, E), R("P1", 0, E)]
    for s in range(3):
        aff("S", AP_[s], AN, 1.0, float(s))
    vw = lambda j: R("VW", 8 - j, 9)
    VT, VX = R("VW", 20, 9), R("VW", 30, 9, 1, 2)
    ZM, ZB, TH, ZN, ZC, TN = [R("ZM", 128 * j, 128) for j in range(6)]
    ms(R("VW", 0, 40), 0.0); ms(R("SLOT", 0, 32), 0.0); ms(R("SLOT", 32 + E, 32), 0.0)
    ts(pi(1), pi(0), -16, A.bitwise_and); ts(pi(3), pi(0), 7, A.bitwise_and); ts(pi(4), pi(0), 1, A.bitwise_and)
    ts(IN, ID, 6080.0, A.mult); ts(I25, ID, 1024 * SHIFT, A.mult)
    ts(pi(5), pi(0), 4, A.logical_shift_right, 1, A.bitwise_and); ts(pi(6), pi(0), 3, A.logical_shift_right, 1, A.bitwise_and)
    ms(R("VW", 7, 1), -1.0); ms(R("VW", 8, 1), 1.0); ms(R("VW", 36, 2), 1.0); cp(pf(0), pi(1))
    ms(R("SEL", 128 * RO, 128), U10); ms(R("SELB", 128 * RO, 128), -SHIFT / 2)
    ms(ZM, -1.0 / 32); ms(ZB, -2.0 ** 75); ms(TH, 0.0); ms(pf(8), 1.0)

    def names(zi, c, w):
        name("ni"); aff("S", R("NI", c, w), zi, 1.0 / 64, -31.5 / 64)
        name("i1"); ts(R("I1", c, w), zi, 42, A.bitwise_and)

    def split(zi, s, bank):
        c = s * E
        name("mf"); aff("S", bank, R("I1", c, E), 31.0, -CEN)
        name("i2"); ts(R("I2", c, E), zi, 63, A.bitwise_and)
        name("skm"); tt(R("SK", c, E), R("I2", c, E), bank, A.add)
        name("ne"); aff("S", R("NE", c, E), R("NI", c, E), 6.0, -6.0 * HALF)

    def prep(t, f1):
        s = t % 3; c = s * E
        n = R("NI", c, E); f2 = R("F2", 0, E)
        name("q1"); aff("S", R("Q1", 0, E), n, 1.0 / 3, -1.0 / 3)
        name("q2"); aff("S", R("Q1", E, E), n, 1.0 / 3, (2.0 - s) / 3)
        name("f1"); aff("S", f1, n, float(REG), float(REG * (3 - s)))
        name("f2"); aff("S", f2, R("Q1", E, E), -3.0 * REG, 0.0)
        name("f3"); tt(f1, f1, f2, A.add)
        name("sl"); tt(R("SLOT", 32, E), f1, R("Q1", 0, E), A.add)

    def wrap(t):
        for (n, o, i) in (("ta", R("TT", 0, E), R("SLOT", 32, E)), ("tb", R("TT", E, E + 32), R("SLOT", 16, E + 32))):
            name(n); add("V", lambda o=o, i=i: g.vector.transpose(ap(o), ap(i)), [i], [o])
        o, win, off = R("OFF", t * E, E), R("TT", 0, 2 * E + 32), R("PERM", 0, 16)
        name("off"); add("V", lambda: g.vector.tensor_copy(ap(o), ap(win).indirect(ap(off))), [win, off], [o])

    def select(t):
        for n in ("SEL", "SELB"):
            o, i = R(n, 128 * t, 128), R(n, 128 * RO, 128)
            add("G", lambda o=o, i=i: g.affine_select(ap(o), ap(i), [[0, 128]], A.is_equal, 0.0, -17 * t - 3, 1), [i], [o])

    have = set(); waiting = [[(p[0], p[1] + j) for p in call for j in range(p[2])] for call in C["START"]]
    for step in C["PIPE"].split():
        j = int(step[1]); s, c0, w = C["ENC"][j]
        c = s * E + c0; zi = R("Z", 3 * c0 + s, w, 3); b1 = R("P%d" % (2 + j % 6), 0, w)
        if step[0] == "a":
            names(zi, c, w)
        elif step[0] == "b":
            aff("S", R("NP", c, w), R("NI", c, w), 1.0, -2304.0)
            tt(R("EQ", c, w), R("NI", c, w), R(AP_[s][0], AP_[s][1] + c0, w), A.is_equal)
            aff("S" if j else "V", R("MF", c, w), R("I1", c, w), 31.0, -CEN)
            mm([(b1, IN, R("NP", c, w), True, False)])
            mm([(b1, I25, R("EQ", c, w), False, False), (b1, IH[1.0], R("MF", c, w), False, True)])
        else:
            tt(R("TAB", s * REG + r * E + c0, w), zi, b1, A.add)
            have.update((s, c0 + i) for i in range(w))
            while waiting and all(x in have for x in waiting[0]):
                waiting.pop(0); send()

    name(""); now[0] = -0.5
    tt(pf(10), pi(4), pi(5), A.not_equal); ts(pf(11), pi(3), 16.0, A.mult); ts(pf(12), pf(10), E + 16.0, A.mult, pf(11), A.add)
    tt(pf(13), pf(12), pi(6), A.add); ts(R("PERM", 0, 16), R("PC", 0, 16), pf(13), A.add)
    select(0)
    prep(0, R("P1", 256, E)); wrap(0); split(R("Z", 0, E, 3), 0, R("P2", 256, E))
    ts(R("WB", 0, 144), R("COL", 0, 144), pf(0), A.is_equal, 1024.0, A.mult)
    ts(pf(2), pi(3), 2 * LN2, A.mult, -11 * LN2, A.add)
    ts(pf(3), pi(4), 10 * LN2, A.mult, pf(2), A.add); ts(pf(5), pi(3), 3.0, A.is_ge, -5 * LN2, A.mult); tt(pf(7), pf(2), pf(5), A.add)
    WX, WK, WR = R("WS", 0, 128, 1, 6), R("WS", 128, 128, 1, 9), R("WS", 256, 128, 1, 9)
    ms(R("WS", 128, 256, 1, 9), 0.0); setrow(WK, 8, 682.5 - CEN); setrow(WR, 8, 31.5)
    for wv, c in ((WX, 3), (WK, 2), (WR, 7)):
        act(wv[:4] + (6,), R("ONE", 0, 128, 1, 6), F.Exp, scale=pf(c, 6), bias=10 * LN2)
    act(R("VW", 20, 6), R("COL", 15, 6), F.Exp, scale=2 * LN2, bias=-2 * LN2); ms(R("VW", 21, 1), 5.0)
    keep(ZM, ZM, [[-1, 128]], A.is_ge, -2.0); keep(ZM, ZM, [[-1, 128]], A.not_equal, 1.0); keep(ZB, ZB, [[-1, 128]], A.not_equal, 2.0 ** 75)
    both = R("ZM", 0, 256)
    keep(both, both, [[0, 2], [-16, 8], [0, 16]], A.is_ge, 0.0); keep(both, both, [[0, 2], [16, 8], [0, 16]], A.is_ge, 0.0, 15, -1)
    setrow(TH, 6, -2.0 ** 77); setrow(TH, 7, 2.0 ** 77); setrow(TH, 8, -2.0 ** 28); setrow(R("VW", 36, 2), 1, -1.0)
    act(R("ZM", 384, 384), R("ZM", 0, 384), F.Identity, scale=-1.0)
    TH, TN = TH[:4] + (9,), TN[:4] + (9,)
    aff("S", R("SP", 0, E), AN, 1.0, -P * r - 384.0)
    for j in range(6):
        setrow(pf(8), j, -128.0 * (RC[j] - RC[j + 1]) - (640.0 if j == 1 else 32.0 * 4 ** j) - 4 ** j / 4.0)
    setrow(pf(8), 6, 0.5); setrow(pf(8), 7, -0.5)
    aff("S", R("RAW", 0, P), R("Z", 0, P), 1.0, 0.0)

    for t in range(RO):
        s = t % 3; last = t == RO - 1; now[0] = t
        sel, selb = R("SEL", 128 * t, 128), R("SELB", 128 * t, 128)
        if not last:
            name("sel"); select(t + 1)
            zi = R("Z", t + 1, E, 3) if t < 2 else R("ZI", 0, E)
            if t >= 2:
                name("zi"); aff("S", zi, R("RAW", t - 2, E, 3), 1.0, 0.0)
                names(zi, E * (t - 2), E)
            split(zi, (t + 1) % 3, R("P0", E, E)); prep(t + 1, R("P0", E, E)); wrap(t + 1)
        for h, (i0, w) in enumerate(C["VB"]):
            name("vb%d" % h); gather("B", R("VB", i0, w), t, R("OFF", t * E + i0 + t * w // 16, w // 16))
            name("fl%d" % h); ts(R("FL", i0, w), R("VB", i0, w), 1.0, A.min, -1.0, A.max)
        a = 0
        for j, (q, n) in enumerate(C["GATH"]):
            name("g%d" % j); gather(q, R("G", 16 * a, 16 * n), t, R("OFF", t * E + a, n)); a += n
        late = []; sends = [max(a + n for (a, n, way) in call) for call in C["SEND"]]
        for h, (i0, w) in enumerate(C["HALVES"]):
            X = lambda n, pn=128, i0=i0, w=w: R(n, i0, w, 1, pn)
            rep = C["REP"][h]; B = R("P%d" % h, 0, w)
            for j in range(rep - 1, -1, -1):
                name("b%d%d" % (h, j)); mm([(R("P%d" % h, j * w, w), sel, X("VB"), True, False)])
                name("B%d%d" % (h, j)); mm([(R("P%d" % h, j * w, w), selb, X("FL"), False, True)])
            name("own%d" % h); tt(X("OWN"), R("NE", s * E + i0, w), B, A.is_equal)
            name("tb%d" % h); aff("S", X("TB"), B, 32.0 / 3, 64.0 * HALF)
            name("sx%d" % h); aff("S", X("SP", 1), B[:4] + (1,), 1.0 / 6, HALF - P * r - s - 384.0)
            if not last:
                name("na%d" % h); aff("S", X("NV"), B, 1024.0, 0.0)
            k = 0
            for n in C["SUB"][h]:
                name("d%d%x" % (h, k)); tt(R("D", 16 * i0 + k * w, w * n), R("G", 16 * i0 + k * w, w * n), R("P%d" % h, 0, w * n), A.subtract)
                k += n
            for k0, k1 in zip(C["KCUT"][h], C["KCUT"][h][1:]):
                d4 = R("D", 16 * i0 + k0 * w, (k1 - k0) * w)
                name("c%d%x" % (h, k0)); ts(d4, d4, HI, A.min, LO, A.max)
        for c, (i0, w) in enumerate(C["PARTS"]):
            h0, hw = [x for x in C["HALVES"] if x[0] <= i0][-1]
            pb, pc = "P%d" % (2 + 2 * c), "P%d" % (3 + 2 * c)
            X = lambda n, pn=128, i0=i0, w=w: R(n, i0, w, 1, pn)
            nm = lambda n, c=c: name("%s%d" % (n, c))
            nk = lambda n, k, c=c: name("%s%d%x" % (n, c, k))
            S1, XP, ZP = [R(pb, w * j, w) for j in range(3)]
            BQ, WO, ZQ = [R(pc, w * j, w) for j in range(3)]
            VO = BQ[:4] + (9,); RB = S1; NB = BQ
            for n, (bank, a) in C["OWNBANK"][c].items():
                if n == "ZP":
                    ZP = R(bank, a, w)
                else:
                    ZQ, BQ, RB = [R(bank, a + w * j, w) for j in range(3)]
            qs = C["PLACEL" if last else "PLACE"][c]
            nm("sk"); mm([(S1, IH[1.0], R("SK", s * E + i0, w), True, False)])
            for k0 in range(0, 16, C["MMN"]):
                if k0 == C["SO"][c]:
                    nm("so"); mm([(S1, IH[4096.0], X("OWN"), False, False)])
                nk("m", k0); mm([(S1, R("WB", 15 - k, 128), R("D", 16 * h0 + k * hw + i0 - h0, w), False, k == 15) for k in range(k0, k0 + C["MMN"])])
            nm("x"); mm([(VO, VX, X("SP", 2), True, False)])
            nm("si"); aff(qs[0], X("SI"), S1, 1.0, 16 * 4780.0 + CEN)
            nm("u"); ts(X("U"), X("SI"), 0x1555, A.bitwise_and)
            nm("w")
            if qs[1] == "S":
                act(X("W"), X("U"), F.Relu, bias=-4088.0)
            else:
                ts(X("W"), X("U"), 4088.0, A.subtract, 0.0, A.max)
            nm("te"); act(X("TES"), X("U"), F.Sign, bias=4095.5, scale=-1.0)
            for j in range(1, 6):
                nm("r%d" % j); aff(qs[1 + j], X("R%d" % j), X("W"), 1.0, RC[j] + (-6.5 if j == 2 else 0.5))
            nm("va"); mm([(VO, VT, X("TES"), False, False), (VO, vw(0), X("W"), False, False)])
            for j, js in enumerate(C["VO"][c]):
                nm("v" + "efg"[j]); mm([(VO, vw(i), X("R%d" % i), False, i == C["VO"][c][-1][-1]) for i in js])
            nm("xa"); mm([(XP, IH[1025.0], X("W"), True, False)])
            nm("sg"); act(X("SG", 9), VO, F.Sign, bias=pf(8, 9))
            nm("xb"); mm([(XP, WX, X("SG", 6), False, True)])
            nm("sj"); aff(qs[7], X("SJ"), XP, 1.0, 0x111111 / 2.0)
            if not last:
                nm("nb"); mm([(NB, WK, X("SG", 9), True, True)])
                nm("nv"); tt(X("NV"), X("NV"), NB, A.add)
            if last:
                nm("nb"); mm([(WO, WR, X("SG", 9), True, True)])
                nm("nv"); tt(X("DR"), X("TB"), WO, A.add)
            for (zz, zb, th, n) in ((ZQ, ZC, TN, "q"), (ZP, ZB, TH, "p")):
                nm(n + "a"); mm([(zz, zb, X("OWN"), True, False)])
                nm(n + "t"); mm([(zz, th, X("SG", 9), False, False)])
            nm("uj"); ts(X("UJ"), X("SJ"), 0x111119, A.bitwise_and)
            nm("sm"); aff(qs[8], X("SJ"), X("UJ"), 0x111111 / 2.0 ** 20, 1.5 * 2 ** 23)
            nm("uk"); ts(X("UJ"), X("SJ"), 15, A.bitwise_and)
            nm("ex"); act(X("EX"), X("UJ"), F.Exp, bias=-24 * LN2, scale=6 * LN2)
            nm("pb"); mm([(ZP, ZM, X("EX"), False, True)])
            nm("qb"); mm([(ZQ, ZN, X("EX"), False, True)])
            raw = R("RAW", 3 * i0 + s, w, 3)
            if not last:
                m1, m2 = R("M1", t * E + i0, w), R("M2", t * E + i0, w) if C["FOLD"][c] else BQ
                nm("mi"); tt(m1, X("NV"), ZP, A.min)
                nm("bq"); tt(m2, R("TAB", t * REG + r * E + i0, w), ZQ, A.min)
                nm("mx"); tt(R("TAB", (t + 3) * REG + r * E + i0, w), m1, m2, A.max)
                if i0 + w in sends:
                    name("send%d" % sends.index(i0 + w)); send(t * E if C["FOLD"][c] else None)

                def plain(X=X, nm=nm, WO=WO, ZP=ZP, ZQ=ZQ, RB=RB, raw=raw):
                    nm("wo"); mm([(WO, WR, X("SG", 9), True, True)])
                    nm("dr"); tt(X("DR"), X("TB"), WO, A.add)
                    nm("ds"); tt(X("DR"), X("DR"), ZP, A.min)
                    nm("rb"); tt(RB, raw, ZQ, A.min)
                    nm("rw"); tt(raw, X("DR"), RB, A.max)
                late.append(plain)
            else:
                nm("mi"); tt(X("DR"), X("DR"), ZP, A.min)
                nm("bq"); tt(BQ, raw, ZQ, A.min)
                nm("mx"); tt(raw, X("DR"), BQ, A.max)
                if i0 + w in sends:
                    j = sends.index(i0 + w); a, b = 3 * ([0] + sends)[j], 3 * (i0 + w); name("send%d" % j)
                    o = add("Y", lambda a=a, b=b: g.sync.dma_start(T.yk[:, a:b], T.RAW[:, a:b]), [R("RAW", a, b - a)], [])
                    ops[o]["dma"] = "st%d" % j
        for f in late:
            f()
    return ops, sent[0]


def depend(ops):
    deps = [set(o["after"]) for o in ops]; acc = {}
    for i, o in enumerate(ops):
        for kind, lst in (("r", o["rd"]), ("w", o["wr"])):
            for x in lst:
                for (j, k2, y) in acc.get(x[0], []):
                    if j != i and (kind == "w" or k2 == "w") and x[1] < y[2] and y[1] < x[2]:
                        if x[3] == y[3] == 3 and (x[1] - y[1]) % 3 and ops[j]["q"] == o["q"]:
                            continue
                        deps[i].add(j)
        for kind, lst in (("r", o["rd"]), ("w", o["wr"])):
            for x in lst:
                l = acc.setdefault(x[0], [])
                if kind == "w" and x[3] == 1 and x[4] == 128:
                    l[:] = [z for z in l if not (x[1] <= z[2][1] and z[2][2] <= x[2])]
                l.append((i, kind, x))
    return deps


def order(ops, deps, names):
    at = [{n: k for k, n in enumerate(x)} for x in names]
    key = [(o["t"], at[o["t"]][o["name"]] if o["t"] >= 0 else 0, i) for i, o in enumerate(ops)]
    left = [i for i, o in enumerate(ops) if -1 < o["t"] < 0]; end = {}; free = {"G": 1500, "V": 600}
    while left:
        can = [(max([free.get(ops[i]["q"], 0)] + [end.get(j, 0) + 100 for j in deps[i]]), i) for i in left if not deps[i] & set(left)]
        s, i = min(can); x = ops[i]["wr"][0]; left.remove(i); key[i] = (-0.5, s, i)
        end[i] = free[ops[i]["q"]] = s + (200 + 2 * (x[2] - x[1]) if ops[i]["q"] == "G" else 60 + max(64, (x[2] - x[1]) // x[3]))
    seq = []; seen = set()

    def put(i):
        if i not in seen:
            seen.add(i)
            for j in sorted(deps[i], key=lambda j: key[j]):
                put(j)
            seq.append(i)
    for i in sorted(range(len(ops)), key=lambda i: key[i]):
        put(i)
    deps = [set(d) for d in deps]; bank = {}
    for i in seq:
        for x in {x[0] for x in ops[i]["rd"] + ops[i]["wr"] if SCRATCH[x[0]][0] == "psum"}:
            d = bank.setdefault(x, {})
            deps[i].update(j for q2, j in d.items() if q2 != ops[i]["q"])
            d[ops[i]["q"]] = i
    return seq, deps


def rank_program(g, core, T, topo):
    r = T.rank_of(core)
    if r is None:
        return helper_program(g, core, T, topo)
    ops, sent = build(g, core, T, topo, r)
    seq, deps = order(ops, depend(ops), [CFG["ORDER"].split()] * (RO - 1) + [CFG["LAST"].split()])
    Q = {"V": g.vector, "S": g.scalar, "P": g.tensor, "G": g, "Y": g.sync}
    used = set(); place = {i: k for k, i in enumerate(seq)}
    for i in seq:
        for j in deps[i]:
            if not (ops[i]["q"] == ops[j]["q"] == "P"):
                used.add(j)
    cnt = {}; sig = {}; known = {}; clock = {}
    for i in seq:
        o = ops[i]; q = o["q"]
        kn = known.setdefault(q, {}); want = {}
        for j in deps[i]:
            if j in sig and not (q == ops[j]["q"] == "P"):
                s, v = sig[j]
                if v > want.get(s, (0, 0))[0]:
                    want[s] = (v, j)
        for s, v in (o["ext"] or {}).items():
            want[s] = (v, None)
        for s, (v, j) in sorted(want.items(), key=lambda z: -(place[z[1][1]] if z[1][1] is not None else 10 ** 9)):
            if kn.get(s, 0) < v:
                Q[q].wait_ge(T.sem[s], v); kn[s] = v
                for s2, v2 in clock.get(j, {}).items():
                    kn[s2] = max(kn.get(s2, 0), v2)
        ins = o["fn"]()
        clock[i] = dict(kn)
        if "dma" in o:
            ins.then_inc(T.sem[o["dma"]], 16); sig[i] = (o["dma"], 16); cnt[o["dma"]] = 16
        elif i in used and "noinc" not in o:
            s = "s" + q; cnt[s] = cnt.get(s, 0) + 1; ins.then_inc(T.sem[s], 1); sig[i] = (s, cnt[s])
    for s, v in cnt.items():
        g.sync.wait_ge(T.sem[s], v)
    g.wait_ge(T.sem.sent, sent)
